import numpy as np
import ml_dtypes


def mxq(x, axis, fmt="e4m3"):
    dtype, down = {"e4m3": (ml_dtypes.float8_e4m3fn, 7), "e5m2": (ml_dtypes.float8_e5m2, 14)}[fmt]
    v = np.moveaxis(np.asarray(x, np.float32).astype(ml_dtypes.bfloat16).astype(np.float64), axis, -1)
    blocks = v.reshape(v.shape[:-1] + (-1, 32))
    amax = np.abs(blocks).max(-1, keepdims=True)
    byte = np.maximum(np.where(amax > 0, np.frexp(amax)[1] - 1 + 127, 0) - down, 1)
    scale = np.exp2(byte - 127.0)
    codes = (blocks / scale).astype(np.float32).astype(dtype).astype(np.float64)
    return np.moveaxis((codes * scale).reshape(v.shape), -1, axis)


WIDE = False


def mx_kscale(k):
    if not WIDE:
        return np.ones(k)
    levels = np.array([10, -10, 5, -5, 0])
    if k % 512:
        return np.exp2(np.random.permutation(np.resize(levels, k // 32))).repeat(32)
    a = np.empty((k // 512, 16))
    for p in range(k // 512):
        a[p, :8] = np.random.permutation(np.resize(levels, 8))
        for g in range(8):
            far = levels[np.abs(levels - a[p, g]) >= 10]
            a[p, g + 8] = far[np.random.randint(len(far))]
    return np.exp2(a.ravel()).repeat(32)


def f64(x):
    return np.asarray(x).astype(np.float64)


def striped8(idx):
    return np.concatenate([x.reshape(-1, 16).T for x in idx]).astype(np.uint16)


def runs(offs, k):
    lists = np.stack([offs[16 * r : 16 * r + 16].T.reshape(-1) for r in range(8)]).astype(np.int64)
    return lists[np.arange(k) % 512 // 64]


def pack_weight(w):
    k, n = w.shape
    w = f64(np.asarray(w, np.float32).astype(ml_dtypes.bfloat16)).reshape(k // 32, 32, n)
    amax = np.abs(w).max(1)
    byte = np.clip(np.where(amax > 0, np.frexp(amax)[1] - 1 + 127 - 7, 1), 1, 254)
    scaled = (w * np.exp2(127.0 - byte)[:, None, :]).reshape(k, n).astype(np.float32)
    words = np.ascontiguousarray(scaled.reshape(k // 512, 128, 4, n).transpose(0, 1, 3, 2)).astype(ml_dtypes.float8_e4m3fn).view(np.uint8)
    return words, np.ascontiguousarray(byte.astype(np.uint8).reshape(k // 512, 16, n))


def unpack_weight(words, scales):
    g, p, n, _ = words.shape
    vals = np.ascontiguousarray(words).view(ml_dtypes.float8_e4m3fn).astype(np.float64) * np.repeat(np.exp2(scales.astype(np.float64) - 127.0), 8, axis=1)[..., None]
    return vals.transpose(0, 1, 3, 2).reshape(g * 512, n)


K, T, S, N, H = 512, 2048, 512, 512, 512
P = 2 ** 7


def setup_inputs():
    n = np.random.standard_normal
    s = mx_kscale(K)[:, None]
    u = mx_kscale(H)
    packed_xT = pack_weight(n((K, T)) * s)
    return {
        "x_words": packed_xT[0],
        "x_scales": packed_xT[1],
        "w1": (n((K, H)) / np.sqrt(K) / s * u).astype(np.float32),
        "prev": (n((H, S)) * u[:, None]).astype(np.float32),
        "c2": np.tile(np.random.uniform(0.05, 0.4, S), (P, 1)).astype(np.float32),
        "w2": (n((H, N)) / np.sqrt(H) / u[:, None]).astype(np.float32),
        "offs": striped8(np.stack([np.random.permutation(T)[:S] for _ in range(8)])),
        "east": striped8(np.stack([np.random.permutation(S) for _ in range(8)])),
        "west": striped8(np.stack([np.random.permutation(S) for _ in range(8)])),
    }


def reference(x_words, x_scales, w1, prev, c2, w2, offs, east, west):
    xq = unpack_weight(x_words, x_scales)[np.arange(K)[:, None], runs(offs, K)]
    y = mxq(f64(w1), 0, "e4m3").T @ xq
    z = 2.0 * y - f64(prev) + f64(c2)[:1] * (y[np.arange(H)[:, None], runs(east, H)] + y[np.arange(H)[:, None], runs(west, H)] - (2.0 * y))
    return mxq(f64(w2), 0, "e4m3").T @ mxq(z, 0, "e4m3")

@@ -1,0 +1,192 @@
+from contextlib import ExitStack
+
+import concourse.mybir as mybir
+from concourse.masks import make_identity
+
+K, T, S, N, H = 512, 2048, 512, 512, 512
+FLOPS = 2 * K * H * S + 2 * H * N * S
+
+F32 = mybir.dt.float32
+BF16 = mybir.dt.bfloat16
+I32 = mybir.dt.int32
+U32 = mybir.dt.uint32
+U16 = mybir.dt.uint16
+U8 = mybir.dt.uint8
+FP8X4 = mybir.dt.float8_e4m3fn_x4
+ADD = mybir.AluOpType.add
+MULT = mybir.AluOpType.mult
+SUB = mybir.AluOpType.subtract
+COPY = mybir.ActivationFunctionType.Copy
+
+P = 128
+PACK = 4
+CH = 128
+NCH = S // CH
+LC = CH // 16
+M_VEC = 88
+
+
+def tile_picked_waveeq_none_p_kernel(tc, x_words, x_scales, w1, prev, c2, w2, offs, east, west, out):
+    nc = tc.nc
+    with ExitStack() as ctx:
+        lists = ctx.enter_context(tc.tile_pool(name="lists", bufs=1))
+        keep = ctx.enter_context(tc.tile_pool(name="keep", bufs=1))
+        psum = ctx.enter_context(tc.psum_pool(name="psum", bufs=1))
+
+        offs_t = lists.tile([P, S // 16], U16, name="offs_t")
+        east_t = lists.tile([P, S // 16], U16, name="east_t")
+        west_t = lists.tile([P, S // 16], U16, name="west_t")
+
+        scale_win = keep.tile([P, T], U8, name="scale_win")
+        nc.vector.memset(scale_win[:].bitcast(I32), 0)
+        nc.sync.dma_start(offs_t[:], offs)
+        for r in range(2):
+            nc.scalar.dma_start(scale_win[r:P:16, :].bitcast(I32), x_scales[0, r:16:2, :].bitcast(I32))
+
+        w1_raw = keep.tile([P, PACK, H], F32, name="w1_raw", tag="w_raw")
+        nc.sync.dma_start(w1_raw[:], w1.rearrange("(p j) c -> p j c", j=PACK))
+        word_win = keep.tile([P, T], U32, name="word_win", tag="big")
+        nc.sync.dma_start(word_win[:].bitcast(I32), x_words[0].rearrange("p c r -> p (c r)").bitcast(I32))
+        nc.sync.dma_start(east_t[:], east)
+        nc.sync.dma_start(west_t[:], west)
+        w2_rows = w2.rearrange("(p j) c -> p j c", j=PACK)
+        w2a_raw = keep.tile([P, PACK, N // 2], F32, name="w2a_raw")
+        nc.sync.dma_start(w2a_raw[:], w2_rows[:, :, 0 : N // 2])
+
+        ident = keep.tile([P, P], F32, name="ident")
+        make_identity(nc, ident[:])
+        c_rows = keep.tile([P, P], F32, name="c_rows")
+        nc.gpsimd.memset(c_rows[:], 0.0)
+        nc.gpsimd.dma_start(c_rows[0:NCH, :], c2[0].rearrange("(b i) -> b i", b=NCH))
+
+        scale_got = keep.tile([P, S], U8, name="scale_got")
+        nc.vector.tensor_copy(scale_got[:], scale_win[:].indirect(offs_t[:]))
+        x_plane = keep.tile([P, S], U8, name="x_plane", align_bytes=64)
+        nc.vector.tensor_copy(x_plane[:].bitcast(I32), scale_got[:].bitcast(I32))
+        for r in range(2):
+            nc.scalar.dma_start(x_plane[2 + r : P : 32, :].bitcast(I32), scale_got[16 + r : P : 32, :].bitcast(I32))
+
+        w1_grp = keep.tile([P, PACK, P, PACK], BF16, name="w1_grp", align_bytes=64)
+        w1_src = w1_raw[:].rearrange("p j (m t) -> p m j t", t=PACK)
+        w1_dst = w1_grp[:].rearrange("p t m j -> p m j t")
+        nc.vector.tensor_copy(w1_dst[:, 0:M_VEC], w1_src[:, 0:M_VEC])
+        nc.scalar.copy(w1_dst[:, M_VEC:P], w1_src[:, M_VEC:P])
+        w1_codes = keep.tile([P, H], U32, name="w1_codes", align_bytes=64)
+        w1_plane = keep.tile([P, H], U8, name="w1_plane", align_bytes=64)
+        nc.vector.quantize_mx(out=w1_codes[:].bitcast(FP8X4), scales=w1_plane[:], in_=w1_grp[:].rearrange("p t m j -> p (t m j)"))
+
+        x_codes = keep.tile([P, S], U32, name="x_codes", align_bytes=64)
+        nc.vector.tensor_copy(x_codes[:], word_win[:].indirect(offs_t[:]))
+
+        w2b_raw = keep.tile([P, PACK, N // 2], F32, name="w2b_raw", tag="w_raw")
+        nc.sync.dma_start(w2b_raw[:], w2_rows[:, :, N // 2 : N])
+        prev_t = keep.tile([P, PACK, S], F32, name="prev_t", tag="big")
+        nc.sync.dma_start(prev_t[:], prev.rearrange("(p t) j -> p t j", t=PACK))
+
+        c_ps = psum.tile([P, P], F32, name="c_ps", tag="back", bufs=2)
+        nc.tensor.transpose(c_ps[:], c_rows[:], ident[:])
+        c_col = keep.tile([P, NCH], F32, name="c_col")
+        nc.scalar.copy(c_col[:], c_ps[:, 0:NCH])
+
+        w2_codes = keep.tile([P, N], U32, name="w2_codes", align_bytes=64)
+        w2_plane = keep.tile([P, N], U8, name="w2_plane", align_bytes=64)
+        w2_grp = [keep.tile([P, N // 2, PACK], BF16, name=f"w2_grp{h}", align_bytes=64) for h in range(2)]
+
+        def weave_w2(copy, h, raw):
+            copy(w2_grp[h][:].rearrange("p (c i) t -> p c t i", i=4), raw[:].rearrange("p t (c i) -> p c t i", i=4))
+
+        def quant_w2(h):
+            cols = slice(h * (N // 2), (h + 1) * (N // 2))
+            nc.vector.quantize_mx(out=w2_codes[:, cols].bitcast(FP8X4), scales=w2_plane[:, cols], in_=w2_grp[h][:].rearrange("p c t -> p (c t)"))
+
+        weave_w2(nc.vector.tensor_copy, 0, w2a_raw)
+
+        y = [keep.tile([P, S], F32, name=f"y{t}") for t in range(PACK)]
+        m2 = [keep.tile([P, S], F32, name=f"m2_{t}") for t in range(PACK)]
+        for t in range(PACK):
+            y_ps = psum.tile([P, S], F32, name=f"y_ps{t}", tag="wide", bufs=4)
+            cols = slice(t * P, (t + 1) * P)
+            nc.tensor.matmul_mx(out=y_ps[:], lhsT=w1_codes[:, cols].bitcast(FP8X4), lhsT_scale=w1_plane[:, cols],
+                                rhs=x_codes[:].bitcast(FP8X4), rhs_scale=x_plane[:], start=True, stop=True)
+            nc.scalar.copy(y[t][:], y_ps[:])
+            nc.scalar.activation(m2[t][:], y_ps[:], COPY, scale=-2.0)
+
+        s1 = [[keep.tile([P, CH], F32, name=f"s1_{b}_{t}") for t in range(PACK)] for b in range(NCH)]
+        s2 = [[keep.tile([P, CH], F32, name=f"s2_{b}_{t}") for t in range(PACK)] for b in range(NCH)]
+        d_sb = [keep.tile([P, 2, P, 2], F32, name=f"d_sb{b}") for b in range(NCH)]
+        a_ps = {}
+        zt = [keep.tile([P, 2, P, 2], BF16, name=f"zt{b}") for b in range(NCH)]
+        z_grp = [keep.tile([P, CH, PACK], BF16, name=f"z_grp{b}", align_bytes=64) for b in range(NCH)]
+        out_rows = out.rearrange("(g p) j -> p g j", p=P)
+
+        def east_gather(b, t):
+            nc.vector.tensor_tensor(s1[b][t][:], y[t][:].indirect(east_t[:, b * LC : (b + 1) * LC]), m2[t][:, b * CH : (b + 1) * CH], ADD)
+
+        def west_gather(b, t):
+            nc.vector.tensor_tensor(s2[b][t][:], y[t][:].indirect(west_t[:, b * LC : (b + 1) * LC]), s1[b][t][:], ADD)
+            if t == 0:
+                a_ps[b] = psum.tile([P, PACK, P], F32, name=f"a_ps{b}", tag="wide", bufs=4)
+            nc.tensor.transpose(a_ps[b][:, t, :], s2[b][t][:], ident[:])
+
+        def make_d(b):
+            d_ps = psum.tile([P, PACK, P], F32, name=f"d_ps{b}", tag="d", bufs=2)
+            cols = slice(b * CH, (b + 1) * CH)
+            for t in range(PACK):
+                nc.tensor.matmul(d_ps[:, t, :], lhsT=prev_t[:, t, cols], rhs=ident[:], start=True, stop=False, is_transpose=True)
+                nc.tensor.matmul(d_ps[:, t, :], lhsT=m2[t][:, cols], rhs=ident[:], start=False, stop=True, is_transpose=True)
+            nc.scalar.copy(d_sb[b][:], d_ps[:].rearrange("j (u e) p -> j u p e", e=2))
+
+        def combine(b):
+            for u in range(2):
+                nc.vector.scalar_tensor_tensor(zt[b][:, u], a_ps[b][:, 2 * u : 2 * u + 2, :].rearrange("j e p -> j p e"),
+                                               c_col[:, b : b + 1], d_sb[b][:, u], MULT, SUB)
+            back = psum.tile([P, 2, CH], F32, name=f"back{b}", tag="back", bufs=2)
+            words = zt[b][:].rearrange("j u p e -> j u (p e)").bitcast(F32)
+            for u in range(2):
+                nc.tensor.transpose(back[:, u, :], words[:, u, :], ident[:])
+            nc.scalar.copy(z_grp[b][:].rearrange("p j t -> p (j t)").bitcast(F32).rearrange("p (j u) -> p j u", u=2),
+                           back[:].rearrange("p u j -> p j u"))
+
+        def finish(b):
+            z_codes = keep.tile([P, CH], U32, name=f"z_codes{b}", align_bytes=64)
+            z_plane = keep.tile([P, CH], U8, name=f"z_plane{b}", align_bytes=64)
+            nc.vector.quantize_mx(out=z_codes[:].bitcast(FP8X4), scales=z_plane[:], in_=z_grp[b][:].rearrange("p j t -> p (j t)"))
+            o_ps = psum.tile([P, PACK, CH], F32, name=f"o_ps{b}", tag="d", bufs=2)
+            for g in range(N // P):
+                cols = slice(g * P, (g + 1) * P)
+                nc.tensor.matmul_mx(out=o_ps[:, g, :], lhsT=w2_codes[:, cols].bitcast(FP8X4), lhsT_scale=w2_plane[:, cols],
+                                    rhs=z_codes[:].bitcast(FP8X4), rhs_scale=z_plane[:], start=True, stop=True)
+            o_sb = keep.tile([P, PACK, CH], F32, name=f"o_sb{b}")
+            nc.scalar.copy(o_sb[:], o_ps[:])
+            nc.sync.dma_start(out_rows[:, :, b * CH : (b + 1) * CH], o_sb[:])
+
+        def gather_pair(b, t0):
+            east_gather(b, t0)
+            east_gather(b, t0 + 1)
+            west_gather(b, t0)
+            west_gather(b, t0 + 1)
+
+        quant_w2(0)
+        for t in range(PACK):
+            east_gather(0, t)
+            east_gather(1, t)
+            west_gather(0, t)
+            west_gather(1, t)
+        make_d(0)
+        make_d(1)
+        weave_w2(nc.scalar.copy, 1, w2b_raw)
+        make_d(2)
+        make_d(3)
+        gather_pair(2, 0)
+        combine(0)
+        gather_pair(2, 2)
+        combine(1)
+        quant_w2(1)
+        gather_pair(3, 0)
+        finish(0)
+        combine(2)
+        finish(1)
+        gather_pair(3, 2)
+        finish(2)
+        combine(3)
+        finish(3)

@@ -1,7 +1,6 @@
 from contextlib import ExitStack
 
 import concourse.mybir as mybir
-from concourse.masks import make_identity
 
 K, T, S, N, H = 512, 2048, 512, 512, 512
 FLOPS = 2 * K * H * S + 2 * H * N * S
@@ -15,6 +14,7 @@ U8 = mybir.dt.uint8
 FP8X4 = mybir.dt.float8_e4m3fn_x4
 ADD = mybir.AluOpType.add
 MULT = mybir.AluOpType.mult
+EQ = mybir.AluOpType.is_equal
 SUB = mybir.AluOpType.subtract
 COPY = mybir.ActivationFunctionType.Copy
 
@@ -23,7 +23,6 @@ PACK = 4
 CH = 128
 NCH = S // CH
 LC = CH // 16
-M_VEC = 88
 
 
 def tile_picked_waveeq_none_p_kernel(tc, x_words, x_scales, w1, prev, c2, w2, offs, east, west, out):
@@ -38,155 +37,183 @@ def tile_picked_waveeq_none_p_kernel(tc, x_words, x_scales, w1, prev, c2, w2, of
         west_t = lists.tile([P, S // 16], U16, name="west_t")
 
         scale_win = keep.tile([P, T], U8, name="scale_win")
-        nc.vector.memset(scale_win[:].bitcast(I32), 0)
+        nc.gpsimd.memset(scale_win[:].bitcast(I32), 0)
         nc.sync.dma_start(offs_t[:], offs)
-        for r in range(2):
-            nc.scalar.dma_start(scale_win[r:P:16, :].bitcast(I32), x_scales[0, r:16:2, :].bitcast(I32))
-
-        w1_raw = keep.tile([P, PACK, H], F32, name="w1_raw", tag="w_raw")
-        nc.sync.dma_start(w1_raw[:], w1.rearrange("(p j) c -> p j c", j=PACK))
-        word_win = keep.tile([P, T], U32, name="word_win", tag="big")
-        nc.sync.dma_start(word_win[:].bitcast(I32), x_words[0].rearrange("p c r -> p (c r)").bitcast(I32))
         nc.sync.dma_start(east_t[:], east)
         nc.sync.dma_start(west_t[:], west)
-        w2_rows = w2.rearrange("(p j) c -> p j c", j=PACK)
-        w2a_raw = keep.tile([P, PACK, N // 2], F32, name="w2a_raw")
-        nc.sync.dma_start(w2a_raw[:], w2_rows[:, :, 0 : N // 2])
+        for r in range(2):
+            nc.sync.dma_start(scale_win[r:P:16, :].bitcast(I32), x_scales[0, r:16:2, :].bitcast(I32))
+
+        word_win = keep.tile([P, T], U32, name="word_win", tag="big")
+        nc.sync.dma_start(word_win[:].bitcast(I32), x_words[0].rearrange("p c r -> p (c r)").bitcast(I32))
+        w1_rows = w1.rearrange("(p j) c -> p j c", j=PACK)
+        w1_raw = [keep.tile([P, PACK, H // 2], F32, name=f"w1_raw{h}", tag=f"w1_raw{h}") for h in range(2)]
+        for h in range(2):
+            nc.sync.dma_start(w1_raw[h][:], w1_rows[:, :, h * (H // 2) : (h + 1) * (H // 2)])
 
         ident = keep.tile([P, P], F32, name="ident")
-        make_identity(nc, ident[:])
-        c_rows = keep.tile([P, P], F32, name="c_rows")
-        nc.gpsimd.memset(c_rows[:], 0.0)
-        nc.gpsimd.dma_start(c_rows[0:NCH, :], c2[0].rearrange("(b i) -> b i", b=NCH))
+        ones = keep.tile([P, P], F32, name="ones")
+        count = keep.tile([P, 32], F32, name="count", align_bytes=64)
+        count_t = keep.tile([P, 32], F32, name="count_t", align_bytes=64)
+        nc.vector.memset(ones[:], 1.0)
+        nc.scalar.activation(ident[:], ones[:], COPY, scale=0.0)
+        nc.vector.tensor_tensor_scan(count[:], ones[:, 0:32], ones[:, 0:32], 0.0, MULT, ADD)
+        nc.vector.transpose(count_t[:], count[:])
+        for q in range(0, P, 32):
+            nc.vector.tensor_tensor(ident[q : q + 32, q : q + 32], count[q : q + 32, :], count_t[q : q + 32, :], EQ)
 
         scale_got = keep.tile([P, S], U8, name="scale_got")
         nc.vector.tensor_copy(scale_got[:], scale_win[:].indirect(offs_t[:]))
         x_plane = keep.tile([P, S], U8, name="x_plane", align_bytes=64)
         nc.vector.tensor_copy(x_plane[:].bitcast(I32), scale_got[:].bitcast(I32))
         for r in range(2):
-            nc.scalar.dma_start(x_plane[2 + r : P : 32, :].bitcast(I32), scale_got[16 + r : P : 32, :].bitcast(I32))
+            nc.sync.dma_start(x_plane[2 + r : P : 32, :].bitcast(I32), scale_got[16 + r : P : 32, :].bitcast(I32))
 
-        w1_grp = keep.tile([P, PACK, P, PACK], BF16, name="w1_grp", align_bytes=64)
-        w1_src = w1_raw[:].rearrange("p j (m t) -> p m j t", t=PACK)
-        w1_dst = w1_grp[:].rearrange("p t m j -> p m j t")
-        nc.vector.tensor_copy(w1_dst[:, 0:M_VEC], w1_src[:, 0:M_VEC])
-        nc.scalar.copy(w1_dst[:, M_VEC:P], w1_src[:, M_VEC:P])
-        w1_codes = keep.tile([P, H], U32, name="w1_codes", align_bytes=64)
-        w1_plane = keep.tile([P, H], U8, name="w1_plane", align_bytes=64)
-        nc.vector.quantize_mx(out=w1_codes[:].bitcast(FP8X4), scales=w1_plane[:], in_=w1_grp[:].rearrange("p t m j -> p (t m j)"))
+        MH = P // 2
+        w1_codes = keep.tile([P, PACK, P], U32, name="w1_codes", align_bytes=64)
+        w1_plane = keep.tile([P, PACK, P], U8, name="w1_plane", align_bytes=64)
+
+        def quantise_w1(h, u, copy):
+            grp = keep.tile([P, 2, MH, PACK], BF16, name=f"w1_grp{h}{u}", tag=f"w1_grp{h}{u}", align_bytes=64)
+            copy(grp[:].rearrange("p t m j -> p m t j"), w1_raw[h][:].rearrange("p j (m t) -> p m t j", t=PACK)[:, :, 2 * u : 2 * u + 2])
+            for e in range(2):
+                t = 2 * u + e
+                nc.vector.quantize_mx(out=w1_codes[:, t, h * MH : (h + 1) * MH].bitcast(FP8X4), scales=w1_plane[:, t, h * MH : (h + 1) * MH],
+                                      in_=grp[:, e].rearrange("p m j -> p (m j)"))
 
         x_codes = keep.tile([P, S], U32, name="x_codes", align_bytes=64)
         nc.vector.tensor_copy(x_codes[:], word_win[:].indirect(offs_t[:]))
+        for h in range(2):
+            quantise_w1(h, 0, nc.vector.tensor_copy)
+            quantise_w1(h, 1, nc.scalar.copy)
 
-        w2b_raw = keep.tile([P, PACK, N // 2], F32, name="w2b_raw", tag="w_raw")
-        nc.sync.dma_start(w2b_raw[:], w2_rows[:, :, N // 2 : N])
         prev_t = keep.tile([P, PACK, S], F32, name="prev_t", tag="big")
         nc.sync.dma_start(prev_t[:], prev.rearrange("(p t) j -> p t j", t=PACK))
-
-        c_ps = psum.tile([P, P], F32, name="c_ps", tag="back", bufs=2)
-        nc.tensor.transpose(c_ps[:], c_rows[:], ident[:])
-        c_col = keep.tile([P, NCH], F32, name="c_col")
-        nc.scalar.copy(c_col[:], c_ps[:, 0:NCH])
+        c_col = keep.tile([P, NCH], F32, name="c_col", tag="w1_grp00", align_bytes=64)
+        with nc.allow_non_contiguous_dma(reason="one value a partition"):
+            nc.sync.dma_start(c_col[:], c2[0].rearrange("(b p) -> p b", p=P))
+        w2_rows = w2.rearrange("(p j) c -> p j c", j=PACK)
+        w2_raw = [keep.tile([P, PACK, N // 2], F32, name=f"w2_raw{h}", tag=f"w1_raw{h}") for h in range(2)]
+        for h in range(2):
+            nc.sync.dma_start(w2_raw[h][:], w2_rows[:, :, h * (N // 2) : (h + 1) * (N // 2)])
 
         w2_codes = keep.tile([P, N], U32, name="w2_codes", align_bytes=64)
         w2_plane = keep.tile([P, N], U8, name="w2_plane", align_bytes=64)
-        w2_grp = [keep.tile([P, N // 2, PACK], BF16, name=f"w2_grp{h}", align_bytes=64) for h in range(2)]
+        w2_grp = keep.tile([P, N, PACK], BF16, name="w2_grp", align_bytes=64)
 
-        def weave_w2(copy, h, raw):
-            copy(w2_grp[h][:].rearrange("p (c i) t -> p c t i", i=4), raw[:].rearrange("p t (c i) -> p c t i", i=4))
-
-        def quant_w2(h):
-            cols = slice(h * (N // 2), (h + 1) * (N // 2))
-            nc.vector.quantize_mx(out=w2_codes[:, cols].bitcast(FP8X4), scales=w2_plane[:, cols], in_=w2_grp[h][:].rearrange("p c t -> p (c t)"))
-
-        weave_w2(nc.vector.tensor_copy, 0, w2a_raw)
+        def weave_w2(h):
+            nc.scalar.copy(w2_grp[:, h * (N // 2) : (h + 1) * (N // 2)].rearrange("p (c i) t -> p c t i", i=4), w2_raw[h][:].rearrange("p t (c i) -> p c t i", i=4))
 
         y = [keep.tile([P, S], F32, name=f"y{t}") for t in range(PACK)]
         m2 = [keep.tile([P, S], F32, name=f"m2_{t}") for t in range(PACK)]
-        for t in range(PACK):
+        halves = [slice(0, S // 2), slice(S // 2, S)]
+
+        def first_product(bank, t, cols):
+            nc.tensor.matmul_mx(out=bank[:], lhsT=w1_codes[:, t].bitcast(FP8X4), lhsT_scale=w1_plane[:, t],
+                                rhs=x_codes[:, cols].bitcast(FP8X4), rhs_scale=x_plane[:, cols], start=True, stop=True)
+
+        banks = [psum.tile([P, S // 2], F32, name="y_ps0a", tag="wide", bufs=4), psum.tile([P, S // 2], F32, name="y_ps0b", tag="back", bufs=2)]
+        for bank, half in zip(banks, halves):
+            first_product(bank, 0, half)
+        nc.scalar.copy(y[0][:, halves[0]], banks[0][:])
+        nc.vector.tensor_copy(y[0][:, halves[1]], banks[1][:])
+        for bank, half in zip(banks, halves):
+            nc.scalar.activation(m2[0][:, half], bank[:], COPY, scale=-2.0)
+        for t in range(1, PACK):
             y_ps = psum.tile([P, S], F32, name=f"y_ps{t}", tag="wide", bufs=4)
-            cols = slice(t * P, (t + 1) * P)
-            nc.tensor.matmul_mx(out=y_ps[:], lhsT=w1_codes[:, cols].bitcast(FP8X4), lhsT_scale=w1_plane[:, cols],
-                                rhs=x_codes[:].bitcast(FP8X4), rhs_scale=x_plane[:], start=True, stop=True)
+            first_product(y_ps, t, slice(0, S))
             nc.scalar.copy(y[t][:], y_ps[:])
             nc.scalar.activation(m2[t][:], y_ps[:], COPY, scale=-2.0)
 
-        s1 = [[keep.tile([P, CH], F32, name=f"s1_{b}_{t}") for t in range(PACK)] for b in range(NCH)]
-        s2 = [[keep.tile([P, CH], F32, name=f"s2_{b}_{t}") for t in range(PACK)] for b in range(NCH)]
-        d_sb = [keep.tile([P, 2, P, 2], F32, name=f"d_sb{b}") for b in range(NCH)]
-        a_ps = {}
-        zt = [keep.tile([P, 2, P, 2], BF16, name=f"zt{b}") for b in range(NCH)]
-        z_grp = [keep.tile([P, CH, PACK], BF16, name=f"z_grp{b}", align_bytes=64) for b in range(NCH)]
+        last = NCH - 1
         out_rows = out.rearrange("(g p) j -> p g j", p=P)
+        s1, a_ps, d_sb, z_grp, back = {}, {}, {}, {}, {}
 
-        def east_gather(b, t):
-            nc.vector.tensor_tensor(s1[b][t][:], y[t][:].indirect(east_t[:, b * LC : (b + 1) * LC]), m2[t][:, b * CH : (b + 1) * CH], ADD)
+        def east_gather(b0, b1, t, tag):
+            s1[b0, t] = keep.tile([P, (b1 - b0) * CH], F32, name=f"s1_{b0}_{t}", tag=tag, align_bytes=64)
+            nc.vector.tensor_tensor(s1[b0, t][:], y[t][:].indirect(east_t[:, b0 * LC : b1 * LC]), m2[t][:, b0 * CH : b1 * CH], ADD)
 
-        def west_gather(b, t):
-            nc.vector.tensor_tensor(s2[b][t][:], y[t][:].indirect(west_t[:, b * LC : (b + 1) * LC]), s1[b][t][:], ADD)
-            if t == 0:
-                a_ps[b] = psum.tile([P, PACK, P], F32, name=f"a_ps{b}", tag="wide", bufs=4)
-            nc.tensor.transpose(a_ps[b][:, t, :], s2[b][t][:], ident[:])
+        def west_gather(b0, b1, t, tag):
+            s2 = keep.tile([P, (b1 - b0) * CH], F32, name=f"s2_{b0}_{t}", tag=tag, align_bytes=64)
+            nc.vector.tensor_tensor(s2[:], y[t][:].indirect(west_t[:, b0 * LC : b1 * LC]), s1[b0, t][:], ADD)
+            u, e = divmod(t, 2)
+            for b in range(b0, b1):
+                if b == last:
+                    if e == 0:
+                        a_ps[b, u] = psum.tile([P, 2, P], F32, name=f"a_ps{b}_{u}", tag="wide", bufs=4)
+                    target = a_ps[b, u][:, e, :]
+                else:
+                    if t == 0:
+                        a_ps[b] = psum.tile([P, 2, 2 * P], F32, name=f"a_ps{b}", tag="wide", bufs=4)
+                    target = a_ps[b][:, e, u * P : (u + 1) * P]
+                nc.tensor.transpose(target, s2[:, (b - b0) * CH : (b - b0 + 1) * CH], ident[:])
+            return s2
 
         def make_d(b):
-            d_ps = psum.tile([P, PACK, P], F32, name=f"d_ps{b}", tag="d", bufs=2)
+            d_ps = psum.tile([P, 2, 2 * P], F32, name=f"d_ps{b}", tag="d", bufs=2)
             cols = slice(b * CH, (b + 1) * CH)
             for t in range(PACK):
-                nc.tensor.matmul(d_ps[:, t, :], lhsT=prev_t[:, t, cols], rhs=ident[:], start=True, stop=False, is_transpose=True)
-                nc.tensor.matmul(d_ps[:, t, :], lhsT=m2[t][:, cols], rhs=ident[:], start=False, stop=True, is_transpose=True)
-            nc.scalar.copy(d_sb[b][:], d_ps[:].rearrange("j (u e) p -> j u p e", e=2))
+                u, e = divmod(t, 2)
+                target = d_ps[:, e, u * P : (u + 1) * P]
+                nc.tensor.matmul(target, lhsT=prev_t[:, t, cols], rhs=ident[:], start=True, stop=False, is_transpose=True)
+                nc.tensor.matmul(target, lhsT=m2[t][:, cols], rhs=ident[:], start=False, stop=True, is_transpose=True)
+            d_sb[b] = keep.tile([P, 2 * P, 2], F32, name=f"d_sb{b}", tag=f"d{b}", align_bytes=64)
+            nc.scalar.copy(d_sb[b][:], d_ps[:].rearrange("j e w -> j w e"))
 
-        def combine(b):
-            for u in range(2):
-                nc.vector.scalar_tensor_tensor(zt[b][:, u], a_ps[b][:, 2 * u : 2 * u + 2, :].rearrange("j e p -> j p e"),
-                                               c_col[:, b : b + 1], d_sb[b][:, u], MULT, SUB)
-            back = psum.tile([P, 2, CH], F32, name=f"back{b}", tag="back", bufs=2)
-            words = zt[b][:].rearrange("j u p e -> j u (p e)").bitcast(F32)
-            for u in range(2):
-                nc.tensor.transpose(back[:, u, :], words[:, u, :], ident[:])
-            nc.scalar.copy(z_grp[b][:].rearrange("p j t -> p (j t)").bitcast(F32).rearrange("p (j u) -> p j u", u=2),
-                           back[:].rearrange("p u j -> p j u"))
+        def combine(b, src, words):
+            n = words.stop - words.start
+            zt = keep.tile([P, n, 2], BF16, name=f"zt{b}_{words.start}", tag=f"zt{b}_{words.start}", align_bytes=64)
+            nc.vector.scalar_tensor_tensor(zt[:], src[:].rearrange("j e w -> j w e"), c_col[:, b : b + 1], d_sb[b][:, words], MULT, SUB)
+            if words.start == 0:
+                back[b] = psum.tile([P, 2, CH], F32, name=f"back{b}", tag="back", bufs=2)
+            for w0 in range(0, n, P):
+                nc.tensor.transpose(back[b][:, (words.start + w0) // P, :], zt[:].rearrange("j w e -> j (w e)").bitcast(F32)[:, w0 : w0 + P], ident[:])
+            if words.stop == 2 * P:
+                z_grp[b] = keep.tile([P, CH, PACK], BF16, name=f"z_grp{b}", tag=f"z{b}", align_bytes=64)
+                nc.scalar.copy(z_grp[b][:].rearrange("p j t -> p (j t)").bitcast(F32).rearrange("p (j u) -> p j u", u=2),
+                               back[b][:].rearrange("p u j -> p j u"))
 
         def finish(b):
             z_codes = keep.tile([P, CH], U32, name=f"z_codes{b}", align_bytes=64)
             z_plane = keep.tile([P, CH], U8, name=f"z_plane{b}", align_bytes=64)
             nc.vector.quantize_mx(out=z_codes[:].bitcast(FP8X4), scales=z_plane[:], in_=z_grp[b][:].rearrange("p j t -> p (j t)"))
-            o_ps = psum.tile([P, PACK, CH], F32, name=f"o_ps{b}", tag="d", bufs=2)
-            for g in range(N // P):
-                cols = slice(g * P, (g + 1) * P)
-                nc.tensor.matmul_mx(out=o_ps[:, g, :], lhsT=w2_codes[:, cols].bitcast(FP8X4), lhsT_scale=w2_plane[:, cols],
-                                    rhs=z_codes[:].bitcast(FP8X4), rhs_scale=z_plane[:], start=True, stop=True)
-            o_sb = keep.tile([P, PACK, CH], F32, name=f"o_sb{b}")
-            nc.scalar.copy(o_sb[:], o_ps[:])
-            nc.sync.dma_start(out_rows[:, :, b * CH : (b + 1) * CH], o_sb[:])
+            parts = [(0, 2, "wide", 4, nc.scalar.copy, nc.scalar), (2, 4, "d", 2, nc.vector.tensor_copy, nc.sync)] if b == last else [(0, 4, "d", 2, nc.vector.tensor_copy if b == 2 else nc.scalar.copy, nc.sync)]
+            for g0, g1, tag, bufs, copy, queue in parts:
+                o_ps = psum.tile([P, g1 - g0, CH], F32, name=f"o_ps{b}_{g0}", tag=tag, bufs=bufs)
+                for g in range(g0, g1):
+                    cols = slice(g * P, (g + 1) * P)
+                    nc.tensor.matmul_mx(out=o_ps[:, g - g0, :], lhsT=w2_codes[:, cols].bitcast(FP8X4), lhsT_scale=w2_plane[:, cols],
+                                        rhs=z_codes[:].bitcast(FP8X4), rhs_scale=z_plane[:], start=True, stop=True)
+                o_sb = keep.tile([P, g1 - g0, CH], F32, name=f"o_sb{b}_{g0}")
+                copy(o_sb[:], o_ps[:])
+                queue.dma_start(out_rows[:, g0:g1, b * CH : (b + 1) * CH], o_sb[:])
 
-        def gather_pair(b, t0):
-            east_gather(b, t0)
-            east_gather(b, t0 + 1)
-            west_gather(b, t0)
-            west_gather(b, t0 + 1)
-
-        quant_w2(0)
+        whole = slice(0, 2 * P)
         for t in range(PACK):
-            east_gather(0, t)
-            east_gather(1, t)
-            west_gather(0, t)
-            west_gather(1, t)
-        make_d(0)
-        make_d(1)
-        weave_w2(nc.scalar.copy, 1, w2b_raw)
-        make_d(2)
+            east_gather(0, 2, t, "ring_a")
+            east_gather(2, 3, t, "ring_b")
+            west_gather(0, 2, t, f"s2a{t}")
+            pa = west_gather(2, 3, t, f"s2b{t}")
+        for b in range(3):
+            make_d(b)
+        weave_w2(0)
+        weave_w2(1)
         make_d(3)
-        gather_pair(2, 0)
-        combine(0)
-        gather_pair(2, 2)
-        combine(1)
-        quant_w2(1)
-        gather_pair(3, 0)
+        east_gather(3, 4, 0, "ring_a")
+        east_gather(3, 4, 1, "ring_b")
+        combine(0, a_ps[0], whole)
+        combine(1, a_ps[1], whole)
+        west_gather(3, 4, 0, "d1")
+        west_gather(3, 4, 1, "s2c1")
+        combine(2, a_ps[2], whole)
+        nc.vector.quantize_mx(out=w2_codes[:].bitcast(FP8X4), scales=w2_plane[:], in_=w2_grp[:].rearrange("p c t -> p (c t)"))
         finish(0)
-        combine(2)
+        east_gather(3, 4, 2, "z0")
+        east_gather(3, 4, 3, "d2")
         finish(1)
-        gather_pair(3, 2)
+        combine(3, a_ps[3, 0], slice(0, P))
+        west_gather(3, 4, 2, "z1")
+        pb = west_gather(3, 4, 3, "s2c3")
         finish(2)
-        combine(3)
+        combine(3, a_ps[3, 1], slice(P, 2 * P))
         finish(3)

@@ -22,7 +22,7 @@ P = 128
 PACK = 4
 CH = 128
 NCH = S // CH
-LC = CH // 16
+XA = 512
 
 
 def tile_picked_waveeq_none_p_kernel(tc, x_words, x_scales, w1, prev, c2, w2, offs, east, west, out):
@@ -37,30 +37,23 @@ def tile_picked_waveeq_none_p_kernel(tc, x_words, x_scales, w1, prev, c2, w2, of
         west_t = lists.tile([P, S // 16], U16, name="west_t")
 
         scale_win = keep.tile([P, T], U8, name="scale_win")
-        nc.gpsimd.memset(scale_win[:].bitcast(I32), 0)
+        nc.vector.memset(scale_win[:].bitcast(I32), 0)
+        word_win = keep.tile([P, T], U32, name="word_win", tag="words")
+        word_rows = x_words[0].rearrange("p c r -> p (c r)").bitcast(I32)
+        nc.sync.dma_start(word_win[:, 0:XA].bitcast(I32), word_rows[:, 0:XA])
         nc.sync.dma_start(offs_t[:], offs)
         nc.sync.dma_start(east_t[:], east)
         nc.sync.dma_start(west_t[:], west)
         for r in range(2):
             nc.sync.dma_start(scale_win[r:P:16, :].bitcast(I32), x_scales[0, r:16:2, :].bitcast(I32))
+        w1_raw = keep.tile([P, PACK, H], F32, name="w1_raw", tag="raw")
+        nc.sync.dma_start(w1_raw[:], w1.rearrange("(p j) c -> p j c", j=PACK))
+        nc.sync.dma_start(word_win[:, XA:].bitcast(I32), word_rows[:, XA:])
 
-        word_win = keep.tile([P, T], U32, name="word_win", tag="big")
-        nc.sync.dma_start(word_win[:].bitcast(I32), x_words[0].rearrange("p c r -> p (c r)").bitcast(I32))
-        w1_rows = w1.rearrange("(p j) c -> p j c", j=PACK)
-        w1_raw = [keep.tile([P, PACK, H // 2], F32, name=f"w1_raw{h}", tag=f"w1_raw{h}") for h in range(2)]
-        for h in range(2):
-            nc.sync.dma_start(w1_raw[h][:], w1_rows[:, :, h * (H // 2) : (h + 1) * (H // 2)])
-
-        ident = keep.tile([P, P], F32, name="ident")
-        ones = keep.tile([P, P], F32, name="ones")
-        count = keep.tile([P, 32], F32, name="count", align_bytes=64)
-        count_t = keep.tile([P, 32], F32, name="count_t", align_bytes=64)
-        nc.vector.memset(ones[:], 1.0)
-        nc.scalar.activation(ident[:], ones[:], COPY, scale=0.0)
-        nc.vector.tensor_tensor_scan(count[:], ones[:, 0:32], ones[:, 0:32], 0.0, MULT, ADD)
-        nc.vector.transpose(count_t[:], count[:])
-        for q in range(0, P, 32):
-            nc.vector.tensor_tensor(ident[q : q + 32, q : q + 32], count[q : q + 32, :], count_t[q : q + 32, :], EQ)
+        y = [keep.tile([P, 2 * S if t < PACK - 1 else S], F32, name=f"y{t}") for t in range(PACK)]
+        nc.vector.memset(y[0][:, S:], 0.0)
+        for t in range(1, PACK - 1):
+            nc.scalar.activation(y[t][:, S:], y[0][:, S:], COPY)
 
         scale_got = keep.tile([P, S], U8, name="scale_got")
         nc.vector.tensor_copy(scale_got[:], scale_win[:].indirect(offs_t[:]))
@@ -69,117 +62,85 @@ def tile_picked_waveeq_none_p_kernel(tc, x_words, x_scales, w1, prev, c2, w2, of
         for r in range(2):
             nc.sync.dma_start(x_plane[2 + r : P : 32, :].bitcast(I32), scale_got[16 + r : P : 32, :].bitcast(I32))
 
-        MH = P // 2
-        w1_codes = keep.tile([P, PACK, P], U32, name="w1_codes", align_bytes=64)
-        w1_plane = keep.tile([P, PACK, P], U8, name="w1_plane", align_bytes=64)
+        w1_codes = [keep.tile([P, 2 * P], U32, name=f"w1_codes{u}", align_bytes=64) for u in range(2)]
+        w1_plane = [keep.tile([P, 2 * P], U8, name=f"w1_plane{u}", align_bytes=64) for u in range(2)]
+        for u, copy in enumerate((nc.vector.tensor_copy, nc.scalar.copy)):
+            grp = keep.tile([P, 2, P, PACK], BF16, name=f"w1_grp{u}", tag=f"w1_grp{u}", align_bytes=64)
+            copy(grp[:].rearrange("p t m j -> p m t j"), w1_raw[:].rearrange("p j (m t) -> p m t j", t=PACK)[:, :, 2 * u : 2 * u + 2])
+            nc.vector.quantize_mx(out=w1_codes[u][:].bitcast(FP8X4), scales=w1_plane[u][:], in_=grp[:].rearrange("p t m j -> p (t m j)"))
 
-        def quantise_w1(h, u, copy):
-            grp = keep.tile([P, 2, MH, PACK], BF16, name=f"w1_grp{h}{u}", tag=f"w1_grp{h}{u}", align_bytes=64)
-            copy(grp[:].rearrange("p t m j -> p m t j"), w1_raw[h][:].rearrange("p j (m t) -> p m t j", t=PACK)[:, :, 2 * u : 2 * u + 2])
-            for e in range(2):
-                t = 2 * u + e
-                nc.vector.quantize_mx(out=w1_codes[:, t, h * MH : (h + 1) * MH].bitcast(FP8X4), scales=w1_plane[:, t, h * MH : (h + 1) * MH],
-                                      in_=grp[:, e].rearrange("p m j -> p (m j)"))
-
+        halves = [slice(0, S // 2), slice(S // 2, S)]
         x_codes = keep.tile([P, S], U32, name="x_codes", align_bytes=64)
-        nc.vector.tensor_copy(x_codes[:], word_win[:].indirect(offs_t[:]))
-        for h in range(2):
-            quantise_w1(h, 0, nc.vector.tensor_copy)
-            quantise_w1(h, 1, nc.scalar.copy)
+        for h, half in enumerate(halves):
+            nc.vector.tensor_copy(x_codes[:, half], word_win[:].indirect(offs_t[:, 16 * h : 16 * h + 16]))
 
-        prev_t = keep.tile([P, PACK, S], F32, name="prev_t", tag="big")
+        c_t = keep.tile([P, S], F32, name="c_t", tag="w1_grp0", align_bytes=64)
+        nc.sync.dma_start(c_t[:], c2)
+        prev_t = keep.tile([P, PACK, S], F32, name="prev_t", tag="raw")
         nc.sync.dma_start(prev_t[:], prev.rearrange("(p t) j -> p t j", t=PACK))
-        c_col = keep.tile([P, NCH], F32, name="c_col", tag="w1_grp00", align_bytes=64)
-        with nc.allow_non_contiguous_dma(reason="one value a partition"):
-            nc.sync.dma_start(c_col[:], c2[0].rearrange("(b p) -> p b", p=P))
-        w2_rows = w2.rearrange("(p j) c -> p j c", j=PACK)
-        w2_raw = [keep.tile([P, PACK, N // 2], F32, name=f"w2_raw{h}", tag=f"w1_raw{h}") for h in range(2)]
-        for h in range(2):
-            nc.sync.dma_start(w2_raw[h][:], w2_rows[:, :, h * (N // 2) : (h + 1) * (N // 2)])
+        w2_raw = keep.tile([P, PACK, N], F32, name="w2_raw", tag="words")
+        nc.sync.dma_start(w2_raw[:], w2.rearrange("(p j) c -> p j c", j=PACK))
+
+        m2 = [keep.tile([P, S], F32, name=f"m2_{t}") for t in range(PACK)]
+
+        def first_product(bank, t, cols):
+            u, e = divmod(t, 2)
+            nc.tensor.matmul_mx(out=bank[:], lhsT=w1_codes[u][:, e * P : (e + 1) * P].bitcast(FP8X4), lhsT_scale=w1_plane[u][:, e * P : (e + 1) * P],
+                                rhs=x_codes[:, cols].bitcast(FP8X4), rhs_scale=x_plane[:, cols], start=True, stop=True)
+
+        banks = [psum.tile([P, S // 2], F32, name=f"y_ps0{h}") for h in range(2)]
+        for bank, half in zip(banks, halves):
+            first_product(bank, 0, half)
+        nc.scalar.copy(y[0][:, halves[0]], banks[0][:])
+        nc.scalar.activation(m2[0][:, halves[0]], banks[0][:], COPY, scale=-2.0)
+        nc.vector.tensor_copy(y[0][:, halves[1]], banks[1][:])
+        nc.scalar.activation(m2[0][:, halves[1]], banks[1][:], COPY, scale=-2.0)
+        for t in range(1, PACK):
+            y_ps = psum.tile([P, S], F32, name=f"y_ps{t}")
+            first_product(y_ps, t, slice(0, S))
+            nc.scalar.copy(y[t][:, 0:S], y_ps[:])
+            nc.scalar.activation(m2[t][:], y_ps[:], COPY, scale=-2.0)
 
         w2_codes = keep.tile([P, N], U32, name="w2_codes", align_bytes=64)
         w2_plane = keep.tile([P, N], U8, name="w2_plane", align_bytes=64)
         w2_grp = keep.tile([P, N, PACK], BF16, name="w2_grp", align_bytes=64)
+        nc.scalar.copy(w2_grp[:].rearrange("p (c i) t -> p c t i", i=4), w2_raw[:].rearrange("p t (c i) -> p c t i", i=4))
 
-        def weave_w2(h):
-            nc.scalar.copy(w2_grp[:, h * (N // 2) : (h + 1) * (N // 2)].rearrange("p (c i) t -> p c t i", i=4), w2_raw[h][:].rearrange("p t (c i) -> p c t i", i=4))
-
-        y = [keep.tile([P, S], F32, name=f"y{t}") for t in range(PACK)]
-        m2 = [keep.tile([P, S], F32, name=f"m2_{t}") for t in range(PACK)]
-        halves = [slice(0, S // 2), slice(S // 2, S)]
-
-        def first_product(bank, t, cols):
-            nc.tensor.matmul_mx(out=bank[:], lhsT=w1_codes[:, t].bitcast(FP8X4), lhsT_scale=w1_plane[:, t],
-                                rhs=x_codes[:, cols].bitcast(FP8X4), rhs_scale=x_plane[:, cols], start=True, stop=True)
-
-        banks = [psum.tile([P, S // 2], F32, name="y_ps0a", tag="wide", bufs=4), psum.tile([P, S // 2], F32, name="y_ps0b", tag="back", bufs=2)]
-        for bank, half in zip(banks, halves):
-            first_product(bank, 0, half)
-        nc.scalar.copy(y[0][:, halves[0]], banks[0][:])
-        nc.vector.tensor_copy(y[0][:, halves[1]], banks[1][:])
-        for bank, half in zip(banks, halves):
-            nc.scalar.activation(m2[0][:, half], bank[:], COPY, scale=-2.0)
-        for t in range(1, PACK):
-            y_ps = psum.tile([P, S], F32, name=f"y_ps{t}", tag="wide", bufs=4)
-            first_product(y_ps, t, slice(0, S))
-            nc.scalar.copy(y[t][:], y_ps[:])
-            nc.scalar.activation(m2[t][:], y_ps[:], COPY, scale=-2.0)
-
-        last = NCH - 1
+        s1 = [keep.tile([P, S], F32, name=f"s1_{t}") for t in range(PACK)]
+        s2 = [keep.tile([P, S], F32, name=f"s2_{t}") for t in range(PACK)]
+        cs = keep.tile([P, NCH, PACK, CH], F32, name="cs")
+        dn = keep.tile([P, NCH, PACK, CH], F32, name="dn")
         out_rows = out.rearrange("(g p) j -> p g j", p=P)
-        s1, a_ps, d_sb, z_grp, back = {}, {}, {}, {}, {}
+        z_grp = {}
 
-        def east_gather(b0, b1, t, tag):
-            s1[b0, t] = keep.tile([P, (b1 - b0) * CH], F32, name=f"s1_{b0}_{t}", tag=tag, align_bytes=64)
-            nc.vector.tensor_tensor(s1[b0, t][:], y[t][:].indirect(east_t[:, b0 * LC : b1 * LC]), m2[t][:, b0 * CH : b1 * CH], ADD)
+        def east_gather(t, j0, j1):
+            nc.vector.tensor_tensor(s1[t][:, j0:j1], y[t][:].indirect(east_t[:, j0 // 16 : j1 // 16]), m2[t][:, j0:j1], ADD)
 
-        def west_gather(b0, b1, t, tag):
-            s2 = keep.tile([P, (b1 - b0) * CH], F32, name=f"s2_{b0}_{t}", tag=tag, align_bytes=64)
-            nc.vector.tensor_tensor(s2[:], y[t][:].indirect(west_t[:, b0 * LC : b1 * LC]), s1[b0, t][:], ADD)
-            u, e = divmod(t, 2)
-            for b in range(b0, b1):
-                if b == last:
-                    if e == 0:
-                        a_ps[b, u] = psum.tile([P, 2, P], F32, name=f"a_ps{b}_{u}", tag="wide", bufs=4)
-                    target = a_ps[b, u][:, e, :]
-                else:
-                    if t == 0:
-                        a_ps[b] = psum.tile([P, 2, 2 * P], F32, name=f"a_ps{b}", tag="wide", bufs=4)
-                    target = a_ps[b][:, e, u * P : (u + 1) * P]
-                nc.tensor.transpose(target, s2[:, (b - b0) * CH : (b - b0 + 1) * CH], ident[:])
-            return s2
+        def west_gather(t, j0, j1):
+            nc.vector.tensor_tensor(s2[t][:, j0:j1], y[t][:].indirect(west_t[:, j0 // 16 : j1 // 16]), s1[t][:, j0:j1], ADD)
 
-        def make_d(b):
-            d_ps = psum.tile([P, 2, 2 * P], F32, name=f"d_ps{b}", tag="d", bufs=2)
-            cols = slice(b * CH, (b + 1) * CH)
-            for t in range(PACK):
-                u, e = divmod(t, 2)
-                target = d_ps[:, e, u * P : (u + 1) * P]
-                nc.tensor.matmul(target, lhsT=prev_t[:, t, cols], rhs=ident[:], start=True, stop=False, is_transpose=True)
-                nc.tensor.matmul(target, lhsT=m2[t][:, cols], rhs=ident[:], start=False, stop=True, is_transpose=True)
-            d_sb[b] = keep.tile([P, 2 * P, 2], F32, name=f"d_sb{b}", tag=f"d{b}", align_bytes=64)
-            nc.scalar.copy(d_sb[b][:], d_ps[:].rearrange("j e w -> j w e"))
+        def chunked(ap):
+            return ap.rearrange("p (b j) -> p b j", j=CH)
 
-        def combine(b, src, words):
-            n = words.stop - words.start
-            zt = keep.tile([P, n, 2], BF16, name=f"zt{b}_{words.start}", tag=f"zt{b}_{words.start}", align_bytes=64)
-            nc.vector.scalar_tensor_tensor(zt[:], src[:].rearrange("j e w -> j w e"), c_col[:, b : b + 1], d_sb[b][:, words], MULT, SUB)
-            if words.start == 0:
-                back[b] = psum.tile([P, 2, CH], F32, name=f"back{b}", tag="back", bufs=2)
-            for w0 in range(0, n, P):
-                nc.tensor.transpose(back[b][:, (words.start + w0) // P, :], zt[:].rearrange("j w e -> j (w e)").bitcast(F32)[:, w0 : w0 + P], ident[:])
-            if words.stop == 2 * P:
-                z_grp[b] = keep.tile([P, CH, PACK], BF16, name=f"z_grp{b}", tag=f"z{b}", align_bytes=64)
-                nc.scalar.copy(z_grp[b][:].rearrange("p j t -> p (j t)").bitcast(F32).rearrange("p (j u) -> p j u", u=2),
-                               back[b][:].rearrange("p u j -> p j u"))
+        def times_c(t, b0, b1):
+            cols = slice(b0 * CH, b1 * CH)
+            nc.vector.tensor_tensor(cs[:, b0:b1, t, :], chunked(s2[t][:, cols]), chunked(c_t[:, cols]), MULT)
+
+        def make_dn(t):
+            nc.vector.tensor_tensor(dn[:, :, t, :], chunked(m2[t][:]), chunked(prev_t[:, t, :]), ADD)
+
+        def make_z(b):
+            z_grp[b] = keep.tile([P, CH, PACK], BF16, name=f"z_grp{b}", align_bytes=64)
+            nc.vector.tensor_tensor(z_grp[b][:].rearrange("p (c i) t -> p c t i", i=4), cs[:, b].rearrange("p t (c i) -> p c t i", i=4),
+                                    dn[:, b].rearrange("p t (c i) -> p c t i", i=4), SUB)
 
         def finish(b):
             z_codes = keep.tile([P, CH], U32, name=f"z_codes{b}", align_bytes=64)
             z_plane = keep.tile([P, CH], U8, name=f"z_plane{b}", align_bytes=64)
             nc.vector.quantize_mx(out=z_codes[:].bitcast(FP8X4), scales=z_plane[:], in_=z_grp[b][:].rearrange("p j t -> p (j t)"))
-            parts = [(0, 2, "wide", 4, nc.scalar.copy, nc.scalar), (2, 4, "d", 2, nc.vector.tensor_copy, nc.sync)] if b == last else [(0, 4, "d", 2, nc.vector.tensor_copy if b == 2 else nc.scalar.copy, nc.sync)]
-            for g0, g1, tag, bufs, copy, queue in parts:
-                o_ps = psum.tile([P, g1 - g0, CH], F32, name=f"o_ps{b}_{g0}", tag=tag, bufs=bufs)
+            parts = [(0, 2, nc.scalar.copy, nc.scalar), (2, 4, nc.vector.tensor_copy, nc.sync)] if b == NCH - 1 else [(0, 4, nc.scalar.copy, nc.sync)]
+            for g0, g1, copy, queue in parts:
+                o_ps = psum.tile([P, g1 - g0, CH], F32, name=f"o_ps{b}_{g0}", tag="o", bufs=3)
                 for g in range(g0, g1):
                     cols = slice(g * P, (g + 1) * P)
                     nc.tensor.matmul_mx(out=o_ps[:, g - g0, :], lhsT=w2_codes[:, cols].bitcast(FP8X4), lhsT_scale=w2_plane[:, cols],
@@ -188,32 +149,29 @@ def tile_picked_waveeq_none_p_kernel(tc, x_words, x_scales, w1, prev, c2, w2, of
                 copy(o_sb[:], o_ps[:])
                 queue.dma_start(out_rows[:, g0:g1, b * CH : (b + 1) * CH], o_sb[:])
 
-        whole = slice(0, 2 * P)
-        for t in range(PACK):
-            east_gather(0, 2, t, "ring_a")
-            east_gather(2, 3, t, "ring_b")
-            west_gather(0, 2, t, f"s2a{t}")
-            pa = west_gather(2, 3, t, f"s2b{t}")
-        for b in range(3):
-            make_d(b)
-        weave_w2(0)
-        weave_w2(1)
-        make_d(3)
-        east_gather(3, 4, 0, "ring_a")
-        east_gather(3, 4, 1, "ring_b")
-        combine(0, a_ps[0], whole)
-        combine(1, a_ps[1], whole)
-        west_gather(3, 4, 0, "d1")
-        west_gather(3, 4, 1, "s2c1")
-        combine(2, a_ps[2], whole)
+        for half in halves:
+            east_gather(0, half.start, half.stop)
+        for half in halves:
+            west_gather(0, half.start, half.stop)
+        for t in range(1, PACK):
+            if t < PACK - 1:
+                east_gather(t, 0, S)
+                times_c(t - 1, 0, NCH)
+                west_gather(t, 0, S)
+            else:
+                east_gather(t, 0, S // 2)
+                times_c(t - 1, 0, NCH)
+                east_gather(t, S // 2, S)
+            make_dn(t - 1)
+        last = PACK - 1
+        make_dn(last)
         nc.vector.quantize_mx(out=w2_codes[:].bitcast(FP8X4), scales=w2_plane[:], in_=w2_grp[:].rearrange("p c t -> p (c t)"))
-        finish(0)
-        east_gather(3, 4, 2, "z0")
-        east_gather(3, 4, 3, "d2")
-        finish(1)
-        combine(3, a_ps[3, 0], slice(0, P))
-        west_gather(3, 4, 2, "z1")
-        pb = west_gather(3, 4, 3, "s2c3")
-        finish(2)
-        combine(3, a_ps[3, 1], slice(P, 2 * P))
-        finish(3)
+        for step in range(NCH + 3):
+            if step < NCH:
+                west_gather(last, step * CH, (step + 1) * CH)
+            if 0 <= step - 3 < NCH:
+                finish(step - 3)
+            if 0 <= step - 1 < NCH:
+                times_c(last, step - 1, step)
+            if 0 <= step - 2 < NCH:
+                make_z(step - 2)

@@ -46,14 +46,12 @@ def tile_picked_waveeq_none_p_kernel(tc, x_words, x_scales, w1, prev, c2, w2, of
         nc.sync.dma_start(west_t[:], west)
         for r in range(2):
             nc.sync.dma_start(scale_win[r:P:16, :].bitcast(I32), x_scales[0, r:16:2, :].bitcast(I32))
+        c_col = keep.tile([P, NCH], F32, name="c_col")
+        with nc.allow_non_contiguous_dma(reason="one value a partition"):
+            nc.sync.dma_start(c_col[:], c2[0].rearrange("(b p) -> p b", p=P))
         w1_raw = keep.tile([P, PACK, H], F32, name="w1_raw", tag="raw")
         nc.sync.dma_start(w1_raw[:], w1.rearrange("(p j) c -> p j c", j=PACK))
         nc.sync.dma_start(word_win[:, XA:].bitcast(I32), word_rows[:, XA:])
-
-        y = [keep.tile([P, 2 * S if t < PACK - 1 else S], F32, name=f"y{t}") for t in range(PACK)]
-        nc.vector.memset(y[0][:, S:], 0.0)
-        for t in range(1, PACK - 1):
-            nc.scalar.activation(y[t][:, S:], y[0][:, S:], COPY)
 
         scale_got = keep.tile([P, S], U8, name="scale_got")
         nc.vector.tensor_copy(scale_got[:], scale_win[:].indirect(offs_t[:]))
@@ -61,6 +59,38 @@ def tile_picked_waveeq_none_p_kernel(tc, x_words, x_scales, w1, prev, c2, w2, of
         nc.vector.tensor_copy(x_plane[:].bitcast(I32), scale_got[:].bitcast(I32))
         for r in range(2):
             nc.sync.dma_start(x_plane[2 + r : P : 32, :].bitcast(I32), scale_got[16 + r : P : 32, :].bitcast(I32))
+
+        y = [keep.tile([P, 2 * S], F32, name=f"y{t}") for t in range(PACK)]
+        nc.vector.memset(y[0][:, S:], 0.0)
+        for t in range(1, PACK):
+            nc.scalar.activation(y[t][:, S:], y[0][:, S:], COPY)
+
+        ident = keep.tile([P, P], F32, name="ident")
+        ones = keep.tile([P, 32], F32, name="ones")
+        count = keep.tile([P, 32], F32, name="count", align_bytes=64)
+        count_t = keep.tile([P, 32], F32, name="count_t", align_bytes=64)
+        nc.vector.memset(ones[:], 1.0)
+        nc.vector.memset(ident[:], 0.0)
+        nc.vector.tensor_tensor_scan(count[:], ones[:], ones[:], 0.0, MULT, ADD)
+        nc.vector.transpose(count_t[:], count[:])
+        for q in range(0, P, 32):
+            nc.vector.tensor_tensor(ident[q : q + 32, q : q + 32], count[q : q + 32, :], count_t[q : q + 32, :], EQ)
+
+        def bank(i, shape, name):
+            return psum.tile(shape, F32, name=name, tag=f"bank{i}")
+
+        def turn(target, src, start=True, stop=True):
+            nc.tensor.matmul(target, lhsT=src, rhs=ident[:], start=start, stop=stop, is_transpose=True)
+
+        c_ps = bank(7, [P, NCH, CH], "c_ps")
+        for b in range(NCH):
+            turn(c_ps[:, b, :], c_col[:, b : b + 1].to_broadcast([P, P]))
+        c_neg = keep.tile([P, S], F32, name="c_neg")
+        c_row = keep.tile([P, S], F32, name="c_row")
+        a_col = keep.tile([P, NCH], F32, name="a_col")
+        nc.scalar.activation(c_neg[:], c_ps[:].rearrange("p b j -> p (b j)"), COPY, scale=-1.0)
+        nc.scalar.copy(c_row[:], c_ps[:].rearrange("p b j -> p (b j)"))
+        nc.scalar.activation(a_col[:], c_col[:], COPY, scale=-2.0, bias=2.0)
 
         w1_codes = [keep.tile([P, 2 * P], U32, name=f"w1_codes{u}", align_bytes=64) for u in range(2)]
         w1_plane = [keep.tile([P, 2 * P], U8, name=f"w1_plane{u}", align_bytes=64) for u in range(2)]
@@ -74,73 +104,43 @@ def tile_picked_waveeq_none_p_kernel(tc, x_words, x_scales, w1, prev, c2, w2, of
         for h, half in enumerate(halves):
             nc.vector.tensor_copy(x_codes[:, half], word_win[:].indirect(offs_t[:, 16 * h : 16 * h + 16]))
 
-        c_t = keep.tile([P, S], F32, name="c_t", tag="w1_grp0", align_bytes=64)
-        nc.sync.dma_start(c_t[:], c2)
         prev_t = keep.tile([P, PACK, S], F32, name="prev_t", tag="raw")
         nc.sync.dma_start(prev_t[:], prev.rearrange("(p t) j -> p t j", t=PACK))
         w2_raw = keep.tile([P, PACK, N], F32, name="w2_raw", tag="words")
         nc.sync.dma_start(w2_raw[:], w2.rearrange("(p j) c -> p j c", j=PACK))
 
-        m2 = [keep.tile([P, S], F32, name=f"m2_{t}") for t in range(PACK)]
 
-        def first_product(bank, t, cols):
+        def first_product(acc, t, cols):
             u, e = divmod(t, 2)
-            nc.tensor.matmul_mx(out=bank[:], lhsT=w1_codes[u][:, e * P : (e + 1) * P].bitcast(FP8X4), lhsT_scale=w1_plane[u][:, e * P : (e + 1) * P],
+            nc.tensor.matmul_mx(out=acc[:], lhsT=w1_codes[u][:, e * P : (e + 1) * P].bitcast(FP8X4), lhsT_scale=w1_plane[u][:, e * P : (e + 1) * P],
                                 rhs=x_codes[:, cols].bitcast(FP8X4), rhs_scale=x_plane[:, cols], start=True, stop=True)
 
-        banks = [psum.tile([P, S // 2], F32, name=f"y_ps0{h}") for h in range(2)]
-        for bank, half in zip(banks, halves):
-            first_product(bank, 0, half)
+        banks = [bank(h, [P, S // 2], f"y_ps0{h}") for h in range(2)]
+        for acc, half in zip(banks, halves):
+            first_product(acc, 0, half)
         nc.scalar.copy(y[0][:, halves[0]], banks[0][:])
-        nc.scalar.activation(m2[0][:, halves[0]], banks[0][:], COPY, scale=-2.0)
         nc.vector.tensor_copy(y[0][:, halves[1]], banks[1][:])
-        nc.scalar.activation(m2[0][:, halves[1]], banks[1][:], COPY, scale=-2.0)
         for t in range(1, PACK):
-            y_ps = psum.tile([P, S], F32, name=f"y_ps{t}")
+            y_ps = bank(1 + t, [P, S], f"y_ps{t}")
             first_product(y_ps, t, slice(0, S))
             nc.scalar.copy(y[t][:, 0:S], y_ps[:])
-            nc.scalar.activation(m2[t][:], y_ps[:], COPY, scale=-2.0)
 
         w2_codes = keep.tile([P, N], U32, name="w2_codes", align_bytes=64)
         w2_plane = keep.tile([P, N], U8, name="w2_plane", align_bytes=64)
         w2_grp = keep.tile([P, N, PACK], BF16, name="w2_grp", align_bytes=64)
-        nc.scalar.copy(w2_grp[:].rearrange("p (c i) t -> p c t i", i=4), w2_raw[:].rearrange("p t (c i) -> p c t i", i=4))
 
-        s1 = [keep.tile([P, S], F32, name=f"s1_{t}") for t in range(PACK)]
-        s2 = [keep.tile([P, S], F32, name=f"s2_{t}") for t in range(PACK)]
-        cs = keep.tile([P, NCH, PACK, CH], F32, name="cs")
-        dn = keep.tile([P, NCH, PACK, CH], F32, name="dn")
+        def weave_w2(q):
+            cols = slice(q * P, (q + 1) * P)
+            nc.scalar.copy(w2_grp[:, cols].rearrange("p (c i) t -> p c t i", i=4), w2_raw[:, :, cols].rearrange("p t (c i) -> p c t i", i=4))
+
         out_rows = out.rearrange("(g p) j -> p g j", p=P)
-        z_grp = {}
 
-        def east_gather(t, j0, j1):
-            nc.vector.tensor_tensor(s1[t][:, j0:j1], y[t][:].indirect(east_t[:, j0 // 16 : j1 // 16]), m2[t][:, j0:j1], ADD)
-
-        def west_gather(t, j0, j1):
-            nc.vector.tensor_tensor(s2[t][:, j0:j1], y[t][:].indirect(west_t[:, j0 // 16 : j1 // 16]), s1[t][:, j0:j1], ADD)
-
-        def chunked(ap):
-            return ap.rearrange("p (b j) -> p b j", j=CH)
-
-        def times_c(t, b0, b1):
-            cols = slice(b0 * CH, b1 * CH)
-            nc.vector.tensor_tensor(cs[:, b0:b1, t, :], chunked(s2[t][:, cols]), chunked(c_t[:, cols]), MULT)
-
-        def make_dn(t):
-            nc.vector.tensor_tensor(dn[:, :, t, :], chunked(m2[t][:]), chunked(prev_t[:, t, :]), ADD)
-
-        def make_z(b):
-            z_grp[b] = keep.tile([P, CH, PACK], BF16, name=f"z_grp{b}", align_bytes=64)
-            nc.vector.tensor_tensor(z_grp[b][:].rearrange("p (c i) t -> p c t i", i=4), cs[:, b].rearrange("p t (c i) -> p c t i", i=4),
-                                    dn[:, b].rearrange("p t (c i) -> p c t i", i=4), SUB)
-
-        def finish(b):
+        def finish(b, z_grp, parts):
             z_codes = keep.tile([P, CH], U32, name=f"z_codes{b}", align_bytes=64)
             z_plane = keep.tile([P, CH], U8, name=f"z_plane{b}", align_bytes=64)
-            nc.vector.quantize_mx(out=z_codes[:].bitcast(FP8X4), scales=z_plane[:], in_=z_grp[b][:].rearrange("p j t -> p (j t)"))
-            parts = [(0, 2, nc.scalar.copy, nc.scalar), (2, 4, nc.vector.tensor_copy, nc.sync)] if b == NCH - 1 else [(0, 4, nc.scalar.copy, nc.sync)]
-            for g0, g1, copy, queue in parts:
-                o_ps = psum.tile([P, g1 - g0, CH], F32, name=f"o_ps{b}_{g0}", tag="o", bufs=3)
+            nc.vector.quantize_mx(out=z_codes[:].bitcast(FP8X4), scales=z_plane[:], in_=z_grp[:].rearrange("p j t -> p (j t)"))
+            for g0, g1, i, copy, queue in parts:
+                o_ps = bank(i, [P, g1 - g0, CH], f"o_ps{b}_{g0}")
                 for g in range(g0, g1):
                     cols = slice(g * P, (g + 1) * P)
                     nc.tensor.matmul_mx(out=o_ps[:, g - g0, :], lhsT=w2_codes[:, cols].bitcast(FP8X4), lhsT_scale=w2_plane[:, cols],
@@ -149,29 +149,51 @@ def tile_picked_waveeq_none_p_kernel(tc, x_words, x_scales, w1, prev, c2, w2, of
                 copy(o_sb[:], o_ps[:])
                 queue.dma_start(out_rows[:, g0:g1, b * CH : (b + 1) * CH], o_sb[:])
 
-        for half in halves:
-            east_gather(0, half.start, half.stop)
-        for half in halves:
-            west_gather(0, half.start, half.stop)
-        for t in range(1, PACK):
-            if t < PACK - 1:
-                east_gather(t, 0, S)
-                times_c(t - 1, 0, NCH)
-                west_gather(t, 0, S)
-            else:
-                east_gather(t, 0, S // 2)
-                times_c(t - 1, 0, NCH)
-                east_gather(t, S // 2, S)
-            make_dn(t - 1)
-        last = PACK - 1
-        make_dn(last)
+        ce = [keep.tile([P, S], F32, name=f"ce{t}") for t in range(PACK)]
+        cw = keep.tile([P, PACK, S], F32, name="cw")
+        y_turned = [bank((5, 6, 7, 0)[b], [P, PACK, P], f"y_turned{b}") for b in range(NCH)]
+        e_turned = [bank(1 + b, [P, PACK, P], f"e_turned{b}") for b in range(NCH)]
+        z_grp = [keep.tile([P, CH, PACK], BF16, name=f"z_grp{b}", align_bytes=64) for b in range(NCH)]
+        ay = [keep.tile([P, PACK, P], F32, name=f"ay{b}") for b in range(NCH)]
+        ep = [keep.tile([P, PACK, P], F32, name=f"ep{b}") for b in range(NCH)]
+        rest = {}
+
+        def turn_slab(t, chunks):
+            for b in chunks:
+                cols = slice(b * CH, (b + 1) * CH)
+                turn(e_turned[b][:, t, :], prev_t[:, t, cols], True, False)
+                turn(e_turned[b][:, t, :], ce[t][:, cols], False, True)
+
+        def make_rest(b):
+            nc.scalar.activation(ep[b][:], e_turned[b][:], COPY, scale=-1.0)
+            rest[b] = bank((5, 6, 7, 0)[b], [P, PACK, CH], f"rest{b}")
+            for t in range(PACK):
+                turn(rest[b][:, t, :], ay[b][:, t, :], True, False)
+                turn(rest[b][:, t, :], ep[b][:, t, :], False, True)
+
+        def make_z(b):
+            cols = slice(b * CH, (b + 1) * CH)
+            nc.vector.tensor_tensor(z_grp[b][:].rearrange("p (c i) t -> p c t i", i=4), cw[:, :, cols].rearrange("p t (c i) -> p c t i", i=4),
+                                    rest[b][:].rearrange("p t (c i) -> p c t i", i=4), ADD)
+
+        for b in range(NCH):
+            for t in range(PACK):
+                turn(y_turned[b][:, t, :], y[t][:, b * CH : (b + 1) * CH])
+            nc.scalar.activation(ay[b][:], y_turned[b][:], COPY, scale=a_col[:, b : b + 1])
+        for t in range(PACK):
+            nc.vector.tensor_tensor(ce[t][:], y[t][:].indirect(east_t[:]), c_neg[:], MULT)
+            turn_slab(t, range(NCH))
+        for q in range(PACK):
+            weave_w2(q)
+        for t in range(PACK):
+            nc.vector.tensor_tensor(cw[:, t, :], y[t][:].indirect(west_t[:]), c_row[:], MULT)
+            make_rest(t)
         nc.vector.quantize_mx(out=w2_codes[:].bitcast(FP8X4), scales=w2_plane[:], in_=w2_grp[:].rearrange("p c t -> p (c t)"))
-        for step in range(NCH + 3):
-            if step < NCH:
-                west_gather(last, step * CH, (step + 1) * CH)
-            if 0 <= step - 3 < NCH:
-                finish(step - 3)
-            if 0 <= step - 1 < NCH:
-                times_c(last, step - 1, step)
-            if 0 <= step - 2 < NCH:
-                make_z(step - 2)
+        make_z(0)
+        make_z(1)
+        finish(0, z_grp[0], [(0, 4, 1, nc.scalar.copy, nc.sync)])
+        make_z(2)
+        finish(1, z_grp[1], [(0, 4, 2, nc.scalar.copy, nc.sync)])
+        make_z(3)
+        finish(2, z_grp[2], [(0, 4, 3, nc.scalar.copy, nc.sync)])
+        finish(3, z_grp[3], [(0, 2, 4, nc.scalar.copy, nc.scalar), (2, 4, 5, nc.vector.tensor_copy, nc.sync)])

@@ -46,16 +46,16 @@ def tile_picked_waveeq_none_p_kernel(tc, x_words, x_scales, w1, prev, c2, w2, of
         nc.sync.dma_start(west_t[:], west)
         for r in range(2):
             nc.sync.dma_start(scale_win[r:P:16, :].bitcast(I32), x_scales[0, r:16:2, :].bitcast(I32))
-        c_col = keep.tile([P, NCH], F32, name="c_col")
-        with nc.allow_non_contiguous_dma(reason="one value a partition"):
-            nc.sync.dma_start(c_col[:], c2[0].rearrange("(b p) -> p b", p=P))
+        c_sq = keep.tile([P, P], F32, name="c_sq")
+        nc.vector.memset(c_sq[:], 0.0)
+        nc.sync.dma_start(c_sq[0:NCH, :], c2[0].rearrange("(b j) -> b j", j=CH))
         w1_raw = keep.tile([P, PACK, H], F32, name="w1_raw", tag="raw")
         nc.sync.dma_start(w1_raw[:], w1.rearrange("(p j) c -> p j c", j=PACK))
         nc.sync.dma_start(word_win[:, XA:].bitcast(I32), word_rows[:, XA:])
 
+        x_plane = keep.tile([P, S], U8, name="x_plane", align_bytes=64)
         scale_got = keep.tile([P, S], U8, name="scale_got")
         nc.vector.tensor_copy(scale_got[:], scale_win[:].indirect(offs_t[:]))
-        x_plane = keep.tile([P, S], U8, name="x_plane", align_bytes=64)
         nc.vector.tensor_copy(x_plane[:].bitcast(I32), scale_got[:].bitcast(I32))
         for r in range(2):
             nc.sync.dma_start(x_plane[2 + r : P : 32, :].bitcast(I32), scale_got[16 + r : P : 32, :].bitcast(I32))
@@ -82,22 +82,28 @@ def tile_picked_waveeq_none_p_kernel(tc, x_words, x_scales, w1, prev, c2, w2, of
         def turn(target, src, start=True, stop=True):
             nc.tensor.matmul(target, lhsT=src, rhs=ident[:], start=start, stop=stop, is_transpose=True)
 
-        c_ps = bank(7, [P, NCH, CH], "c_ps")
-        for b in range(NCH):
-            turn(c_ps[:, b, :], c_col[:, b : b + 1].to_broadcast([P, P]))
-        c_neg = keep.tile([P, S], F32, name="c_neg")
-        c_row = keep.tile([P, S], F32, name="c_row")
+        c_turned = bank(6, [P, P], "c_turned")
+        turn(c_turned[:], c_sq[:])
         a_col = keep.tile([P, NCH], F32, name="a_col")
-        nc.scalar.activation(c_neg[:], c_ps[:].rearrange("p b j -> p (b j)"), COPY, scale=-1.0)
-        nc.scalar.copy(c_row[:], c_ps[:].rearrange("p b j -> p (b j)"))
-        nc.scalar.activation(a_col[:], c_col[:], COPY, scale=-2.0, bias=2.0)
+        c_col = keep.tile([P, NCH], F32, name="c_col")
+        nc.scalar.copy(c_col[:], c_turned[:, 0:NCH])
+        nc.scalar.activation(a_col[:], c_turned[:, 0:NCH], COPY, scale=-2.0, bias=2.0)
 
-        w1_codes = [keep.tile([P, 2 * P], U32, name=f"w1_codes{u}", align_bytes=64) for u in range(2)]
-        w1_plane = [keep.tile([P, 2 * P], U8, name=f"w1_plane{u}", align_bytes=64) for u in range(2)]
+        c_ps = bank(7, [P, 2, CH], "c_ps")
+        for b in range(2):
+            turn(c_ps[:, b, :], c_col[:, 2 + b : 3 + b].to_broadcast([P, P]))
+        k_row = keep.tile([P, S], F32, name="k_row")
+        c_row = keep.tile([P, S // 2], F32, name="c_row")
+        nc.vector.memset(k_row[:, 0 : S // 2], 1.0)
+        nc.scalar.activation(k_row[:, S // 2 :], c_ps[:].rearrange("p b j -> p (b j)"), COPY, scale=-1.0)
+        nc.scalar.copy(c_row[:], c_ps[:].rearrange("p b j -> p (b j)"))
+
+        w1_codes = keep.tile([P, H], U32, name="w1_codes", align_bytes=64)
+        w1_plane = keep.tile([P, H], U8, name="w1_plane", align_bytes=64)
         for u, copy in enumerate((nc.vector.tensor_copy, nc.scalar.copy)):
             grp = keep.tile([P, 2, P, PACK], BF16, name=f"w1_grp{u}", tag=f"w1_grp{u}", align_bytes=64)
             copy(grp[:].rearrange("p t m j -> p m t j"), w1_raw[:].rearrange("p j (m t) -> p m t j", t=PACK)[:, :, 2 * u : 2 * u + 2])
-            nc.vector.quantize_mx(out=w1_codes[u][:].bitcast(FP8X4), scales=w1_plane[u][:], in_=grp[:].rearrange("p t m j -> p (t m j)"))
+            nc.vector.quantize_mx(out=w1_codes[:, 2 * u * P : 2 * (u + 1) * P].bitcast(FP8X4), scales=w1_plane[:, 2 * u * P : 2 * (u + 1) * P], in_=grp[:].rearrange("p t m j -> p (t m j)"))
 
         halves = [slice(0, S // 2), slice(S // 2, S)]
         x_codes = keep.tile([P, S], U32, name="x_codes", align_bytes=64)
@@ -106,13 +112,12 @@ def tile_picked_waveeq_none_p_kernel(tc, x_words, x_scales, w1, prev, c2, w2, of
 
         prev_t = keep.tile([P, PACK, S], F32, name="prev_t", tag="raw")
         nc.sync.dma_start(prev_t[:], prev.rearrange("(p t) j -> p t j", t=PACK))
-        w2_raw = keep.tile([P, PACK, N], F32, name="w2_raw", tag="words")
+        w2_raw = keep.tile([P, PACK, N], F32, name="w2_raw", tag="w1_grp1", align_bytes=64)
         nc.sync.dma_start(w2_raw[:], w2.rearrange("(p j) c -> p j c", j=PACK))
 
 
         def first_product(acc, t, cols):
-            u, e = divmod(t, 2)
-            nc.tensor.matmul_mx(out=acc[:], lhsT=w1_codes[u][:, e * P : (e + 1) * P].bitcast(FP8X4), lhsT_scale=w1_plane[u][:, e * P : (e + 1) * P],
+            nc.tensor.matmul_mx(out=acc[:], lhsT=w1_codes[:, t * P : (t + 1) * P].bitcast(FP8X4), lhsT_scale=w1_plane[:, t * P : (t + 1) * P],
                                 rhs=x_codes[:, cols].bitcast(FP8X4), rhs_scale=x_plane[:, cols], start=True, stop=True)
 
         banks = [bank(h, [P, S // 2], f"y_ps0{h}") for h in range(2)]
@@ -138,62 +143,91 @@ def tile_picked_waveeq_none_p_kernel(tc, x_words, x_scales, w1, prev, c2, w2, of
         def finish(b, z_grp, parts):
             z_codes = keep.tile([P, CH], U32, name=f"z_codes{b}", align_bytes=64)
             z_plane = keep.tile([P, CH], U8, name=f"z_plane{b}", align_bytes=64)
-            nc.vector.quantize_mx(out=z_codes[:].bitcast(FP8X4), scales=z_plane[:], in_=z_grp[:].rearrange("p j t -> p (j t)"))
+            nc.vector.quantize_mx(out=z_codes[:].bitcast(FP8X4), scales=z_plane[:], in_=z_grp.rearrange("p j t -> p (j t)"))
+            ways = []
             for g0, g1, i, copy, queue in parts:
                 o_ps = bank(i, [P, g1 - g0, CH], f"o_ps{b}_{g0}")
                 for g in range(g0, g1):
                     cols = slice(g * P, (g + 1) * P)
                     nc.tensor.matmul_mx(out=o_ps[:, g - g0, :], lhsT=w2_codes[:, cols].bitcast(FP8X4), lhsT_scale=w2_plane[:, cols],
                                         rhs=z_codes[:].bitcast(FP8X4), rhs_scale=z_plane[:], start=True, stop=True)
+                ways.append((b, g0, g1, o_ps, copy, queue))
+            return ways
+
+        def store(ways):
+            for b, g0, g1, o_ps, copy, queue in ways:
                 o_sb = keep.tile([P, g1 - g0, CH], F32, name=f"o_sb{b}_{g0}")
                 copy(o_sb[:], o_ps[:])
                 queue.dma_start(out_rows[:, g0:g1, b * CH : (b + 1) * CH], o_sb[:])
 
-        ce = [keep.tile([P, S], F32, name=f"ce{t}") for t in range(PACK)]
-        cw = keep.tile([P, PACK, S], F32, name="cw")
-        y_turned = [bank((5, 6, 7, 0)[b], [P, PACK, P], f"y_turned{b}") for b in range(NCH)]
-        e_turned = [bank(1 + b, [P, PACK, P], f"e_turned{b}") for b in range(NCH)]
-        z_grp = [keep.tile([P, CH, PACK], BF16, name=f"z_grp{b}", align_bytes=64) for b in range(NCH)]
-        ay = [keep.tile([P, PACK, P], F32, name=f"ay{b}") for b in range(NCH)]
-        ep = [keep.tile([P, PACK, P], F32, name=f"ep{b}") for b in range(NCH)]
-        rest = {}
 
-        def turn_slab(t, chunks):
-            for b in chunks:
-                cols = slice(b * CH, (b + 1) * CH)
-                turn(e_turned[b][:, t, :], prev_t[:, t, cols], True, False)
-                turn(e_turned[b][:, t, :], ce[t][:, cols], False, True)
+        HALF = S // 2
+        ke = [keep.tile([P, S], F32, name=f"ke{t}") for t in range(PACK)]
+        sw = [keep.tile([P, HALF], F32, name=f"sw{t}") for t in range(PACK)]
+        cw = keep.tile([P, PACK, HALF], F32, name="cw", align_bytes=64)
+        z_grp = [keep.tile([P, CH, PACK], BF16, name=f"z_grp{b}", align_bytes=64)[:] if b != 1 else
+                 cw[:, PACK - 1, :].bitcast(BF16).rearrange("p (j t) -> p j t", t=PACK) for b in range(NCH)]
+        ay = [keep.tile([P, PACK, P], F32, name=f"ay{b}") for b in range(NCH)]
+        part = [keep.tile([P, PACK, P], F32, name=f"part{b}") for b in range(NCH)]
+        home = (5, 6, 7, 0)
+        rest = {}
+        for b in range(NCH):
+            cols = slice(b * CH, (b + 1) * CH)
+            y_turned = bank(home[b], [P, PACK, P], f"y_turned{b}")
+            if b < 2:
+                nc.tensor.matmul_mx(out=y_turned[:].rearrange("j t p -> j (t p)"), lhsT=x_codes[:, cols].bitcast(FP8X4), lhsT_scale=x_plane[:, cols],
+                                    rhs=w1_codes[:].bitcast(FP8X4), rhs_scale=w1_plane[:], start=True, stop=True)
+            else:
+                for t in range(PACK):
+                    turn(y_turned[:, t, :], y[t][:, cols])
+            nc.scalar.activation(ay[b][:], y_turned[:], COPY, scale=a_col[:, b : b + 1])
+        turned = [bank(1 + b, [P, PACK, P], f"turned{b}") for b in range(NCH)]
+
+        def open_rest(b):
+            rest[b] = bank(home[b], [P, PACK, CH], f"rest{b}")
+            for t in range(PACK):
+                turn(rest[b][:, t, :], ay[b][:, t, :], t == 0, False)
 
         def make_rest(b):
-            nc.scalar.activation(ep[b][:], e_turned[b][:], COPY, scale=-1.0)
-            rest[b] = bank((5, 6, 7, 0)[b], [P, PACK, CH], f"rest{b}")
+            nc.scalar.activation(part[b][:], turned[b][:], COPY, scale=c_col[:, b : b + 1] if b < 2 else -1.0)
             for t in range(PACK):
-                turn(rest[b][:, t, :], ay[b][:, t, :], True, False)
-                turn(rest[b][:, t, :], ep[b][:, t, :], False, True)
+                turn(rest[b][:, t, :], part[b][:, t, :], False, t == PACK - 1)
 
         def make_z(b):
-            cols = slice(b * CH, (b + 1) * CH)
-            nc.vector.tensor_tensor(z_grp[b][:].rearrange("p (c i) t -> p c t i", i=4), cw[:, :, cols].rearrange("p t (c i) -> p c t i", i=4),
-                                    rest[b][:].rearrange("p t (c i) -> p c t i", i=4), ADD)
+            other = prev_t[:, :, b * CH : (b + 1) * CH] if b < 2 else cw[:, :, (b - 2) * CH : (b - 1) * CH]
+            nc.vector.tensor_tensor(z_grp[b].rearrange("p (c i) t -> p c t i", i=4), rest[b][:].rearrange("p t (c i) -> p c t i", i=4),
+                                    other.rearrange("p t (c i) -> p c t i", i=4), SUB if b < 2 else ADD)
 
-        for b in range(NCH):
+        open_rest(0)
+        open_rest(1)
+        for b in range(2, NCH):
             for t in range(PACK):
-                turn(y_turned[b][:, t, :], y[t][:, b * CH : (b + 1) * CH])
-            nc.scalar.activation(ay[b][:], y_turned[b][:], COPY, scale=a_col[:, b : b + 1])
+                turn(turned[b][:, t, :], prev_t[:, t, b * CH : (b + 1) * CH], t == 0, False)
         for t in range(PACK):
-            nc.vector.tensor_tensor(ce[t][:], y[t][:].indirect(east_t[:]), c_neg[:], MULT)
-            turn_slab(t, range(NCH))
+            nc.vector.tensor_tensor(ke[t][:], y[t][:].indirect(east_t[:]), k_row[:], MULT)
+            for b in range(2, NCH):
+                turn(turned[b][:, t, :], ke[t][:, b * CH : (b + 1) * CH], False, t == PACK - 1)
+        open_rest(2)
+        open_rest(3)
         for q in range(PACK):
             weave_w2(q)
         for t in range(PACK):
-            nc.vector.tensor_tensor(cw[:, t, :], y[t][:].indirect(west_t[:]), c_row[:], MULT)
-            make_rest(t)
+            nc.vector.tensor_tensor(sw[t][:], y[t][:].indirect(west_t[:, 0:16]), ke[t][:, halves[0]], ADD)
+            for b in range(2):
+                turn(turned[b][:, t, :], sw[t][:, b * CH : (b + 1) * CH])
+        make_rest(2)
+        make_rest(3)
+        make_rest(0)
+        make_rest(1)
+        for t in range(PACK - 1):
+            nc.vector.tensor_tensor(cw[:, t, :], y[t][:].indirect(west_t[:, 16:32]), c_row[:], MULT)
         nc.vector.quantize_mx(out=w2_codes[:].bitcast(FP8X4), scales=w2_plane[:], in_=w2_grp[:].rearrange("p c t -> p (c t)"))
         make_z(0)
         make_z(1)
-        finish(0, z_grp[0], [(0, 4, 1, nc.scalar.copy, nc.sync)])
+        store(finish(0, z_grp[0], [(0, 4, 3, nc.scalar.copy, nc.sync)]))
+        store(finish(1, z_grp[1], [(0, 4, 4, nc.scalar.copy, nc.sync)]))
+        nc.vector.tensor_tensor(cw[:, PACK - 1, :], y[PACK - 1][:].indirect(west_t[:, 16:32]), c_row[:], MULT)
         make_z(2)
-        finish(1, z_grp[1], [(0, 4, 2, nc.scalar.copy, nc.sync)])
+        ways = finish(2, z_grp[2], [(0, 2, 1, nc.scalar.copy, nc.sync), (2, 4, 2, nc.vector.tensor_copy, nc.sync)])
         make_z(3)
-        finish(2, z_grp[2], [(0, 4, 3, nc.scalar.copy, nc.sync)])
-        finish(3, z_grp[3], [(0, 2, 4, nc.scalar.copy, nc.scalar), (2, 4, 5, nc.vector.tensor_copy, nc.sync)])
+        store(ways + finish(3, z_grp[3], [(0, 2, 5, nc.scalar.copy, nc.scalar), (2, 4, 6, nc.vector.tensor_copy, nc.sync)]))

@@ -110,10 +110,14 @@ def tile_picked_waveeq_none_p_kernel(tc, x_words, x_scales, w1, prev, c2, w2, of
         for h, half in enumerate(halves):
             nc.vector.tensor_copy(x_codes[:, half], word_win[:].indirect(offs_t[:, 16 * h : 16 * h + 16]))
 
-        prev_t = keep.tile([P, PACK, S], F32, name="prev_t", tag="raw")
-        nc.sync.dma_start(prev_t[:], prev.rearrange("(p t) j -> p t j", t=PACK))
+        prev_rows = prev.rearrange("(p t) j -> p t j", t=PACK)
+        prev_t = keep.tile([P, PACK, S - CH], F32, name="prev_t", tag="raw")
+        nc.sync.dma_start(prev_t[:], prev_rows[:, :, CH:])
         w2_raw = keep.tile([P, PACK, N], F32, name="w2_raw", tag="w1_grp1", align_bytes=64)
         nc.sync.dma_start(w2_raw[:], w2.rearrange("(p j) c -> p j c", j=PACK))
+        cw = keep.tile([P, PACK + 1, S // 2], F32, name="cw", tag="words")
+        prev_0 = cw[:, PACK - 1 :, :].rearrange("p a (b j) -> p (a b) j", j=CH)
+        nc.sync.dma_start(prev_0, prev_rows[:, :, 0:CH])
 
 
         def first_product(acc, t, cols):
@@ -140,35 +144,36 @@ def tile_picked_waveeq_none_p_kernel(tc, x_words, x_scales, w1, prev, c2, w2, of
 
         out_rows = out.rearrange("(g p) j -> p g j", p=P)
 
-        def finish(b, z_grp, parts):
-            z_codes = keep.tile([P, CH], U32, name=f"z_codes{b}", align_bytes=64)
-            z_plane = keep.tile([P, CH], U8, name=f"z_plane{b}", align_bytes=64)
-            nc.vector.quantize_mx(out=z_codes[:].bitcast(FP8X4), scales=z_plane[:], in_=z_grp.rearrange("p j t -> p (j t)"))
+        def finish(j0, j1, z, parts):
+            z_codes = keep.tile([P, j1 - j0], U32, name=f"z_codes{j0}", align_bytes=64)
+            z_plane = keep.tile([P, j1 - j0], U8, name=f"z_plane{j0}", align_bytes=64)
+            nc.vector.quantize_mx(out=z_codes[:].bitcast(FP8X4), scales=z_plane[:], in_=z.rearrange("p j t -> p (j t)"))
             ways = []
-            for g0, g1, i, copy, queue in parts:
-                o_ps = bank(i, [P, g1 - g0, CH], f"o_ps{b}_{g0}")
-                for g in range(g0, g1):
+            for g0, i, copy, queue in parts:
+                o_ps = bank(i, [P, 2, j1 - j0], f"o_ps{j0}_{g0}")
+                for g in range(g0, g0 + 2):
                     cols = slice(g * P, (g + 1) * P)
                     nc.tensor.matmul_mx(out=o_ps[:, g - g0, :], lhsT=w2_codes[:, cols].bitcast(FP8X4), lhsT_scale=w2_plane[:, cols],
                                         rhs=z_codes[:].bitcast(FP8X4), rhs_scale=z_plane[:], start=True, stop=True)
-                ways.append((b, g0, g1, o_ps, copy, queue))
+                ways.append((j0, j1, g0, o_ps, copy, queue))
             return ways
 
         def store(ways):
-            for b, g0, g1, o_ps, copy, queue in ways:
-                o_sb = keep.tile([P, g1 - g0, CH], F32, name=f"o_sb{b}_{g0}")
+            for j0, j1, g0, o_ps, copy, queue in ways:
+                o_sb = keep.tile([P, 2, j1 - j0], F32, name=f"o_sb{j0}_{g0}")
                 copy(o_sb[:], o_ps[:])
-                queue.dma_start(out_rows[:, g0:g1, b * CH : (b + 1) * CH], o_sb[:])
-
+                queue.dma_start(out_rows[:, g0 : g0 + 2, j0:j1], o_sb[:])
 
         HALF = S // 2
-        ke = [keep.tile([P, S], F32, name=f"ke{t}") for t in range(PACK)]
-        sw = [keep.tile([P, HALF], F32, name=f"sw{t}") for t in range(PACK)]
-        cw = keep.tile([P, PACK, HALF], F32, name="cw", align_bytes=64)
-        z_grp = [keep.tile([P, CH, PACK], BF16, name=f"z_grp{b}", align_bytes=64)[:] if b != 1 else
-                 cw[:, PACK - 1, :].bitcast(BF16).rearrange("p (j t) -> p j t", t=PACK) for b in range(NCH)]
+        ke = [keep.tile([P, S], F32, name=f"ke{t}")[:] for t in range(PACK - 1)]
+        ke.append(cw[:].rearrange("p a w -> p (a w)")[:, CH : CH + S])
+        sw = [keep.tile([P, HALF], F32, name=f"sw{t}", tag=f"sw{t}") for t in range(PACK)]
+        z_tile = keep.tile([P, HALF, PACK], BF16, name="z_tile", align_bytes=64)
+        z_left = z_tile[:]
+        z_grp = [z_left[:, b * CH : (b + 1) * CH] for b in range(2)]
+        z_grp += [keep.tile([P, CH, PACK], BF16, name=f"z_grp{b}", align_bytes=64)[:] for b in range(2, NCH)]
         ay = [keep.tile([P, PACK, P], F32, name=f"ay{b}") for b in range(NCH)]
-        part = [keep.tile([P, PACK, P], F32, name=f"part{b}") for b in range(NCH)]
+        part = [keep.tile([P, PACK, P], F32, name=f"part{b}")[:] for b in range(2)]
         home = (5, 6, 7, 0)
         rest = {}
         for b in range(NCH):
@@ -189,12 +194,12 @@ def tile_picked_waveeq_none_p_kernel(tc, x_words, x_scales, w1, prev, c2, w2, of
                 turn(rest[b][:, t, :], ay[b][:, t, :], t == 0, False)
 
         def make_rest(b):
-            nc.scalar.activation(part[b][:], turned[b][:], COPY, scale=c_col[:, b : b + 1] if b < 2 else -1.0)
+            nc.scalar.activation(part[b], turned[b][:], COPY, scale=c_col[:, b : b + 1] if b < 2 else -1.0)
             for t in range(PACK):
                 turn(rest[b][:, t, :], part[b][:, t, :], False, t == PACK - 1)
 
         def make_z(b):
-            other = prev_t[:, :, b * CH : (b + 1) * CH] if b < 2 else cw[:, :, (b - 2) * CH : (b - 1) * CH]
+            other = (prev_0, prev_t[:, :, 0:CH], cw[:, 0:PACK, 0:CH], cw[:, 0:PACK, CH:])[b]
             nc.vector.tensor_tensor(z_grp[b].rearrange("p (c i) t -> p c t i", i=4), rest[b][:].rearrange("p t (c i) -> p c t i", i=4),
                                     other.rearrange("p t (c i) -> p c t i", i=4), SUB if b < 2 else ADD)
 
@@ -202,32 +207,31 @@ def tile_picked_waveeq_none_p_kernel(tc, x_words, x_scales, w1, prev, c2, w2, of
         open_rest(1)
         for b in range(2, NCH):
             for t in range(PACK):
-                turn(turned[b][:, t, :], prev_t[:, t, b * CH : (b + 1) * CH], t == 0, False)
+                turn(turned[b][:, t, :], prev_t[:, t, (b - 1) * CH : b * CH], t == 0, False)
         for t in range(PACK):
-            nc.vector.tensor_tensor(ke[t][:], y[t][:].indirect(east_t[:]), k_row[:], MULT)
+            nc.vector.tensor_tensor(ke[t], y[t][:].indirect(east_t[:]), k_row[:], MULT)
             for b in range(2, NCH):
                 turn(turned[b][:, t, :], ke[t][:, b * CH : (b + 1) * CH], False, t == PACK - 1)
-        open_rest(2)
-        open_rest(3)
         for q in range(PACK):
             weave_w2(q)
         for t in range(PACK):
             nc.vector.tensor_tensor(sw[t][:], y[t][:].indirect(west_t[:, 0:16]), ke[t][:, halves[0]], ADD)
             for b in range(2):
                 turn(turned[b][:, t, :], sw[t][:, b * CH : (b + 1) * CH])
-        make_rest(2)
-        make_rest(3)
-        make_rest(0)
-        make_rest(1)
+        open_rest(2)
+        open_rest(3)
+        part_right = keep.tile([P, 2, PACK, P], F32, name="part_right", tag=f"sw{PACK - 1}")
+        part += [part_right[:, 0], part_right[:, 1]]
+        for b in range(NCH):
+            make_rest(b)
         for t in range(PACK - 1):
             nc.vector.tensor_tensor(cw[:, t, :], y[t][:].indirect(west_t[:, 16:32]), c_row[:], MULT)
         nc.vector.quantize_mx(out=w2_codes[:].bitcast(FP8X4), scales=w2_plane[:], in_=w2_grp[:].rearrange("p c t -> p (c t)"))
         make_z(0)
         make_z(1)
-        store(finish(0, z_grp[0], [(0, 4, 3, nc.scalar.copy, nc.sync)]))
-        store(finish(1, z_grp[1], [(0, 4, 4, nc.scalar.copy, nc.sync)]))
         nc.vector.tensor_tensor(cw[:, PACK - 1, :], y[PACK - 1][:].indirect(west_t[:, 16:32]), c_row[:], MULT)
+        store(finish(0, HALF, z_left, [(0, 1, nc.scalar.copy, nc.sync), (2, 2, nc.scalar.copy, nc.sync)]))
         make_z(2)
-        ways = finish(2, z_grp[2], [(0, 2, 1, nc.scalar.copy, nc.sync), (2, 4, 2, nc.vector.tensor_copy, nc.sync)])
+        ways = finish(2 * CH, 3 * CH, z_grp[2], [(0, 3, nc.scalar.copy, nc.sync), (2, 4, nc.vector.tensor_copy, nc.sync)])
         make_z(3)
-        store(ways + finish(3, z_grp[3], [(0, 2, 5, nc.scalar.copy, nc.scalar), (2, 4, 6, nc.vector.tensor_copy, nc.sync)]))
+        store(ways + finish(3 * CH, S, z_grp[3], [(0, 5, nc.scalar.copy, nc.scalar), (2, 6, nc.vector.tensor_copy, nc.sync)]))

@@ -40,10 +40,9 @@ def tile_picked_waveeq_none_p_kernel(tc, x_words, x_scales, w1, prev, c2, w2, of
         nc.vector.memset(scale_win[:].bitcast(I32), 0)
         word_win = keep.tile([P, T], U32, name="word_win", tag="words")
         word_rows = x_words[0].rearrange("p c r -> p (c r)").bitcast(I32)
-        nc.sync.dma_start(word_win[:, 0:XA].bitcast(I32), word_rows[:, 0:XA])
+        nc.sync.dma_start(word_win[:, 0 : XA // 2].bitcast(I32), word_rows[:, 0 : XA // 2])
         nc.sync.dma_start(offs_t[:], offs)
-        nc.sync.dma_start(east_t[:], east)
-        nc.sync.dma_start(west_t[:], west)
+        nc.sync.dma_start(word_win[:, XA // 2 : XA].bitcast(I32), word_rows[:, XA // 2 : XA])
         for r in range(2):
             nc.sync.dma_start(scale_win[r:P:16, :].bitcast(I32), x_scales[0, r:16:2, :].bitcast(I32))
         c_sq = keep.tile([P, P], F32, name="c_sq")
@@ -52,6 +51,8 @@ def tile_picked_waveeq_none_p_kernel(tc, x_words, x_scales, w1, prev, c2, w2, of
         w1_raw = keep.tile([P, PACK, H], F32, name="w1_raw", tag="raw")
         nc.sync.dma_start(w1_raw[:], w1.rearrange("(p j) c -> p j c", j=PACK))
         nc.sync.dma_start(word_win[:, XA:].bitcast(I32), word_rows[:, XA:])
+        nc.sync.dma_start(east_t[:], east)
+        nc.sync.dma_start(west_t[:], west)
 
         x_plane = keep.tile([P, S], U8, name="x_plane", align_bytes=64)
         scale_got = keep.tile([P, S], U8, name="scale_got")
@@ -89,15 +90,6 @@ def tile_picked_waveeq_none_p_kernel(tc, x_words, x_scales, w1, prev, c2, w2, of
         nc.scalar.copy(c_col[:], c_turned[:, 0:NCH])
         nc.scalar.activation(a_col[:], c_turned[:, 0:NCH], COPY, scale=-2.0, bias=2.0)
 
-        c_ps = bank(7, [P, 2, CH], "c_ps")
-        for b in range(2):
-            turn(c_ps[:, b, :], c_col[:, 2 + b : 3 + b].to_broadcast([P, P]))
-        k_row = keep.tile([P, S], F32, name="k_row")
-        c_row = keep.tile([P, S // 2], F32, name="c_row")
-        nc.vector.memset(k_row[:, 0 : S // 2], 1.0)
-        nc.scalar.activation(k_row[:, S // 2 :], c_ps[:].rearrange("p b j -> p (b j)"), COPY, scale=-1.0)
-        nc.scalar.copy(c_row[:], c_ps[:].rearrange("p b j -> p (b j)"))
-
         w1_codes = keep.tile([P, H], U32, name="w1_codes", align_bytes=64)
         w1_plane = keep.tile([P, H], U8, name="w1_plane", align_bytes=64)
         for u, copy in enumerate((nc.vector.tensor_copy, nc.scalar.copy)):
@@ -110,6 +102,15 @@ def tile_picked_waveeq_none_p_kernel(tc, x_words, x_scales, w1, prev, c2, w2, of
         for h, half in enumerate(halves):
             nc.vector.tensor_copy(x_codes[:, half], word_win[:].indirect(offs_t[:, 16 * h : 16 * h + 16]))
 
+        c_ps = bank(7, [P, 2, CH], "c_ps")
+        for b in range(2):
+            turn(c_ps[:, b, :], c_col[:, 2 + b : 3 + b].to_broadcast([P, P]))
+        k_row = keep.tile([P, S], F32, name="k_row")
+        c_row = keep.tile([P, S // 2], F32, name="c_row")
+        nc.vector.memset(k_row[:, 0 : S // 2], 1.0)
+        nc.scalar.activation(k_row[:, S // 2 :], c_ps[:].rearrange("p b j -> p (b j)"), COPY, scale=-1.0)
+        nc.scalar.copy(c_row[:], c_ps[:].rearrange("p b j -> p (b j)"))
+
         prev_rows = prev.rearrange("(p t) j -> p t j", t=PACK)
         prev_t = keep.tile([P, PACK, S - CH], F32, name="prev_t", tag="raw")
         nc.sync.dma_start(prev_t[:], prev_rows[:, :, CH:])
@@ -121,17 +122,18 @@ def tile_picked_waveeq_none_p_kernel(tc, x_words, x_scales, w1, prev, c2, w2, of
 
 
         def first_product(acc, t, cols):
-            nc.tensor.matmul_mx(out=acc[:], lhsT=w1_codes[:, t * P : (t + 1) * P].bitcast(FP8X4), lhsT_scale=w1_plane[:, t * P : (t + 1) * P],
+            nc.tensor.matmul_mx(out=acc, lhsT=w1_codes[:, t * P : (t + 1) * P].bitcast(FP8X4), lhsT_scale=w1_plane[:, t * P : (t + 1) * P],
                                 rhs=x_codes[:, cols].bitcast(FP8X4), rhs_scale=x_plane[:, cols], start=True, stop=True)
 
-        banks = [bank(h, [P, S // 2], f"y_ps0{h}") for h in range(2)]
-        for acc, half in zip(banks, halves):
-            first_product(acc, 0, half)
-        nc.scalar.copy(y[0][:, halves[0]], banks[0][:])
-        nc.vector.tensor_copy(y[0][:, halves[1]], banks[1][:])
+        pieces = [(0, slice(0, S // 2), nc.scalar.copy), (1, slice(S // 2, S - CH), nc.vector.tensor_copy), (7, slice(S - CH, S), nc.scalar.copy)]
+        for i, cols, copy in pieces:
+            y_ps = bank(i, [P, cols.stop - cols.start], f"y_ps0_{i}")
+            first_product(y_ps[:], 0, cols)
+            copy(y[0][:, cols], y_ps[:])
         for t in range(1, PACK):
             y_ps = bank(1 + t, [P, S], f"y_ps{t}")
-            first_product(y_ps, t, slice(0, S))
+            for cols in halves if t == 1 else [slice(0, S)]:
+                first_product(y_ps[:, cols], t, cols)
             nc.scalar.copy(y[t][:, 0:S], y_ps[:])
 
         w2_codes = keep.tile([P, N], U32, name="w2_codes", align_bytes=64)
@@ -149,20 +151,22 @@ def tile_picked_waveeq_none_p_kernel(tc, x_words, x_scales, w1, prev, c2, w2, of
             z_plane = keep.tile([P, j1 - j0], U8, name=f"z_plane{j0}", align_bytes=64)
             nc.vector.quantize_mx(out=z_codes[:].bitcast(FP8X4), scales=z_plane[:], in_=z.rearrange("p j t -> p (j t)"))
             ways = []
-            for g0, i, copy, queue in parts:
-                o_ps = bank(i, [P, 2, j1 - j0], f"o_ps{j0}_{g0}")
-                for g in range(g0, g0 + 2):
+            width = PACK // len(parts)
+            for n, (i, copy, queue) in enumerate(parts):
+                g0 = n * width
+                o_ps = bank(i, [P, width, j1 - j0], f"o_ps{j0}_{g0}")
+                for g in range(g0, g0 + width):
                     cols = slice(g * P, (g + 1) * P)
                     nc.tensor.matmul_mx(out=o_ps[:, g - g0, :], lhsT=w2_codes[:, cols].bitcast(FP8X4), lhsT_scale=w2_plane[:, cols],
                                         rhs=z_codes[:].bitcast(FP8X4), rhs_scale=z_plane[:], start=True, stop=True)
-                ways.append((j0, j1, g0, o_ps, copy, queue))
+                ways.append((j0, j1, g0, width, o_ps, copy, queue))
             return ways
 
         def store(ways):
-            for j0, j1, g0, o_ps, copy, queue in ways:
-                o_sb = keep.tile([P, 2, j1 - j0], F32, name=f"o_sb{j0}_{g0}")
+            for j0, j1, g0, width, o_ps, copy, queue in ways:
+                o_sb = keep.tile([P, width, j1 - j0], F32, name=f"o_sb{j0}_{g0}")
                 copy(o_sb[:], o_ps[:])
-                queue.dma_start(out_rows[:, g0 : g0 + 2, j0:j1], o_sb[:])
+                queue.dma_start(out_rows[:, g0 : g0 + width, j0:j1], o_sb[:])
 
         HALF = S // 2
         ke = [keep.tile([P, S], F32, name=f"ke{t}")[:] for t in range(PACK - 1)]
@@ -172,23 +176,24 @@ def tile_picked_waveeq_none_p_kernel(tc, x_words, x_scales, w1, prev, c2, w2, of
         z_left = z_tile[:]
         z_grp = [z_left[:, b * CH : (b + 1) * CH] for b in range(2)]
         z_grp += [keep.tile([P, CH, PACK], BF16, name=f"z_grp{b}", align_bytes=64)[:] for b in range(2, NCH)]
-        ay = [keep.tile([P, PACK, P], F32, name=f"ay{b}") for b in range(NCH)]
+        ay = [keep.tile([P, PACK, P], F32, name=f"ay{b}")[:] for b in range(2)]
+        y_turned = []
         part = [keep.tile([P, PACK, P], F32, name=f"part{b}")[:] for b in range(2)]
         home = (5, 6, 7, 0)
         rest = {}
         for b in range(NCH):
             cols = slice(b * CH, (b + 1) * CH)
-            y_turned = bank(home[b], [P, PACK, P], f"y_turned{b}")
+            y_turned.append(bank(home[b], [P, PACK, P], f"y_turned{b}"))
             if b < 2:
-                nc.tensor.matmul_mx(out=y_turned[:].rearrange("j t p -> j (t p)"), lhsT=x_codes[:, cols].bitcast(FP8X4), lhsT_scale=x_plane[:, cols],
+                nc.tensor.matmul_mx(out=y_turned[b][:].rearrange("j t p -> j (t p)"), lhsT=x_codes[:, cols].bitcast(FP8X4), lhsT_scale=x_plane[:, cols],
                                     rhs=w1_codes[:].bitcast(FP8X4), rhs_scale=w1_plane[:], start=True, stop=True)
             else:
                 for t in range(PACK):
-                    turn(y_turned[:, t, :], y[t][:, cols])
-            nc.scalar.activation(ay[b][:], y_turned[:], COPY, scale=a_col[:, b : b + 1])
+                    turn(y_turned[b][:, t, :], y[t][:, cols])
         turned = [bank(1 + b, [P, PACK, P], f"turned{b}") for b in range(NCH)]
 
         def open_rest(b):
+            nc.scalar.activation(ay[b], y_turned[b][:], COPY, scale=a_col[:, b : b + 1])
             rest[b] = bank(home[b], [P, PACK, CH], f"rest{b}")
             for t in range(PACK):
                 turn(rest[b][:, t, :], ay[b][:, t, :], t == 0, False)
@@ -218,20 +223,24 @@ def tile_picked_waveeq_none_p_kernel(tc, x_words, x_scales, w1, prev, c2, w2, of
             nc.vector.tensor_tensor(sw[t][:], y[t][:].indirect(west_t[:, 0:16]), ke[t][:, halves[0]], ADD)
             for b in range(2):
                 turn(turned[b][:, t, :], sw[t][:, b * CH : (b + 1) * CH])
+        ay_2 = keep.tile([P, PACK, P], F32, name="ay_2", tag=f"sw{PACK - 2}")
+        late = keep.tile([P, 3, PACK, P], F32, name="late", tag=f"sw{PACK - 1}")
+        ay += [ay_2[:], late[:, 0]]
+        part += [late[:, 1], late[:, 2]]
         open_rest(2)
+        make_rest(0)
+        make_rest(1)
         open_rest(3)
-        part_right = keep.tile([P, 2, PACK, P], F32, name="part_right", tag=f"sw{PACK - 1}")
-        part += [part_right[:, 0], part_right[:, 1]]
-        for b in range(NCH):
-            make_rest(b)
+        make_rest(2)
+        make_rest(3)
         for t in range(PACK - 1):
             nc.vector.tensor_tensor(cw[:, t, :], y[t][:].indirect(west_t[:, 16:32]), c_row[:], MULT)
         nc.vector.quantize_mx(out=w2_codes[:].bitcast(FP8X4), scales=w2_plane[:], in_=w2_grp[:].rearrange("p c t -> p (c t)"))
         make_z(0)
         make_z(1)
         nc.vector.tensor_tensor(cw[:, PACK - 1, :], y[PACK - 1][:].indirect(west_t[:, 16:32]), c_row[:], MULT)
-        store(finish(0, HALF, z_left, [(0, 1, nc.scalar.copy, nc.sync), (2, 2, nc.scalar.copy, nc.sync)]))
+        store(finish(0, HALF, z_left, [(1, nc.scalar.copy, nc.sync), (2, nc.scalar.copy, nc.sync)]))
         make_z(2)
-        ways = finish(2 * CH, 3 * CH, z_grp[2], [(0, 3, nc.scalar.copy, nc.sync), (2, 4, nc.vector.tensor_copy, nc.sync)])
+        ways = finish(2 * CH, 3 * CH, z_grp[2], [(3, nc.scalar.copy, nc.sync), (4, nc.vector.tensor_copy, nc.sync)])
         make_z(3)
-        store(ways + finish(3 * CH, S, z_grp[3], [(0, 5, nc.scalar.copy, nc.scalar), (2, 6, nc.vector.tensor_copy, nc.sync)]))
+        store(ways + finish(3 * CH, S, z_grp[3], [(5, nc.scalar.copy, nc.scalar), (6, nc.vector.tensor_copy, nc.sync), (7, nc.scalar.copy, nc.scalar), (0, nc.vector.tensor_copy, nc.sync)]))

@@ -176,7 +176,7 @@ def tile_picked_waveeq_none_p_kernel(tc, x_words, x_scales, w1, prev, c2, w2, of
         z_left = z_tile[:]
         z_grp = [z_left[:, b * CH : (b + 1) * CH] for b in range(2)]
         z_grp += [keep.tile([P, CH, PACK], BF16, name=f"z_grp{b}", align_bytes=64)[:] for b in range(2, NCH)]
-        ay = [keep.tile([P, PACK, P], F32, name=f"ay{b}")[:] for b in range(2)]
+        ay = [keep.tile([P, PACK, P], F32, name=f"ay{b}")[:] for b in range(NCH)]
         y_turned = []
         part = [keep.tile([P, PACK, P], F32, name=f"part{b}")[:] for b in range(2)]
         home = (5, 6, 7, 0)
@@ -190,11 +190,11 @@ def tile_picked_waveeq_none_p_kernel(tc, x_words, x_scales, w1, prev, c2, w2, of
             else:
                 for t in range(PACK):
                     turn(y_turned[b][:, t, :], y[t][:, cols])
+            nc.scalar.activation(ay[b], y_turned[b][:], COPY, scale=a_col[:, b : b + 1])
         turned = [bank(1 + b, [P, PACK, P], f"turned{b}") for b in range(NCH)]
 
         def open_rest(b):
-            nc.scalar.activation(ay[b], y_turned[b][:], COPY, scale=a_col[:, b : b + 1])
-            rest[b] = bank(home[b], [P, PACK, CH], f"rest{b}")
+            rest[b] = bank((5, 6, 7, 2)[b], [P, PACK, CH], f"rest{b}")
             for t in range(PACK):
                 turn(rest[b][:, t, :], ay[b][:, t, :], t == 0, False)
 
@@ -223,10 +223,8 @@ def tile_picked_waveeq_none_p_kernel(tc, x_words, x_scales, w1, prev, c2, w2, of
             nc.vector.tensor_tensor(sw[t][:], y[t][:].indirect(west_t[:, 0:16]), ke[t][:, halves[0]], ADD)
             for b in range(2):
                 turn(turned[b][:, t, :], sw[t][:, b * CH : (b + 1) * CH])
-        ay_2 = keep.tile([P, PACK, P], F32, name="ay_2", tag=f"sw{PACK - 2}")
-        late = keep.tile([P, 3, PACK, P], F32, name="late", tag=f"sw{PACK - 1}")
-        ay += [ay_2[:], late[:, 0]]
-        part += [late[:, 1], late[:, 2]]
+        late = keep.tile([P, 2, PACK, P], F32, name="late", tag=f"sw{PACK - 1}")
+        part += [late[:, 0], late[:, 1]]
         open_rest(2)
         make_rest(0)
         make_rest(1)
@@ -239,8 +237,8 @@ def tile_picked_waveeq_none_p_kernel(tc, x_words, x_scales, w1, prev, c2, w2, of
         make_z(0)
         make_z(1)
         nc.vector.tensor_tensor(cw[:, PACK - 1, :], y[PACK - 1][:].indirect(west_t[:, 16:32]), c_row[:], MULT)
-        store(finish(0, HALF, z_left, [(1, nc.scalar.copy, nc.sync), (2, nc.scalar.copy, nc.sync)]))
+        store(finish(0, HALF, z_left, [(i, nc.scalar.copy, nc.sync) for i in (1, 0, 3, 4)]))
         make_z(2)
-        ways = finish(2 * CH, 3 * CH, z_grp[2], [(3, nc.scalar.copy, nc.sync), (4, nc.vector.tensor_copy, nc.sync)])
+        ways = finish(2 * CH, 3 * CH, z_grp[2], [(5, nc.scalar.copy, nc.sync), (6, nc.vector.tensor_copy, nc.sync)])
         make_z(3)
-        store(ways + finish(3 * CH, S, z_grp[3], [(5, nc.scalar.copy, nc.scalar), (6, nc.vector.tensor_copy, nc.sync), (7, nc.scalar.copy, nc.scalar), (0, nc.vector.tensor_copy, nc.sync)]))
+        store(ways + finish(3 * CH, S, z_grp[3], [(7, nc.scalar.copy, nc.scalar), (2, nc.vector.tensor_copy, nc.sync)]))

@@ -38,7 +38,7 @@ def tile_picked_waveeq_none_p_kernel(tc, x_words, x_scales, w1, prev, c2, w2, of
 
         scale_win = keep.tile([P, T], U8, name="scale_win")
         nc.vector.memset(scale_win[:].bitcast(I32), 0)
-        word_win = keep.tile([P, T], U32, name="word_win", tag="words")
+        word_win = keep.tile([P, T], U32, name="word_win", tag="words", align_bytes=64)
         word_rows = x_words[0].rearrange("p c r -> p (c r)").bitcast(I32)
         nc.sync.dma_start(word_win[:, 0 : XA // 2].bitcast(I32), word_rows[:, 0 : XA // 2])
         nc.sync.dma_start(offs_t[:], offs)
@@ -116,9 +116,8 @@ def tile_picked_waveeq_none_p_kernel(tc, x_words, x_scales, w1, prev, c2, w2, of
         nc.sync.dma_start(prev_t[:], prev_rows[:, :, CH:])
         w2_raw = keep.tile([P, PACK, N], F32, name="w2_raw", tag="w1_grp1", align_bytes=64)
         nc.sync.dma_start(w2_raw[:], w2.rearrange("(p j) c -> p j c", j=PACK))
-        cw = keep.tile([P, PACK + 1, S // 2], F32, name="cw", tag="words")
-        prev_0 = cw[:, PACK - 1 :, :].rearrange("p a (b j) -> p (a b) j", j=CH)
-        nc.sync.dma_start(prev_0, prev_rows[:, :, 0:CH])
+        prev_0 = keep.tile([P, PACK, CH], F32, name="prev_0", tag="words", align_bytes=64)
+        nc.sync.dma_start(prev_0[:], prev_rows[:, :, 0:CH])
 
 
         def first_product(acc, t, cols):
@@ -136,13 +135,18 @@ def tile_picked_waveeq_none_p_kernel(tc, x_words, x_scales, w1, prev, c2, w2, of
                 first_product(y_ps[:, cols], t, cols)
             nc.scalar.copy(y[t][:, 0:S], y_ps[:])
 
-        w2_codes = keep.tile([P, N], U32, name="w2_codes", align_bytes=64)
-        w2_plane = keep.tile([P, N], U8, name="w2_plane", align_bytes=64)
+        w2_codes, w2_plane = [], []
         w2_grp = keep.tile([P, N, PACK], BF16, name="w2_grp", align_bytes=64)
 
         def weave_w2(q):
             cols = slice(q * P, (q + 1) * P)
             nc.scalar.copy(w2_grp[:, cols].rearrange("p (c i) t -> p c t i", i=4), w2_raw[:, :, cols].rearrange("p t (c i) -> p c t i", i=4))
+
+        def quantise_w2(h, tag):
+            w2_codes.append(keep.tile([P, N // 2], U32, name=f"w2_codes{h}", tag=tag, align_bytes=64))
+            w2_plane.append(keep.tile([P, N // 2], U8, name=f"w2_plane{h}", align_bytes=64))
+            nc.vector.quantize_mx(out=w2_codes[h][:].bitcast(FP8X4), scales=w2_plane[h][:],
+                                  in_=w2_grp[:, h * (N // 2) : (h + 1) * (N // 2)].rearrange("p c t -> p (c t)"))
 
         out_rows = out.rearrange("(g p) j -> p g j", p=P)
 
@@ -156,8 +160,8 @@ def tile_picked_waveeq_none_p_kernel(tc, x_words, x_scales, w1, prev, c2, w2, of
                 g0 = n * width
                 o_ps = bank(i, [P, width, j1 - j0], f"o_ps{j0}_{g0}")
                 for g in range(g0, g0 + width):
-                    cols = slice(g * P, (g + 1) * P)
-                    nc.tensor.matmul_mx(out=o_ps[:, g - g0, :], lhsT=w2_codes[:, cols].bitcast(FP8X4), lhsT_scale=w2_plane[:, cols],
+                    cols = slice(g % 2 * P, (g % 2 + 1) * P)
+                    nc.tensor.matmul_mx(out=o_ps[:, g - g0, :], lhsT=w2_codes[g // 2][:, cols].bitcast(FP8X4), lhsT_scale=w2_plane[g // 2][:, cols],
                                         rhs=z_codes[:].bitcast(FP8X4), rhs_scale=z_plane[:], start=True, stop=True)
                 ways.append((j0, j1, g0, width, o_ps, copy, queue))
             return ways
@@ -169,6 +173,7 @@ def tile_picked_waveeq_none_p_kernel(tc, x_words, x_scales, w1, prev, c2, w2, of
                 queue.dma_start(out_rows[:, g0 : g0 + width, j0:j1], o_sb[:])
 
         HALF = S // 2
+        cw = keep.tile([P, PACK, HALF], F32, name="cw")
         ke = [keep.tile([P, S], F32, name=f"ke{t}")[:] for t in range(PACK - 1)]
         ke.append(cw[:].rearrange("p a w -> p (a w)")[:, CH : CH + S])
         sw = [keep.tile([P, HALF], F32, name=f"sw{t}", tag=f"sw{t}") for t in range(PACK)]
@@ -194,7 +199,7 @@ def tile_picked_waveeq_none_p_kernel(tc, x_words, x_scales, w1, prev, c2, w2, of
         turned = [bank(1 + b, [P, PACK, P], f"turned{b}") for b in range(NCH)]
 
         def open_rest(b):
-            rest[b] = bank((5, 6, 7, 2)[b], [P, PACK, CH], f"rest{b}")
+            rest[b] = bank(home[b], [P, PACK, CH], f"rest{b}")
             for t in range(PACK):
                 turn(rest[b][:, t, :], ay[b][:, t, :], t == 0, False)
 
@@ -204,7 +209,7 @@ def tile_picked_waveeq_none_p_kernel(tc, x_words, x_scales, w1, prev, c2, w2, of
                 turn(rest[b][:, t, :], part[b][:, t, :], False, t == PACK - 1)
 
         def make_z(b):
-            other = (prev_0, prev_t[:, :, 0:CH], cw[:, 0:PACK, 0:CH], cw[:, 0:PACK, CH:])[b]
+            other = (prev_0[:], prev_t[:, :, 0:CH], cw[:, 0:PACK, 0:CH], cw[:, 0:PACK, CH:])[b]
             nc.vector.tensor_tensor(z_grp[b].rearrange("p (c i) t -> p c t i", i=4), rest[b][:].rearrange("p t (c i) -> p c t i", i=4),
                                     other.rearrange("p t (c i) -> p c t i", i=4), SUB if b < 2 else ADD)
 
@@ -217,6 +222,7 @@ def tile_picked_waveeq_none_p_kernel(tc, x_words, x_scales, w1, prev, c2, w2, of
             nc.vector.tensor_tensor(ke[t], y[t][:].indirect(east_t[:]), k_row[:], MULT)
             for b in range(2, NCH):
                 turn(turned[b][:, t, :], ke[t][:, b * CH : (b + 1) * CH], False, t == PACK - 1)
+        open_rest(3)
         for q in range(PACK):
             weave_w2(q)
         for t in range(PACK):
@@ -228,17 +234,16 @@ def tile_picked_waveeq_none_p_kernel(tc, x_words, x_scales, w1, prev, c2, w2, of
         open_rest(2)
         make_rest(0)
         make_rest(1)
-        open_rest(3)
         make_rest(2)
         make_rest(3)
-        for t in range(PACK - 1):
+        for t in range(PACK):
             nc.vector.tensor_tensor(cw[:, t, :], y[t][:].indirect(west_t[:, 16:32]), c_row[:], MULT)
-        nc.vector.quantize_mx(out=w2_codes[:].bitcast(FP8X4), scales=w2_plane[:], in_=w2_grp[:].rearrange("p c t -> p (c t)"))
+        quantise_w2(0, "w2_codes0")
         make_z(0)
         make_z(1)
-        nc.vector.tensor_tensor(cw[:, PACK - 1, :], y[PACK - 1][:].indirect(west_t[:, 16:32]), c_row[:], MULT)
-        store(finish(0, HALF, z_left, [(i, nc.scalar.copy, nc.sync) for i in (1, 0, 3, 4)]))
+        quantise_w2(1, "words")
+        store(finish(0, HALF, z_left, [(i, nc.scalar.copy, nc.sync) for i in (1, 2, 3, 4)]))
         make_z(2)
         ways = finish(2 * CH, 3 * CH, z_grp[2], [(5, nc.scalar.copy, nc.sync), (6, nc.vector.tensor_copy, nc.sync)])
         make_z(3)
-        store(ways + finish(3 * CH, S, z_grp[3], [(7, nc.scalar.copy, nc.scalar), (2, nc.vector.tensor_copy, nc.sync)]))
+        store(ways + finish(3 * CH, S, z_grp[3], [(7, nc.scalar.copy, nc.scalar), (0, nc.vector.tensor_copy, nc.sync)]))

@@ -150,37 +150,35 @@ def tile_picked_waveeq_none_p_kernel(tc, x_words, x_scales, w1, prev, c2, w2, of
 
         out_rows = out.rearrange("(g p) j -> p g j", p=P)
 
-        def finish(j0, j1, z, parts):
-            z_codes = keep.tile([P, j1 - j0], U32, name=f"z_codes{j0}", align_bytes=64)
-            z_plane = keep.tile([P, j1 - j0], U8, name=f"z_plane{j0}", align_bytes=64)
-            nc.vector.quantize_mx(out=z_codes[:].bitcast(FP8X4), scales=z_plane[:], in_=z.rearrange("p j t -> p (j t)"))
+        def quantise_z(b):
+            z_codes = keep.tile([P, CH], U32, name=f"z_codes{b}", align_bytes=64)
+            z_plane = keep.tile([P, CH], U8, name=f"z_plane{b}", align_bytes=64)
+            nc.vector.quantize_mx(out=z_codes[:].bitcast(FP8X4), scales=z_plane[:], in_=z_grp[b].rearrange("p j t -> p (j t)"))
+            return z_codes, z_plane
+
+        def multiply(b, z_mx, parts):
             ways = []
-            width = PACK // len(parts)
-            for n, (i, copy, queue) in enumerate(parts):
-                g0 = n * width
-                o_ps = bank(i, [P, width, j1 - j0], f"o_ps{j0}_{g0}")
-                for g in range(g0, g0 + width):
-                    cols = slice(g % 2 * P, (g % 2 + 1) * P)
-                    nc.tensor.matmul_mx(out=o_ps[:, g - g0, :], lhsT=w2_codes[g // 2][:, cols].bitcast(FP8X4), lhsT_scale=w2_plane[g // 2][:, cols],
-                                        rhs=z_codes[:].bitcast(FP8X4), rhs_scale=z_plane[:], start=True, stop=True)
-                ways.append((j0, j1, g0, width, o_ps, copy, queue))
+            for h, (i, copy, queue) in enumerate(parts):
+                o_ps = bank(i, [P, 2, CH], f"o_ps{b}_{h}")
+                for e in range(2):
+                    cols = slice(e * P, (e + 1) * P)
+                    nc.tensor.matmul_mx(out=o_ps[:, e, :], lhsT=w2_codes[h][:, cols].bitcast(FP8X4), lhsT_scale=w2_plane[h][:, cols],
+                                        rhs=z_mx[0][:].bitcast(FP8X4), rhs_scale=z_mx[1][:], start=True, stop=True)
+                ways.append((b, h, o_ps, copy, queue))
             return ways
 
         def store(ways):
-            for j0, j1, g0, width, o_ps, copy, queue in ways:
-                o_sb = keep.tile([P, width, j1 - j0], F32, name=f"o_sb{j0}_{g0}")
+            for b, h, o_ps, copy, queue in ways:
+                o_sb = keep.tile([P, 2, CH], F32, name=f"o_sb{b}_{h}")
                 copy(o_sb[:], o_ps[:])
-                queue.dma_start(out_rows[:, g0 : g0 + width, j0:j1], o_sb[:])
+                queue.dma_start(out_rows[:, 2 * h : 2 * h + 2, b * CH : (b + 1) * CH], o_sb[:])
 
         HALF = S // 2
         cw = keep.tile([P, PACK, HALF], F32, name="cw")
         ke = [keep.tile([P, S], F32, name=f"ke{t}")[:] for t in range(PACK - 1)]
         ke.append(cw[:].rearrange("p a w -> p (a w)")[:, CH : CH + S])
         sw = [keep.tile([P, HALF], F32, name=f"sw{t}", tag=f"sw{t}") for t in range(PACK)]
-        z_tile = keep.tile([P, HALF, PACK], BF16, name="z_tile", align_bytes=64)
-        z_left = z_tile[:]
-        z_grp = [z_left[:, b * CH : (b + 1) * CH] for b in range(2)]
-        z_grp += [keep.tile([P, CH, PACK], BF16, name=f"z_grp{b}", align_bytes=64)[:] for b in range(2, NCH)]
+        z_grp = [keep.tile([P, CH, PACK], BF16, name=f"z_grp{b}", align_bytes=64)[:] for b in range(NCH)]
         ay = [keep.tile([P, PACK, P], F32, name=f"ay{b}")[:] for b in range(NCH)]
         y_turned = []
         part = [keep.tile([P, PACK, P], F32, name=f"part{b}")[:] for b in range(2)]
@@ -241,9 +239,11 @@ def tile_picked_waveeq_none_p_kernel(tc, x_words, x_scales, w1, prev, c2, w2, of
         quantise_w2(0, "w2_codes0")
         make_z(0)
         make_z(1)
+        z_mx = [quantise_z(0)]
         quantise_w2(1, "words")
-        store(finish(0, HALF, z_left, [(i, nc.scalar.copy, nc.sync) for i in (1, 2, 3, 4)]))
+        store(multiply(0, z_mx[0], [(1, nc.scalar.copy, nc.sync), (2, nc.scalar.copy, nc.sync)]))
         make_z(2)
-        ways = finish(2 * CH, 3 * CH, z_grp[2], [(5, nc.scalar.copy, nc.sync), (6, nc.vector.tensor_copy, nc.sync)])
+        store(multiply(1, quantise_z(1), [(3, nc.scalar.copy, nc.sync), (4, nc.scalar.copy, nc.sync)]))
+        ways = multiply(2, quantise_z(2), [(5, nc.scalar.copy, nc.sync), (6, nc.vector.tensor_copy, nc.sync)])
         make_z(3)
-        store(ways + finish(3 * CH, S, z_grp[3], [(7, nc.scalar.copy, nc.scalar), (0, nc.vector.tensor_copy, nc.sync)]))
+        store(ways + multiply(3, quantise_z(3), [(1, nc.scalar.copy, nc.scalar), (2, nc.vector.tensor_copy, nc.sync)]))

@@ -90,17 +90,22 @@ def tile_picked_waveeq_none_p_kernel(tc, x_words, x_scales, w1, prev, c2, w2, of
         nc.scalar.copy(c_col[:], c_turned[:, 0:NCH])
         nc.scalar.activation(a_col[:], c_turned[:, 0:NCH], COPY, scale=-2.0, bias=2.0)
 
-        w1_codes = keep.tile([P, H], U32, name="w1_codes", align_bytes=64)
-        w1_plane = keep.tile([P, H], U8, name="w1_plane", align_bytes=64)
+        w1_grp = [keep.tile([P, 2, P, PACK], BF16, name=f"w1_grp{u}", tag=f"w1_grp{u}", align_bytes=64) for u in range(2)]
         for u, copy in enumerate((nc.vector.tensor_copy, nc.scalar.copy)):
-            grp = keep.tile([P, 2, P, PACK], BF16, name=f"w1_grp{u}", tag=f"w1_grp{u}", align_bytes=64)
-            copy(grp[:].rearrange("p t m j -> p m t j"), w1_raw[:].rearrange("p j (m t) -> p m t j", t=PACK)[:, :, 2 * u : 2 * u + 2])
-            nc.vector.quantize_mx(out=w1_codes[:, 2 * u * P : 2 * (u + 1) * P].bitcast(FP8X4), scales=w1_plane[:, 2 * u * P : 2 * (u + 1) * P], in_=grp[:].rearrange("p t m j -> p (t m j)"))
+            copy(w1_grp[u][:].rearrange("p t m j -> p m t j"), w1_raw[:].rearrange("p j (m t) -> p m t j", t=PACK)[:, :, 2 * u : 2 * u + 2])
+        w1_codes, w1_plane = [], []
 
+        def quantise_w1(u, tag):
+            w1_codes.append(keep.tile([P, 2 * P], U32, name=f"w1_codes{u}", tag=tag, align_bytes=64))
+            w1_plane.append(keep.tile([P, 2 * P], U8, name=f"w1_plane{u}", align_bytes=64))
+            nc.vector.quantize_mx(out=w1_codes[u][:].bitcast(FP8X4), scales=w1_plane[u][:], in_=w1_grp[u][:].rearrange("p t m j -> p (t m j)"))
+
+        quantise_w1(0, "w1_codes0")
         halves = [slice(0, S // 2), slice(S // 2, S)]
         x_codes = keep.tile([P, S], U32, name="x_codes", align_bytes=64)
         for h, half in enumerate(halves):
             nc.vector.tensor_copy(x_codes[:, half], word_win[:].indirect(offs_t[:, 16 * h : 16 * h + 16]))
+        quantise_w1(1, "words")
 
         c_ps = bank(7, [P, 2, CH], "c_ps")
         for b in range(2):
@@ -111,17 +116,15 @@ def tile_picked_waveeq_none_p_kernel(tc, x_words, x_scales, w1, prev, c2, w2, of
         nc.scalar.activation(k_row[:, S // 2 :], c_ps[:].rearrange("p b j -> p (b j)"), COPY, scale=-1.0)
         nc.scalar.copy(c_row[:], c_ps[:].rearrange("p b j -> p (b j)"))
 
-        prev_rows = prev.rearrange("(p t) j -> p t j", t=PACK)
-        prev_t = keep.tile([P, PACK, S - CH], F32, name="prev_t", tag="raw")
-        nc.sync.dma_start(prev_t[:], prev_rows[:, :, CH:])
+        prev_t = keep.tile([P, PACK, S], F32, name="prev_t", tag="raw")
+        nc.sync.dma_start(prev_t[:], prev.rearrange("(p t) j -> p t j", t=PACK))
         w2_raw = keep.tile([P, PACK, N], F32, name="w2_raw", tag="w1_grp1", align_bytes=64)
         nc.sync.dma_start(w2_raw[:], w2.rearrange("(p j) c -> p j c", j=PACK))
-        prev_0 = keep.tile([P, PACK, CH], F32, name="prev_0", tag="words", align_bytes=64)
-        nc.sync.dma_start(prev_0[:], prev_rows[:, :, 0:CH])
 
 
         def first_product(acc, t, cols):
-            nc.tensor.matmul_mx(out=acc, lhsT=w1_codes[:, t * P : (t + 1) * P].bitcast(FP8X4), lhsT_scale=w1_plane[:, t * P : (t + 1) * P],
+            u, e = divmod(t, 2)
+            nc.tensor.matmul_mx(out=acc, lhsT=w1_codes[u][:, e * P : (e + 1) * P].bitcast(FP8X4), lhsT_scale=w1_plane[u][:, e * P : (e + 1) * P],
                                 rhs=x_codes[:, cols].bitcast(FP8X4), rhs_scale=x_plane[:, cols], start=True, stop=True)
 
         pieces = [(0, slice(0, S // 2), nc.scalar.copy), (1, slice(S // 2, S - CH), nc.vector.tensor_copy), (7, slice(S - CH, S), nc.scalar.copy)]
@@ -135,18 +138,13 @@ def tile_picked_waveeq_none_p_kernel(tc, x_words, x_scales, w1, prev, c2, w2, of
                 first_product(y_ps[:, cols], t, cols)
             nc.scalar.copy(y[t][:, 0:S], y_ps[:])
 
-        w2_codes, w2_plane = [], []
+        w2_codes = keep.tile([P, N], U32, name="w2_codes", align_bytes=64)
+        w2_plane = keep.tile([P, N], U8, name="w2_plane", align_bytes=64)
         w2_grp = keep.tile([P, N, PACK], BF16, name="w2_grp", align_bytes=64)
 
         def weave_w2(q):
             cols = slice(q * P, (q + 1) * P)
             nc.scalar.copy(w2_grp[:, cols].rearrange("p (c i) t -> p c t i", i=4), w2_raw[:, :, cols].rearrange("p t (c i) -> p c t i", i=4))
-
-        def quantise_w2(h, tag):
-            w2_codes.append(keep.tile([P, N // 2], U32, name=f"w2_codes{h}", tag=tag, align_bytes=64))
-            w2_plane.append(keep.tile([P, N // 2], U8, name=f"w2_plane{h}", align_bytes=64))
-            nc.vector.quantize_mx(out=w2_codes[h][:].bitcast(FP8X4), scales=w2_plane[h][:],
-                                  in_=w2_grp[:, h * (N // 2) : (h + 1) * (N // 2)].rearrange("p c t -> p (c t)"))
 
         out_rows = out.rearrange("(g p) j -> p g j", p=P)
 
@@ -161,8 +159,8 @@ def tile_picked_waveeq_none_p_kernel(tc, x_words, x_scales, w1, prev, c2, w2, of
             for h, (i, copy, queue) in enumerate(parts):
                 o_ps = bank(i, [P, 2, CH], f"o_ps{b}_{h}")
                 for e in range(2):
-                    cols = slice(e * P, (e + 1) * P)
-                    nc.tensor.matmul_mx(out=o_ps[:, e, :], lhsT=w2_codes[h][:, cols].bitcast(FP8X4), lhsT_scale=w2_plane[h][:, cols],
+                    cols = slice((2 * h + e) * P, (2 * h + e + 1) * P)
+                    nc.tensor.matmul_mx(out=o_ps[:, e, :], lhsT=w2_codes[:, cols].bitcast(FP8X4), lhsT_scale=w2_plane[:, cols],
                                         rhs=z_mx[0][:].bitcast(FP8X4), rhs_scale=z_mx[1][:], start=True, stop=True)
                 ways.append((b, h, o_ps, copy, queue))
             return ways
@@ -188,8 +186,9 @@ def tile_picked_waveeq_none_p_kernel(tc, x_words, x_scales, w1, prev, c2, w2, of
             cols = slice(b * CH, (b + 1) * CH)
             y_turned.append(bank(home[b], [P, PACK, P], f"y_turned{b}"))
             if b < 2:
-                nc.tensor.matmul_mx(out=y_turned[b][:].rearrange("j t p -> j (t p)"), lhsT=x_codes[:, cols].bitcast(FP8X4), lhsT_scale=x_plane[:, cols],
-                                    rhs=w1_codes[:].bitcast(FP8X4), rhs_scale=w1_plane[:], start=True, stop=True)
+                for u in range(2):
+                    nc.tensor.matmul_mx(out=y_turned[b][:, 2 * u : 2 * u + 2].rearrange("j t p -> j (t p)"), lhsT=x_codes[:, cols].bitcast(FP8X4),
+                                        lhsT_scale=x_plane[:, cols], rhs=w1_codes[u][:].bitcast(FP8X4), rhs_scale=w1_plane[u][:], start=True, stop=True)
             else:
                 for t in range(PACK):
                     turn(y_turned[b][:, t, :], y[t][:, cols])
@@ -207,7 +206,7 @@ def tile_picked_waveeq_none_p_kernel(tc, x_words, x_scales, w1, prev, c2, w2, of
                 turn(rest[b][:, t, :], part[b][:, t, :], False, t == PACK - 1)
 
         def make_z(b):
-            other = (prev_0[:], prev_t[:, :, 0:CH], cw[:, 0:PACK, 0:CH], cw[:, 0:PACK, CH:])[b]
+            other = prev_t[:, :, b * CH : (b + 1) * CH] if b < 2 else cw[:, :, (b - 2) * CH : (b - 1) * CH]
             nc.vector.tensor_tensor(z_grp[b].rearrange("p (c i) t -> p c t i", i=4), rest[b][:].rearrange("p t (c i) -> p c t i", i=4),
                                     other.rearrange("p t (c i) -> p c t i", i=4), SUB if b < 2 else ADD)
 
@@ -215,7 +214,7 @@ def tile_picked_waveeq_none_p_kernel(tc, x_words, x_scales, w1, prev, c2, w2, of
         open_rest(1)
         for b in range(2, NCH):
             for t in range(PACK):
-                turn(turned[b][:, t, :], prev_t[:, t, (b - 1) * CH : b * CH], t == 0, False)
+                turn(turned[b][:, t, :], prev_t[:, t, b * CH : (b + 1) * CH], t == 0, False)
         for t in range(PACK):
             nc.vector.tensor_tensor(ke[t], y[t][:].indirect(east_t[:]), k_row[:], MULT)
             for b in range(2, NCH):
@@ -236,12 +235,10 @@ def tile_picked_waveeq_none_p_kernel(tc, x_words, x_scales, w1, prev, c2, w2, of
         make_rest(3)
         for t in range(PACK):
             nc.vector.tensor_tensor(cw[:, t, :], y[t][:].indirect(west_t[:, 16:32]), c_row[:], MULT)
-        quantise_w2(0, "w2_codes0")
+        nc.vector.quantize_mx(out=w2_codes[:].bitcast(FP8X4), scales=w2_plane[:], in_=w2_grp[:].rearrange("p c t -> p (c t)"))
         make_z(0)
         make_z(1)
-        z_mx = [quantise_z(0)]
-        quantise_w2(1, "words")
-        store(multiply(0, z_mx[0], [(1, nc.scalar.copy, nc.sync), (2, nc.scalar.copy, nc.sync)]))
+        store(multiply(0, quantise_z(0), [(1, nc.scalar.copy, nc.sync), (2, nc.scalar.copy, nc.sync)]))
         make_z(2)
         store(multiply(1, quantise_z(1), [(3, nc.scalar.copy, nc.sync), (4, nc.scalar.copy, nc.sync)]))
         ways = multiply(2, quantise_z(2), [(5, nc.scalar.copy, nc.sync), (6, nc.vector.tensor_copy, nc.sync)])

@@ -48,9 +48,11 @@ def tile_picked_waveeq_none_p_kernel(tc, x_words, x_scales, w1, prev, c2, w2, of
         c_sq = keep.tile([P, P], F32, name="c_sq")
         nc.vector.memset(c_sq[:], 0.0)
         nc.sync.dma_start(c_sq[0:NCH, :], c2[0].rearrange("(b j) -> b j", j=CH))
-        w1_raw = keep.tile([P, PACK, H], F32, name="w1_raw", tag="raw")
-        nc.sync.dma_start(w1_raw[:], w1.rearrange("(p j) c -> p j c", j=PACK))
         nc.sync.dma_start(word_win[:, XA:].bitcast(I32), word_rows[:, XA:])
+        w1_rows = w1.rearrange("(p j) c -> p j c", j=PACK)
+        w1_raw = [keep.tile([P, PACK, H // 2], F32, name=f"w1_raw{h}", tag=f"raw{h}") for h in range(2)]
+        for h in range(2):
+            nc.sync.dma_start(w1_raw[h][:], w1_rows[:, :, h * H // 2 : (h + 1) * H // 2])
         nc.sync.dma_start(east_t[:], east)
         nc.sync.dma_start(west_t[:], west)
 
@@ -90,22 +92,25 @@ def tile_picked_waveeq_none_p_kernel(tc, x_words, x_scales, w1, prev, c2, w2, of
         nc.scalar.copy(c_col[:], c_turned[:, 0:NCH])
         nc.scalar.activation(a_col[:], c_turned[:, 0:NCH], COPY, scale=-2.0, bias=2.0)
 
-        w1_grp = [keep.tile([P, 2, P, PACK], BF16, name=f"w1_grp{u}", tag=f"w1_grp{u}", align_bytes=64) for u in range(2)]
-        for u, copy in enumerate((nc.vector.tensor_copy, nc.scalar.copy)):
-            copy(w1_grp[u][:].rearrange("p t m j -> p m t j"), w1_raw[:].rearrange("p j (m t) -> p m t j", t=PACK)[:, :, 2 * u : 2 * u + 2])
-        w1_codes, w1_plane = [], []
-
-        def quantise_w1(u, tag):
-            w1_codes.append(keep.tile([P, 2 * P], U32, name=f"w1_codes{u}", tag=tag, align_bytes=64))
-            w1_plane.append(keep.tile([P, 2 * P], U8, name=f"w1_plane{u}", align_bytes=64))
-            nc.vector.quantize_mx(out=w1_codes[u][:].bitcast(FP8X4), scales=w1_plane[u][:], in_=w1_grp[u][:].rearrange("p t m j -> p (t m j)"))
-
-        quantise_w1(0, "w1_codes0")
         halves = [slice(0, S // 2), slice(S // 2, S)]
         x_codes = keep.tile([P, S], U32, name="x_codes", align_bytes=64)
         for h, half in enumerate(halves):
             nc.vector.tensor_copy(x_codes[:, half], word_win[:].indirect(offs_t[:, 16 * h : 16 * h + 16]))
-        quantise_w1(1, "words")
+
+        w1_codes = [keep.tile([P, 2 * P], U32, name=f"w1_codes{u}", align_bytes=64) for u in range(2)]
+        w1_plane = [keep.tile([P, 2 * P], U8, name=f"w1_plane{u}", align_bytes=64) for u in range(2)]
+        for h in range(2):
+            dealt = w1_raw[h][:].rearrange("p j (m t) -> p m t j", t=PACK)
+            grp = [keep.tile([P, P // 2, PACK], BF16, name=f"w1_grp{h}_{t}", align_bytes=64)[:] for t in range(2)]
+            for t in range(2):
+                nc.vector.tensor_copy(grp[t], dealt[:, :, t])
+            pair = keep.tile([P, 2, P // 2, PACK], BF16, name=f"w1_pair{h}", align_bytes=64)
+            nc.scalar.copy(pair[:].rearrange("p t m j -> p m t j"), dealt[:, :, 2:4])
+            grp += [pair[:, 0], pair[:, 1]]
+            for t in range(PACK):
+                u, e = divmod(t, 2)
+                cols = slice(e * P + h * P // 2, e * P + (h + 1) * P // 2)
+                nc.vector.quantize_mx(out=w1_codes[u][:, cols].bitcast(FP8X4), scales=w1_plane[u][:, cols], in_=grp[t].rearrange("p m j -> p (m j)"))
 
         c_ps = bank(7, [P, 2, CH], "c_ps")
         for b in range(2):
@@ -116,9 +121,9 @@ def tile_picked_waveeq_none_p_kernel(tc, x_words, x_scales, w1, prev, c2, w2, of
         nc.scalar.activation(k_row[:, S // 2 :], c_ps[:].rearrange("p b j -> p (b j)"), COPY, scale=-1.0)
         nc.scalar.copy(c_row[:], c_ps[:].rearrange("p b j -> p (b j)"))
 
-        prev_t = keep.tile([P, PACK, S], F32, name="prev_t", tag="raw")
+        prev_t = keep.tile([P, PACK, S], F32, name="prev_t", tag="words", align_bytes=64)
         nc.sync.dma_start(prev_t[:], prev.rearrange("(p t) j -> p t j", t=PACK))
-        w2_raw = keep.tile([P, PACK, N], F32, name="w2_raw", tag="w1_grp1", align_bytes=64)
+        w2_raw = keep.tile([P, PACK, N], F32, name="w2_raw", tag="raw0")
         nc.sync.dma_start(w2_raw[:], w2.rearrange("(p j) c -> p j c", j=PACK))
 
 

@@ -22,7 +22,7 @@ P = 128
 PACK = 4
 CH = 128
 NCH = S // CH
-XA = 512
+XA = 1024
 
 
 def tile_picked_waveeq_none_p_kernel(tc, x_words, x_scales, w1, prev, c2, w2, offs, east, west, out):
@@ -99,18 +99,18 @@ def tile_picked_waveeq_none_p_kernel(tc, x_words, x_scales, w1, prev, c2, w2, of
 
         w1_codes = [keep.tile([P, 2 * P], U32, name=f"w1_codes{u}", align_bytes=64) for u in range(2)]
         w1_plane = [keep.tile([P, 2 * P], U8, name=f"w1_plane{u}", align_bytes=64) for u in range(2)]
+        groups = [(0, 1), (1, 2), (2, 4)]
+        w1_grp = [keep.tile([P, hi - lo, P, PACK], BF16, name=f"w1_grp{lo}", align_bytes=64) for lo, hi in groups]
         for h in range(2):
             dealt = w1_raw[h][:].rearrange("p j (m t) -> p m t j", t=PACK)
-            grp = [keep.tile([P, P // 2, PACK], BF16, name=f"w1_grp{h}_{t}", align_bytes=64)[:] for t in range(2)]
-            for t in range(2):
-                nc.vector.tensor_copy(grp[t], dealt[:, :, t])
-            pair = keep.tile([P, 2, P // 2, PACK], BF16, name=f"w1_pair{h}", align_bytes=64)
-            nc.scalar.copy(pair[:].rearrange("p t m j -> p m t j"), dealt[:, :, 2:4])
-            grp += [pair[:, 0], pair[:, 1]]
-            for t in range(PACK):
-                u, e = divmod(t, 2)
-                cols = slice(e * P + h * P // 2, e * P + (h + 1) * P // 2)
-                nc.vector.quantize_mx(out=w1_codes[u][:, cols].bitcast(FP8X4), scales=w1_plane[u][:, cols], in_=grp[t].rearrange("p m j -> p (m j)"))
+            for grp, (lo, hi) in zip(w1_grp, groups):
+                copy = nc.vector.tensor_copy if h == 1 and lo < 2 else nc.scalar.copy
+                copy(grp[:, :, h * P // 2 : (h + 1) * P // 2].rearrange("p t m j -> p m t j"), dealt[:, :, lo:hi])
+        runs = [(0, 0, P // 2), (0, P // 2, P), (1, 0, P), (2, 0, 2 * P)]
+        for g, lo, hi in runs:
+            u, cols = g // 2, slice(g % 2 * P + lo, g % 2 * P + hi)
+            nc.vector.quantize_mx(out=w1_codes[u][:, cols].bitcast(FP8X4), scales=w1_plane[u][:, cols],
+                                  in_=w1_grp[g][:].rearrange("p t m j -> p (t m j)")[:, PACK * lo : PACK * hi])
 
         c_ps = bank(7, [P, 2, CH], "c_ps")
         for b in range(2):
@@ -132,7 +132,7 @@ def tile_picked_waveeq_none_p_kernel(tc, x_words, x_scales, w1, prev, c2, w2, of
             nc.tensor.matmul_mx(out=acc, lhsT=w1_codes[u][:, e * P : (e + 1) * P].bitcast(FP8X4), lhsT_scale=w1_plane[u][:, e * P : (e + 1) * P],
                                 rhs=x_codes[:, cols].bitcast(FP8X4), rhs_scale=x_plane[:, cols], start=True, stop=True)
 
-        pieces = [(0, slice(0, S // 2), nc.scalar.copy), (1, slice(S // 2, S - CH), nc.vector.tensor_copy), (7, slice(S - CH, S), nc.scalar.copy)]
+        pieces = [(0, slice(0, S // 2), nc.scalar.copy), (1, slice(S // 2, S - CH), nc.vector.tensor_copy), (7, slice(S - CH, S), nc.vector.tensor_copy)]
         for i, cols, copy in pieces:
             y_ps = bank(i, [P, cols.stop - cols.start], f"y_ps0_{i}")
             first_product(y_ps[:], 0, cols)

@@ -99,18 +99,15 @@ def tile_picked_waveeq_none_p_kernel(tc, x_words, x_scales, w1, prev, c2, w2, of
 
         w1_codes = [keep.tile([P, 2 * P], U32, name=f"w1_codes{u}", align_bytes=64) for u in range(2)]
         w1_plane = [keep.tile([P, 2 * P], U8, name=f"w1_plane{u}", align_bytes=64) for u in range(2)]
-        groups = [(0, 1), (1, 2), (2, 4)]
-        w1_grp = [keep.tile([P, hi - lo, P, PACK], BF16, name=f"w1_grp{lo}", align_bytes=64) for lo, hi in groups]
+        w1_grp = [keep.tile([P, 2, P, PACK], BF16, name=f"w1_grp{u}", align_bytes=64) for u in range(2)]
         for h in range(2):
-            dealt = w1_raw[h][:].rearrange("p j (m t) -> p m t j", t=PACK)
-            for grp, (lo, hi) in zip(w1_grp, groups):
-                copy = nc.vector.tensor_copy if h == 1 and lo < 2 else nc.scalar.copy
-                copy(grp[:, :, h * P // 2 : (h + 1) * P // 2].rearrange("p t m j -> p m t j"), dealt[:, :, lo:hi])
-        runs = [(0, 0, P // 2), (0, P // 2, P), (1, 0, P), (2, 0, 2 * P)]
-        for g, lo, hi in runs:
-            u, cols = g // 2, slice(g % 2 * P + lo, g % 2 * P + hi)
-            nc.vector.quantize_mx(out=w1_codes[u][:, cols].bitcast(FP8X4), scales=w1_plane[u][:, cols],
-                                  in_=w1_grp[g][:].rearrange("p t m j -> p (t m j)")[:, PACK * lo : PACK * hi])
+            dealt = w1_raw[h][:].rearrange("p j (m t) -> p m j t", t=PACK)
+            for u in range(2):
+                copy = nc.vector.tensor_copy if (h, u) == (1, 0) else nc.scalar.copy
+                copy(w1_grp[u][:, :, h * P // 2 : (h + 1) * P // 2].rearrange("p t m j -> p m j t"), dealt[:, :, :, 2 * u : 2 * u + 2])
+        for u, lo, hi in [(0, 0, P // 2), (0, P // 2, P), (0, P, 2 * P), (1, 0, 2 * P)]:
+            nc.vector.quantize_mx(out=w1_codes[u][:, lo:hi].bitcast(FP8X4), scales=w1_plane[u][:, lo:hi],
+                                  in_=w1_grp[u][:].rearrange("p t m j -> p (t m j)")[:, PACK * lo : PACK * hi])
 
         c_ps = bank(7, [P, 2, CH], "c_ps")
         for b in range(2):

@@ -99,15 +99,14 @@ def tile_picked_waveeq_none_p_kernel(tc, x_words, x_scales, w1, prev, c2, w2, of
 
         w1_codes = [keep.tile([P, 2 * P], U32, name=f"w1_codes{u}", align_bytes=64) for u in range(2)]
         w1_plane = [keep.tile([P, 2 * P], U8, name=f"w1_plane{u}", align_bytes=64) for u in range(2)]
-        w1_grp = [keep.tile([P, 2, P, PACK], BF16, name=f"w1_grp{u}", align_bytes=64) for u in range(2)]
-        for h in range(2):
+        w1_grp = keep.tile([P, PACK, P, PACK], BF16, name="w1_grp", align_bytes=64)
+        for h, lo, hi, copy in [(0, 0, 4, nc.scalar.copy), (1, 0, 2, nc.vector.tensor_copy), (1, 2, 4, nc.vector.tensor_copy)]:
             dealt = w1_raw[h][:].rearrange("p j (m t) -> p m j t", t=PACK)
-            for u in range(2):
-                copy = nc.vector.tensor_copy if (h, u) == (1, 0) else nc.scalar.copy
-                copy(w1_grp[u][:, :, h * P // 2 : (h + 1) * P // 2].rearrange("p t m j -> p m j t"), dealt[:, :, :, 2 * u : 2 * u + 2])
-        for u, lo, hi in [(0, 0, P // 2), (0, P // 2, P), (0, P, 2 * P), (1, 0, 2 * P)]:
+            copy(w1_grp[:, lo:hi, h * P // 2 : (h + 1) * P // 2].rearrange("p t m j -> p m j t"), dealt[:, :, :, lo:hi])
+        w1_flat = w1_grp[:].rearrange("p t m j -> p (t m j)")
+        for u, lo, hi in [(0, 0, P), (0, P, 2 * P), (1, 0, 2 * P)]:
             nc.vector.quantize_mx(out=w1_codes[u][:, lo:hi].bitcast(FP8X4), scales=w1_plane[u][:, lo:hi],
-                                  in_=w1_grp[u][:].rearrange("p t m j -> p (t m j)")[:, PACK * lo : PACK * hi])
+                                  in_=w1_flat[:, PACK * (2 * P * u + lo) : PACK * (2 * P * u + hi)])
 
         c_ps = bank(7, [P, 2, CH], "c_ps")
         for b in range(2):

@@ -208,8 +208,8 @@ def tile_picked_waveeq_none_p_kernel(tc, x_words, x_scales, w1, prev, c2, w2, of
 
         def make_z(b):
             other = prev_t[:, :, b * CH : (b + 1) * CH] if b < 2 else cw[:, :, (b - 2) * CH : (b - 1) * CH]
-            nc.vector.tensor_tensor(z_grp[b].rearrange("p (c i) t -> p c t i", i=4), rest[b][:].rearrange("p t (c i) -> p c t i", i=4),
-                                    other.rearrange("p t (c i) -> p c t i", i=4), SUB if b < 2 else ADD)
+            nc.vector.tensor_tensor(z_grp[b].rearrange("p (c i) t -> p c t i", i=2), rest[b][:].rearrange("p t (c i) -> p c t i", i=2),
+                                    other.rearrange("p t (c i) -> p c t i", i=2), SUB if b < 2 else ADD)
 
         open_rest(0)
         open_rest(1)

@@ -99,14 +99,14 @@ def tile_picked_waveeq_none_p_kernel(tc, x_words, x_scales, w1, prev, c2, w2, of
 
         w1_codes = [keep.tile([P, 2 * P], U32, name=f"w1_codes{u}", align_bytes=64) for u in range(2)]
         w1_plane = [keep.tile([P, 2 * P], U8, name=f"w1_plane{u}", align_bytes=64) for u in range(2)]
-        w1_grp = keep.tile([P, PACK, P, PACK], BF16, name="w1_grp", align_bytes=64)
-        for h, lo, hi, copy in [(0, 0, 4, nc.scalar.copy), (1, 0, 2, nc.vector.tensor_copy), (1, 2, 4, nc.vector.tensor_copy)]:
+        w1_grp = [keep.tile([P, 2, P, PACK], BF16, name=f"w1_grp{u}", align_bytes=64) for u in range(2)]
+        for h, copy in enumerate((nc.scalar.copy, nc.vector.tensor_copy)):
             dealt = w1_raw[h][:].rearrange("p j (m t) -> p m j t", t=PACK)
-            copy(w1_grp[:, lo:hi, h * P // 2 : (h + 1) * P // 2].rearrange("p t m j -> p m j t"), dealt[:, :, :, lo:hi])
-        w1_flat = w1_grp[:].rearrange("p t m j -> p (t m j)")
+            for u in range(2):
+                copy(w1_grp[u][:, :, h * P // 2 : (h + 1) * P // 2].rearrange("p t m j -> p m j t"), dealt[:, :, :, 2 * u : 2 * u + 2])
         for u, lo, hi in [(0, 0, P), (0, P, 2 * P), (1, 0, 2 * P)]:
             nc.vector.quantize_mx(out=w1_codes[u][:, lo:hi].bitcast(FP8X4), scales=w1_plane[u][:, lo:hi],
-                                  in_=w1_flat[:, PACK * (2 * P * u + lo) : PACK * (2 * P * u + hi)])
+                                  in_=w1_grp[u][:].rearrange("p t m j -> p (t m j)")[:, PACK * lo : PACK * hi])
 
         c_ps = bank(7, [P, 2, CH], "c_ps")
         for b in range(2):
@@ -128,7 +128,7 @@ def tile_picked_waveeq_none_p_kernel(tc, x_words, x_scales, w1, prev, c2, w2, of
             nc.tensor.matmul_mx(out=acc, lhsT=w1_codes[u][:, e * P : (e + 1) * P].bitcast(FP8X4), lhsT_scale=w1_plane[u][:, e * P : (e + 1) * P],
                                 rhs=x_codes[:, cols].bitcast(FP8X4), rhs_scale=x_plane[:, cols], start=True, stop=True)
 
-        pieces = [(0, slice(0, S // 2), nc.scalar.copy), (1, slice(S // 2, S - CH), nc.vector.tensor_copy), (7, slice(S - CH, S), nc.vector.tensor_copy)]
+        pieces = [(0, slice(0, S // 2), nc.scalar.copy), (1, slice(S // 2, S - CH), nc.vector.tensor_copy), (7, slice(S - CH, S), nc.scalar.copy)]
         for i, cols, copy in pieces:
             y_ps = bank(i, [P, cols.stop - cols.start], f"y_ps0_{i}")
             first_product(y_ps[:], 0, cols)

@@ -128,6 +128,11 @@ def tile_picked_waveeq_none_p_kernel(tc, x_words, x_scales, w1, prev, c2, w2, of
             nc.tensor.matmul_mx(out=acc, lhsT=w1_codes[u][:, e * P : (e + 1) * P].bitcast(FP8X4), lhsT_scale=w1_plane[u][:, e * P : (e + 1) * P],
                                 rhs=x_codes[:, cols].bitcast(FP8X4), rhs_scale=x_plane[:, cols], start=True, stop=True)
 
+        HALF = S // 2
+        cw = keep.tile([P, PACK, HALF], F32, name="cw")
+        ke = [keep.tile([P, S], F32, name=f"ke{t}")[:] for t in range(PACK - 1)]
+        ke.append(cw[:].rearrange("p a w -> p (a w)")[:, CH : CH + S])
+
         pieces = [(0, slice(0, S // 2), nc.scalar.copy), (1, slice(S // 2, S - CH), nc.vector.tensor_copy), (7, slice(S - CH, S), nc.scalar.copy)]
         for i, cols, copy in pieces:
             y_ps = bank(i, [P, cols.stop - cols.start], f"y_ps0_{i}")
@@ -138,10 +143,12 @@ def tile_picked_waveeq_none_p_kernel(tc, x_words, x_scales, w1, prev, c2, w2, of
             for cols in halves if t == 1 else [slice(0, S)]:
                 first_product(y_ps[:, cols], t, cols)
             nc.scalar.copy(y[t][:, 0:S], y_ps[:])
+        for t in range(2, PACK):
+            nc.scalar.activation(ke[t][:, halves[0]], y[t][:].indirect(east_t[:, 0:16]), COPY)
 
         w2_codes = keep.tile([P, N], U32, name="w2_codes", align_bytes=64)
         w2_plane = keep.tile([P, N], U8, name="w2_plane", align_bytes=64)
-        w2_grp = keep.tile([P, N, PACK], BF16, name="w2_grp", align_bytes=64)
+        w2_grp = keep.tile([P, N, PACK], BF16, name="w2_grp", tag="z2", align_bytes=64)
 
         def weave_w2(q):
             cols = slice(q * P, (q + 1) * P)
@@ -172,12 +179,8 @@ def tile_picked_waveeq_none_p_kernel(tc, x_words, x_scales, w1, prev, c2, w2, of
                 copy(o_sb[:], o_ps[:])
                 queue.dma_start(out_rows[:, 2 * h : 2 * h + 2, b * CH : (b + 1) * CH], o_sb[:])
 
-        HALF = S // 2
-        cw = keep.tile([P, PACK, HALF], F32, name="cw")
-        ke = [keep.tile([P, S], F32, name=f"ke{t}")[:] for t in range(PACK - 1)]
-        ke.append(cw[:].rearrange("p a w -> p (a w)")[:, CH : CH + S])
         sw = [keep.tile([P, HALF], F32, name=f"sw{t}", tag=f"sw{t}") for t in range(PACK)]
-        z_grp = [keep.tile([P, CH, PACK], BF16, name=f"z_grp{b}", align_bytes=64)[:] for b in range(NCH)]
+        z_grp = {}
         ay = [keep.tile([P, PACK, P], F32, name=f"ay{b}")[:] for b in range(NCH)]
         y_turned = []
         part = [keep.tile([P, PACK, P], F32, name=f"part{b}")[:] for b in range(2)]
@@ -207,6 +210,7 @@ def tile_picked_waveeq_none_p_kernel(tc, x_words, x_scales, w1, prev, c2, w2, of
                 turn(rest[b][:, t, :], part[b][:, t, :], False, t == PACK - 1)
 
         def make_z(b):
+            z_grp[b] = keep.tile([P, CH, PACK], BF16, name=f"z_grp{b}", tag=f"z{b}", align_bytes=64)[:]
             other = prev_t[:, :, b * CH : (b + 1) * CH] if b < 2 else cw[:, :, (b - 2) * CH : (b - 1) * CH]
             nc.vector.tensor_tensor(z_grp[b].rearrange("p (c i) t -> p c t i", i=2), rest[b][:].rearrange("p t (c i) -> p c t i", i=2),
                                     other.rearrange("p t (c i) -> p c t i", i=2), SUB if b < 2 else ADD)
@@ -217,12 +221,15 @@ def tile_picked_waveeq_none_p_kernel(tc, x_words, x_scales, w1, prev, c2, w2, of
             for t in range(PACK):
                 turn(turned[b][:, t, :], prev_t[:, t, b * CH : (b + 1) * CH], t == 0, False)
         for t in range(PACK):
-            nc.vector.tensor_tensor(ke[t], y[t][:].indirect(east_t[:]), k_row[:], MULT)
+            if t < 2:
+                nc.vector.tensor_tensor(ke[t], y[t][:].indirect(east_t[:]), k_row[:], MULT)
+            else:
+                nc.vector.tensor_tensor(ke[t][:, halves[1]], y[t][:].indirect(east_t[:, 16:32]), k_row[:, halves[1]], MULT)
             for b in range(2, NCH):
                 turn(turned[b][:, t, :], ke[t][:, b * CH : (b + 1) * CH], False, t == PACK - 1)
         open_rest(3)
-        for q in range(PACK):
-            weave_w2(q)
+        weave_w2(0)
+        weave_w2(1)
         for t in range(PACK):
             nc.vector.tensor_tensor(sw[t][:], y[t][:].indirect(west_t[:, 0:16]), ke[t][:, halves[0]], ADD)
             for b in range(2):
@@ -234,11 +241,13 @@ def tile_picked_waveeq_none_p_kernel(tc, x_words, x_scales, w1, prev, c2, w2, of
         make_rest(1)
         make_rest(2)
         make_rest(3)
+        weave_w2(2)
+        weave_w2(3)
         for t in range(PACK):
             nc.vector.tensor_tensor(cw[:, t, :], y[t][:].indirect(west_t[:, 16:32]), c_row[:], MULT)
-        nc.vector.quantize_mx(out=w2_codes[:].bitcast(FP8X4), scales=w2_plane[:], in_=w2_grp[:].rearrange("p c t -> p (c t)"))
         make_z(0)
         make_z(1)
+        nc.vector.quantize_mx(out=w2_codes[:].bitcast(FP8X4), scales=w2_plane[:], in_=w2_grp[:].rearrange("p c t -> p (c t)"))
         store(multiply(0, quantise_z(0), [(1, nc.scalar.copy, nc.sync), (2, nc.scalar.copy, nc.sync)]))
         make_z(2)
         store(multiply(1, quantise_z(1), [(3, nc.scalar.copy, nc.sync), (4, nc.scalar.copy, nc.sync)]))

@@ -156,10 +156,14 @@ def tile_picked_waveeq_none_p_kernel(tc, x_words, x_scales, w1, prev, c2, w2, of
 
         out_rows = out.rearrange("(g p) j -> p g j", p=P)
 
+        def cuts(b):
+            return [slice(0, CH // 2), slice(CH // 2, CH)] if b == NCH - 1 else [slice(0, CH)]
+
         def quantise_z(b):
             z_codes = keep.tile([P, CH], U32, name=f"z_codes{b}", align_bytes=64)
             z_plane = keep.tile([P, CH], U8, name=f"z_plane{b}", align_bytes=64)
-            nc.vector.quantize_mx(out=z_codes[:].bitcast(FP8X4), scales=z_plane[:], in_=z_grp[b].rearrange("p j t -> p (j t)"))
+            for cols in cuts(b):
+                nc.vector.quantize_mx(out=z_codes[:, cols].bitcast(FP8X4), scales=z_plane[:, cols], in_=z_grp[b][:, cols].rearrange("p j t -> p (j t)"))
             return z_codes, z_plane
 
         def multiply(b, z_mx, parts):
@@ -212,8 +216,9 @@ def tile_picked_waveeq_none_p_kernel(tc, x_words, x_scales, w1, prev, c2, w2, of
         def make_z(b):
             z_grp[b] = keep.tile([P, CH, PACK], BF16, name=f"z_grp{b}", tag=f"z{b}", align_bytes=64)[:]
             other = prev_t[:, :, b * CH : (b + 1) * CH] if b < 2 else cw[:, :, (b - 2) * CH : (b - 1) * CH]
-            nc.vector.tensor_tensor(z_grp[b].rearrange("p (c i) t -> p c t i", i=2), rest[b][:].rearrange("p t (c i) -> p c t i", i=2),
-                                    other.rearrange("p t (c i) -> p c t i", i=2), SUB if b < 2 else ADD)
+            for cols in cuts(b):
+                nc.vector.tensor_tensor(z_grp[b][:, cols].rearrange("p (c i) t -> p c t i", i=2), rest[b][:, :, cols].rearrange("p t (c i) -> p c t i", i=2),
+                                        other[:, :, cols].rearrange("p t (c i) -> p c t i", i=2), SUB if b < 2 else ADD)
 
         open_rest(0)
         open_rest(1)

@@ -148,7 +148,7 @@ def tile_picked_waveeq_none_p_kernel(tc, x_words, x_scales, w1, prev, c2, w2, of
 
         w2_codes = keep.tile([P, N], U32, name="w2_codes", align_bytes=64)
         w2_plane = keep.tile([P, N], U8, name="w2_plane", align_bytes=64)
-        w2_grp = keep.tile([P, N, PACK], BF16, name="w2_grp", tag="z2", align_bytes=64)
+        w2_grp = keep.tile([P, N, PACK], BF16, name="w2_grp", align_bytes=64)
 
         def weave_w2(q):
             cols = slice(q * P, (q + 1) * P)
@@ -157,7 +157,7 @@ def tile_picked_waveeq_none_p_kernel(tc, x_words, x_scales, w1, prev, c2, w2, of
         out_rows = out.rearrange("(g p) j -> p g j", p=P)
 
         def cuts(b):
-            return [slice(0, CH // 2), slice(CH // 2, CH)] if b == NCH - 1 else [slice(0, CH)]
+            return [slice(0, CH // 2), slice(CH // 2, CH)] if b == 1 else [slice(0, CH)]
 
         def quantise_z(b):
             z_codes = keep.tile([P, CH], U32, name=f"z_codes{b}", align_bytes=64)
@@ -187,7 +187,7 @@ def tile_picked_waveeq_none_p_kernel(tc, x_words, x_scales, w1, prev, c2, w2, of
         z_grp = {}
         ay = [keep.tile([P, PACK, P], F32, name=f"ay{b}")[:] for b in range(NCH)]
         y_turned = []
-        part = [keep.tile([P, PACK, P], F32, name=f"part{b}")[:] for b in range(2)]
+        part = [keep.tile([P, PACK, P], F32, name=f"part{b}")[:] for b in range(NCH)]
         home = (5, 6, 7, 0)
         rest = {}
         for b in range(NCH):
@@ -214,7 +214,7 @@ def tile_picked_waveeq_none_p_kernel(tc, x_words, x_scales, w1, prev, c2, w2, of
                 turn(rest[b][:, t, :], part[b][:, t, :], False, t == PACK - 1)
 
         def make_z(b):
-            z_grp[b] = keep.tile([P, CH, PACK], BF16, name=f"z_grp{b}", tag=f"z{b}", align_bytes=64)[:]
+            z_grp[b] = keep.tile([P, CH, PACK], BF16, name=f"z_grp{b}", align_bytes=64)[:]
             other = prev_t[:, :, b * CH : (b + 1) * CH] if b < 2 else cw[:, :, (b - 2) * CH : (b - 1) * CH]
             for cols in cuts(b):
                 nc.vector.tensor_tensor(z_grp[b][:, cols].rearrange("p (c i) t -> p c t i", i=2), rest[b][:, :, cols].rearrange("p t (c i) -> p c t i", i=2),
@@ -233,29 +233,23 @@ def tile_picked_waveeq_none_p_kernel(tc, x_words, x_scales, w1, prev, c2, w2, of
             for b in range(2, NCH):
                 turn(turned[b][:, t, :], ke[t][:, b * CH : (b + 1) * CH], False, t == PACK - 1)
         open_rest(3)
-        weave_w2(0)
-        weave_w2(1)
+        for q in range(PACK):
+            weave_w2(q)
         for t in range(PACK):
             nc.vector.tensor_tensor(sw[t][:], y[t][:].indirect(west_t[:, 0:16]), ke[t][:, halves[0]], ADD)
             for b in range(2):
                 turn(turned[b][:, t, :], sw[t][:, b * CH : (b + 1) * CH])
-        late = keep.tile([P, 2, PACK, P], F32, name="late", tag=f"sw{PACK - 1}")
-        part += [late[:, 0], late[:, 1]]
         open_rest(2)
-        make_rest(0)
-        make_rest(1)
-        make_rest(2)
-        make_rest(3)
-        weave_w2(2)
-        weave_w2(3)
+        for b in (2, 3, 0, 1):
+            make_rest(b)
         for t in range(PACK):
             nc.vector.tensor_tensor(cw[:, t, :], y[t][:].indirect(west_t[:, 16:32]), c_row[:], MULT)
-        make_z(0)
-        make_z(1)
         nc.vector.quantize_mx(out=w2_codes[:].bitcast(FP8X4), scales=w2_plane[:], in_=w2_grp[:].rearrange("p c t -> p (c t)"))
-        store(multiply(0, quantise_z(0), [(1, nc.scalar.copy, nc.sync), (2, nc.scalar.copy, nc.sync)]))
         make_z(2)
-        store(multiply(1, quantise_z(1), [(3, nc.scalar.copy, nc.sync), (4, nc.scalar.copy, nc.sync)]))
-        ways = multiply(2, quantise_z(2), [(5, nc.scalar.copy, nc.sync), (6, nc.vector.tensor_copy, nc.sync)])
         make_z(3)
-        store(ways + multiply(3, quantise_z(3), [(1, nc.scalar.copy, nc.scalar), (2, nc.vector.tensor_copy, nc.sync)]))
+        store(multiply(2, quantise_z(2), [(3, nc.scalar.copy, nc.sync), (4, nc.scalar.copy, nc.sync)]))
+        make_z(0)
+        store(multiply(3, quantise_z(3), [(1, nc.scalar.copy, nc.sync), (2, nc.scalar.copy, nc.sync)]))
+        ways = multiply(0, quantise_z(0), [(7, nc.scalar.copy, nc.sync), (0, nc.vector.tensor_copy, nc.sync)])
+        make_z(1)
+        store(ways + multiply(1, quantise_z(1), [(3, nc.scalar.copy, nc.scalar), (4, nc.vector.tensor_copy, nc.sync)]))

@@ -23,6 +23,7 @@ PACK = 4
 CH = 128
 NCH = S // CH
 XA = 1024
+HALF = S // 2
 
 
 def tile_picked_waveeq_none_p_kernel(tc, x_words, x_scales, w1, prev, c2, w2, offs, east, west, out):
@@ -87,10 +88,10 @@ def tile_picked_waveeq_none_p_kernel(tc, x_words, x_scales, w1, prev, c2, w2, of
 
         c_turned = bank(6, [P, P], "c_turned")
         turn(c_turned[:], c_sq[:])
-        a_col = keep.tile([P, NCH], F32, name="a_col")
+        a_col = keep.tile([P, 2], F32, name="a_col")
         c_col = keep.tile([P, NCH], F32, name="c_col")
         nc.scalar.copy(c_col[:], c_turned[:, 0:NCH])
-        nc.scalar.activation(a_col[:], c_turned[:, 0:NCH], COPY, scale=-2.0, bias=2.0)
+        nc.scalar.activation(a_col[:], c_turned[:, 0:2], COPY, scale=-2.0, bias=2.0)
 
         halves = [slice(0, S // 2), slice(S // 2, S)]
         x_codes = keep.tile([P, S], U32, name="x_codes", align_bytes=64)
@@ -111,53 +112,64 @@ def tile_picked_waveeq_none_p_kernel(tc, x_words, x_scales, w1, prev, c2, w2, of
         c_ps = bank(7, [P, 2, CH], "c_ps")
         for b in range(2):
             turn(c_ps[:, b, :], c_col[:, 2 + b : 3 + b].to_broadcast([P, P]))
-        k_row = keep.tile([P, S], F32, name="k_row")
-        c_row = keep.tile([P, S // 2], F32, name="c_row")
-        nc.vector.memset(k_row[:, 0 : S // 2], 1.0)
-        nc.scalar.activation(k_row[:, S // 2 :], c_ps[:].rearrange("p b j -> p (b j)"), COPY, scale=-1.0)
-        nc.scalar.copy(c_row[:], c_ps[:].rearrange("p b j -> p (b j)"))
+        a_row = keep.tile([P, HALF], F32, name="a_row")
+        nc.scalar.activation(a_row[:], c_ps[:].rearrange("p b j -> p (b j)"), COPY, scale=-2.0, bias=2.0)
 
-        prev_t = keep.tile([P, PACK, S], F32, name="prev_t", tag="words", align_bytes=64)
-        nc.sync.dma_start(prev_t[:], prev.rearrange("(p t) j -> p t j", t=PACK))
-        w2_raw = keep.tile([P, PACK, N], F32, name="w2_raw", tag="raw0")
+        w2_raw = keep.tile([P, PACK, N], F32, name="w2_raw", tag="words", align_bytes=64)
         nc.sync.dma_start(w2_raw[:], w2.rearrange("(p j) c -> p j c", j=PACK))
-
+        prev_t = keep.tile([P, PACK, S], F32, name="prev_t", tag="raw0")
+        nc.sync.dma_start(prev_t[:], prev.rearrange("(p t) j -> p t j", t=PACK))
 
         def first_product(acc, t, cols):
             u, e = divmod(t, 2)
             nc.tensor.matmul_mx(out=acc, lhsT=w1_codes[u][:, e * P : (e + 1) * P].bitcast(FP8X4), lhsT_scale=w1_plane[u][:, e * P : (e + 1) * P],
                                 rhs=x_codes[:, cols].bitcast(FP8X4), rhs_scale=x_plane[:, cols], start=True, stop=True)
 
-        HALF = S // 2
-        cw = keep.tile([P, PACK, HALF], F32, name="cw")
-        ke = [keep.tile([P, S], F32, name=f"ke{t}")[:] for t in range(PACK - 1)]
-        ke.append(cw[:].rearrange("p a w -> p (a w)")[:, CH : CH + S])
-
-        pieces = [(0, slice(0, S // 2), nc.scalar.copy), (1, slice(S // 2, S - CH), nc.vector.tensor_copy), (7, slice(S - CH, S), nc.scalar.copy)]
+        pieces = [(0, slice(0, S // 2), nc.scalar.copy), (6, slice(S // 2, S - CH), nc.vector.tensor_copy), (7, slice(S - CH, S), nc.scalar.copy)]
         for i, cols, copy in pieces:
             y_ps = bank(i, [P, cols.stop - cols.start], f"y_ps0_{i}")
             first_product(y_ps[:], 0, cols)
             copy(y[0][:, cols], y_ps[:])
         for t in range(1, PACK):
-            y_ps = bank(1 + t, [P, S], f"y_ps{t}")
+            y_ps = bank(t, [P, S], f"y_ps{t}")
             for cols in halves if t == 1 else [slice(0, S)]:
                 first_product(y_ps[:, cols], t, cols)
             nc.scalar.copy(y[t][:, 0:S], y_ps[:])
+
+        ye = [keep.tile([P, S], F32, name=f"ye{t}") for t in range(PACK)]
+        yw = [keep.tile([P, S], F32, name=f"yw{t}") for t in range(PACK)]
         for t in range(2, PACK):
-            nc.scalar.activation(ke[t][:, halves[0]], y[t][:].indirect(east_t[:, 0:16]), COPY)
+            nc.scalar.activation(ye[t][:], y[t][:].indirect(east_t[:]), COPY)
+
+        ay = [keep.tile([P, PACK, P], F32, name=f"ay{b}")[:] for b in range(2)]
+        for b in range(2):
+            cols = slice(b * CH, (b + 1) * CH)
+            y_turned = bank(4 + b, [P, PACK, P], f"y_turned{b}")
+            for u in range(2):
+                nc.tensor.matmul_mx(out=y_turned[:, 2 * u : 2 * u + 2].rearrange("j t p -> j (t p)"), lhsT=x_codes[:, cols].bitcast(FP8X4),
+                                    lhsT_scale=x_plane[:, cols], rhs=w1_codes[u][:].bitcast(FP8X4), rhs_scale=w1_plane[u][:], start=True, stop=True)
+            nc.scalar.activation(ay[b], y_turned[:], COPY, scale=a_col[:, b : b + 1])
 
         w2_codes = keep.tile([P, N], U32, name="w2_codes", align_bytes=64)
         w2_plane = keep.tile([P, N], U8, name="w2_plane", align_bytes=64)
         w2_grp = keep.tile([P, N, PACK], BF16, name="w2_grp", align_bytes=64)
-
-        def weave_w2(q):
+        ay_right = keep.tile([P, PACK, HALF], F32, name="ay_right")
+        own = keep.tile([P, PACK, HALF], F32, name="own")
+        for t in range(PACK):
+            nc.gpsimd.tensor_tensor(ay_right[:, t, :], y[t][:, halves[1]], a_row[:], MULT)
+        for q in range(2):
+            cols = slice(q * P, (q + 1) * P)
+            nc.gpsimd.tensor_scalar(w2_grp[:, cols], w2_raw[:, :, cols].rearrange("p t c -> p c t"), 1.0, 0.0, MULT, ADD)
+        for q in range(2, PACK):
             cols = slice(q * P, (q + 1) * P)
             nc.scalar.copy(w2_grp[:, cols].rearrange("p (c i) t -> p c t i", i=4), w2_raw[:, :, cols].rearrange("p t (c i) -> p c t i", i=4))
+        for t in range(PACK):
+            nc.gpsimd.tensor_tensor(own[:, t, :], ay_right[:, t, :], prev_t[:, t, halves[1]], SUB)
 
         out_rows = out.rearrange("(g p) j -> p g j", p=P)
 
         def cuts(b):
-            return [slice(0, CH // 2), slice(CH // 2, CH)] if b == 1 else [slice(0, CH)]
+            return [slice(0, CH // 2), slice(CH // 2, CH)] if b == NCH - 1 else [slice(0, CH)]
 
         def quantise_z(b):
             z_codes = keep.tile([P, CH], U32, name=f"z_codes{b}", align_bytes=64)
@@ -183,73 +195,57 @@ def tile_picked_waveeq_none_p_kernel(tc, x_words, x_scales, w1, prev, c2, w2, of
                 copy(o_sb[:], o_ps[:])
                 queue.dma_start(out_rows[:, 2 * h : 2 * h + 2, b * CH : (b + 1) * CH], o_sb[:])
 
-        sw = [keep.tile([P, HALF], F32, name=f"sw{t}", tag=f"sw{t}") for t in range(PACK)]
         z_grp = {}
-        ay = [keep.tile([P, PACK, P], F32, name=f"ay{b}")[:] for b in range(NCH)]
-        y_turned = []
         part = [keep.tile([P, PACK, P], F32, name=f"part{b}")[:] for b in range(NCH)]
-        home = (5, 6, 7, 0)
-        rest = {}
-        for b in range(NCH):
-            cols = slice(b * CH, (b + 1) * CH)
-            y_turned.append(bank(home[b], [P, PACK, P], f"y_turned{b}"))
-            if b < 2:
-                for u in range(2):
-                    nc.tensor.matmul_mx(out=y_turned[b][:, 2 * u : 2 * u + 2].rearrange("j t p -> j (t p)"), lhsT=x_codes[:, cols].bitcast(FP8X4),
-                                        lhsT_scale=x_plane[:, cols], rhs=w1_codes[u][:].bitcast(FP8X4), rhs_scale=w1_plane[u][:], start=True, stop=True)
-            else:
-                for t in range(PACK):
-                    turn(y_turned[b][:, t, :], y[t][:, cols])
-            nc.scalar.activation(ay[b], y_turned[b][:], COPY, scale=a_col[:, b : b + 1])
-        turned = [bank(1 + b, [P, PACK, P], f"turned{b}") for b in range(NCH)]
+        turned = [bank(i, [P, PACK, P], f"turned{b}") for b, i in enumerate((6, 7, 0, 1))]
+        rest = [bank(i, [P, PACK, CH], f"rest{b}") for b, i in enumerate((4, 5, 2, 3))]
 
-        def open_rest(b):
-            rest[b] = bank(home[b], [P, PACK, CH], f"rest{b}")
-            for t in range(PACK):
-                turn(rest[b][:, t, :], ay[b][:, t, :], t == 0, False)
+        def turn_in(src, t, chunks, start=False, stop=False):
+            for b in chunks:
+                turn(turned[b][:, t, :], src[t][:, b * CH : (b + 1) * CH], start, stop)
 
         def make_rest(b):
-            nc.scalar.activation(part[b], turned[b][:], COPY, scale=c_col[:, b : b + 1] if b < 2 else -1.0)
+            nc.scalar.activation(part[b], turned[b][:], COPY, scale=c_col[:, b : b + 1])
             for t in range(PACK):
-                turn(rest[b][:, t, :], part[b][:, t, :], False, t == PACK - 1)
+                turn(rest[b][:, t, :], part[b][:, t, :], b >= 2 and t == 0, t == PACK - 1)
 
         def make_z(b):
             z_grp[b] = keep.tile([P, CH, PACK], BF16, name=f"z_grp{b}", align_bytes=64)[:]
-            other = prev_t[:, :, b * CH : (b + 1) * CH] if b < 2 else cw[:, :, (b - 2) * CH : (b - 1) * CH]
+            other = prev_t[:, :, b * CH : (b + 1) * CH] if b < 2 else own[:, :, (b - 2) * CH : (b - 1) * CH]
             for cols in cuts(b):
                 nc.vector.tensor_tensor(z_grp[b][:, cols].rearrange("p (c i) t -> p c t i", i=2), rest[b][:, :, cols].rearrange("p t (c i) -> p c t i", i=2),
                                         other[:, :, cols].rearrange("p t (c i) -> p c t i", i=2), SUB if b < 2 else ADD)
 
-        open_rest(0)
-        open_rest(1)
-        for b in range(2, NCH):
-            for t in range(PACK):
-                turn(turned[b][:, t, :], prev_t[:, t, b * CH : (b + 1) * CH], t == 0, False)
-        for t in range(PACK):
-            if t < 2:
-                nc.vector.tensor_tensor(ke[t], y[t][:].indirect(east_t[:]), k_row[:], MULT)
-            else:
-                nc.vector.tensor_tensor(ke[t][:, halves[1]], y[t][:].indirect(east_t[:, 16:32]), k_row[:, halves[1]], MULT)
-            for b in range(2, NCH):
-                turn(turned[b][:, t, :], ke[t][:, b * CH : (b + 1) * CH], False, t == PACK - 1)
-        open_rest(3)
-        for q in range(PACK):
-            weave_w2(q)
-        for t in range(PACK):
-            nc.vector.tensor_tensor(sw[t][:], y[t][:].indirect(west_t[:, 0:16]), ke[t][:, halves[0]], ADD)
-            for b in range(2):
-                turn(turned[b][:, t, :], sw[t][:, b * CH : (b + 1) * CH])
-        open_rest(2)
-        for b in (2, 3, 0, 1):
+        every = range(NCH)
+        nc.vector.tensor_copy(ye[0][:], y[0][:].indirect(east_t[:]))
+        turn_in(ye, 0, every, start=True)
+        nc.vector.tensor_copy(yw[0][:], y[0][:].indirect(west_t[:]))
+        turn_in(yw, 0, every)
+        turn_in(ye, 2, every)
+        nc.vector.tensor_copy(ye[1][:], y[1][:].indirect(east_t[:]))
+        turn_in(ye, 1, every)
+        turn_in(ye, 3, every)
+        nc.vector.tensor_copy(yw[1][:], y[1][:].indirect(west_t[:]))
+        turn_in(yw, 1, every)
+        for t in range(2, PACK):
+            nc.vector.tensor_copy(yw[t][:, halves[0]], y[t][:].indirect(west_t[:, 0:16]))
+            turn_in(yw, t, (0, 1), stop=t == PACK - 1)
+            for i in range(PACK):
+                turn(rest[t - 2][:, i, :], ay[t - 2][:, i, :], i == 0, False)
+        nc.vector.tensor_copy(ye[3][:, halves[1]], y[2][:].indirect(west_t[:, 16:32]))
+        for b in (2, 3):
+            turn(turned[b][:, 2, :], ye[3][:, b * CH : (b + 1) * CH], False, False)
+        make_rest(0)
+        nc.vector.tensor_copy(yw[3][:, halves[1]], y[3][:].indirect(west_t[:, 16:32]))
+        turn_in(yw, 3, (2, 3), stop=True)
+        for b in range(1, NCH):
             make_rest(b)
-        for t in range(PACK):
-            nc.vector.tensor_tensor(cw[:, t, :], y[t][:].indirect(west_t[:, 16:32]), c_row[:], MULT)
         nc.vector.quantize_mx(out=w2_codes[:].bitcast(FP8X4), scales=w2_plane[:], in_=w2_grp[:].rearrange("p c t -> p (c t)"))
-        make_z(2)
-        make_z(3)
-        store(multiply(2, quantise_z(2), [(3, nc.scalar.copy, nc.sync), (4, nc.scalar.copy, nc.sync)]))
         make_z(0)
-        store(multiply(3, quantise_z(3), [(1, nc.scalar.copy, nc.sync), (2, nc.scalar.copy, nc.sync)]))
-        ways = multiply(0, quantise_z(0), [(7, nc.scalar.copy, nc.sync), (0, nc.vector.tensor_copy, nc.sync)])
         make_z(1)
-        store(ways + multiply(1, quantise_z(1), [(3, nc.scalar.copy, nc.scalar), (4, nc.vector.tensor_copy, nc.sync)]))
+        store(multiply(0, quantise_z(0), [(6, nc.scalar.copy, nc.sync), (7, nc.scalar.copy, nc.sync)]))
+        make_z(2)
+        store(multiply(1, quantise_z(1), [(0, nc.scalar.copy, nc.sync), (1, nc.scalar.copy, nc.sync)]))
+        ways = multiply(2, quantise_z(2), [(4, nc.scalar.copy, nc.sync), (5, nc.vector.tensor_copy, nc.sync)])
+        make_z(3)
+        store(ways + multiply(3, quantise_z(3), [(6, nc.scalar.copy, nc.scalar), (7, nc.vector.tensor_copy, nc.sync)]))

@@ -138,8 +138,7 @@ def tile_picked_waveeq_none_p_kernel(tc, x_words, x_scales, w1, prev, c2, w2, of
 
         ye = [keep.tile([P, S], F32, name=f"ye{t}") for t in range(PACK)]
         yw = [keep.tile([P, S], F32, name=f"yw{t}") for t in range(PACK)]
-        for t in range(2, PACK):
-            nc.scalar.activation(ye[t][:], y[t][:].indirect(east_t[:]), COPY)
+        nc.scalar.activation(ye[2][:], y[2][:].indirect(east_t[:]), COPY)
 
         ay = [keep.tile([P, PACK, P], F32, name=f"ay{b}")[:] for b in range(2)]
         for b in range(2):
@@ -149,22 +148,18 @@ def tile_picked_waveeq_none_p_kernel(tc, x_words, x_scales, w1, prev, c2, w2, of
                 nc.tensor.matmul_mx(out=y_turned[:, 2 * u : 2 * u + 2].rearrange("j t p -> j (t p)"), lhsT=x_codes[:, cols].bitcast(FP8X4),
                                     lhsT_scale=x_plane[:, cols], rhs=w1_codes[u][:].bitcast(FP8X4), rhs_scale=w1_plane[u][:], start=True, stop=True)
             nc.scalar.activation(ay[b], y_turned[:], COPY, scale=a_col[:, b : b + 1])
+        for h in range(2):
+            nc.scalar.activation(ye[3][:, halves[h]], y[3][:].indirect(east_t[:, 16 * h : 16 * h + 16]), COPY)
 
-        w2_codes = keep.tile([P, N], U32, name="w2_codes", align_bytes=64)
         w2_plane = keep.tile([P, N], U8, name="w2_plane", align_bytes=64)
-        w2_grp = keep.tile([P, N, PACK], BF16, name="w2_grp", align_bytes=64)
+        w2_grp = [keep.tile([P, N // 2, PACK], BF16, name="w2_grp0", align_bytes=64)]
         ay_right = keep.tile([P, PACK, HALF], F32, name="ay_right")
-        own = keep.tile([P, PACK, HALF], F32, name="own")
+        own = [keep.tile([P, PACK, CH], F32, name=f"own{b}") for b in range(2)]
         for t in range(PACK):
             nc.gpsimd.tensor_tensor(ay_right[:, t, :], y[t][:, halves[1]], a_row[:], MULT)
-        for q in range(2):
-            cols = slice(q * P, (q + 1) * P)
-            nc.gpsimd.tensor_scalar(w2_grp[:, cols], w2_raw[:, :, cols].rearrange("p t c -> p c t"), 1.0, 0.0, MULT, ADD)
-        for q in range(2, PACK):
-            cols = slice(q * P, (q + 1) * P)
-            nc.scalar.copy(w2_grp[:, cols].rearrange("p (c i) t -> p c t i", i=4), w2_raw[:, :, cols].rearrange("p t (c i) -> p c t i", i=4))
-        for t in range(PACK):
-            nc.gpsimd.tensor_tensor(own[:, t, :], ay_right[:, t, :], prev_t[:, t, halves[1]], SUB)
+        nc.gpsimd.tensor_scalar(w2_grp[0][:], w2_raw[:, :, halves[0]].rearrange("p t c -> p c t"), 1.0, 0.0, MULT, ADD)
+        for b in range(2, NCH):
+            nc.gpsimd.tensor_tensor(own[b - 2][:], ay_right[:, :, (b - 2) * CH : (b - 1) * CH], prev_t[:, :, b * CH : (b + 1) * CH], SUB)
 
         out_rows = out.rearrange("(g p) j -> p g j", p=P)
 
@@ -196,13 +191,13 @@ def tile_picked_waveeq_none_p_kernel(tc, x_words, x_scales, w1, prev, c2, w2, of
                 queue.dma_start(out_rows[:, 2 * h : 2 * h + 2, b * CH : (b + 1) * CH], o_sb[:])
 
         z_grp = {}
-        part = [keep.tile([P, PACK, P], F32, name=f"part{b}")[:] for b in range(NCH)]
+        part = [keep.tile([P, PACK, P], F32, name=f"part{b}", tag=f"part{b}", align_bytes=64)[:] for b in range(NCH)]
         turned = [bank(i, [P, PACK, P], f"turned{b}") for b, i in enumerate((6, 7, 0, 1))]
         rest = [bank(i, [P, PACK, CH], f"rest{b}") for b, i in enumerate((4, 5, 2, 3))]
 
         def turn_in(src, t, chunks, start=False, stop=False):
             for b in chunks:
-                turn(turned[b][:, t, :], src[t][:, b * CH : (b + 1) * CH], start, stop)
+                turn(turned[b][:, t, :], src[:, b * CH : (b + 1) * CH], start, stop)
 
         def make_rest(b):
             nc.scalar.activation(part[b], turned[b][:], COPY, scale=c_col[:, b : b + 1])
@@ -211,38 +206,62 @@ def tile_picked_waveeq_none_p_kernel(tc, x_words, x_scales, w1, prev, c2, w2, of
 
         def make_z(b):
             z_grp[b] = keep.tile([P, CH, PACK], BF16, name=f"z_grp{b}", align_bytes=64)[:]
-            other = prev_t[:, :, b * CH : (b + 1) * CH] if b < 2 else own[:, :, (b - 2) * CH : (b - 1) * CH]
+            other = prev_t[:, :, b * CH : (b + 1) * CH] if b < 2 else own[b - 2][:]
             for cols in cuts(b):
                 nc.vector.tensor_tensor(z_grp[b][:, cols].rearrange("p (c i) t -> p c t i", i=2), rest[b][:, :, cols].rearrange("p t (c i) -> p c t i", i=2),
                                         other[:, :, cols].rearrange("p t (c i) -> p c t i", i=2), SUB if b < 2 else ADD)
 
         every = range(NCH)
+
+        def gather(target, t, places, h):
+            nc.vector.tensor_copy(target, y[t][:].indirect(places[:, 16 * h : 16 * h + 16]))
+
+        def turn_half(src, t, h, stop=False):
+            for e in range(2):
+                turn(turned[2 * h + e][:, t, :], src[:, e * CH : (e + 1) * CH], False, stop)
+
+        def open_rest(b):
+            for t in range(PACK):
+                turn(rest[b][:, t, :], ay[b][:, t, :], t == 0, False)
+
         nc.vector.tensor_copy(ye[0][:], y[0][:].indirect(east_t[:]))
-        turn_in(ye, 0, every, start=True)
+        turn_in(ye[0], 0, every, start=True)
         nc.vector.tensor_copy(yw[0][:], y[0][:].indirect(west_t[:]))
-        turn_in(yw, 0, every)
-        turn_in(ye, 2, every)
-        nc.vector.tensor_copy(ye[1][:], y[1][:].indirect(east_t[:]))
-        turn_in(ye, 1, every)
-        turn_in(ye, 3, every)
-        nc.vector.tensor_copy(yw[1][:], y[1][:].indirect(west_t[:]))
-        turn_in(yw, 1, every)
-        for t in range(2, PACK):
-            nc.vector.tensor_copy(yw[t][:, halves[0]], y[t][:].indirect(west_t[:, 0:16]))
-            turn_in(yw, t, (0, 1), stop=t == PACK - 1)
-            for i in range(PACK):
-                turn(rest[t - 2][:, i, :], ay[t - 2][:, i, :], i == 0, False)
-        nc.vector.tensor_copy(ye[3][:, halves[1]], y[2][:].indirect(west_t[:, 16:32]))
-        for b in (2, 3):
-            turn(turned[b][:, 2, :], ye[3][:, b * CH : (b + 1) * CH], False, False)
+        turn_in(yw[0], 0, every)
+        gather(ye[1][:, halves[0]], 1, east_t, 0)
+        turn_half(ye[1][:, halves[0]], 1, 0)
+        turn_in(ye[2], 2, every)
+        gather(yw[1][:, halves[0]], 1, west_t, 0)
+        turn_half(yw[1][:, halves[0]], 1, 0)
+        open_rest(0)
+        gather(yw[2][:, halves[0]], 2, west_t, 0)
+        turn_half(yw[2][:, halves[0]], 2, 0)
+        open_rest(1)
+        turn_half(ye[3][:, halves[0]], 3, 0)
+        gather(yw[3][:, halves[0]], 3, west_t, 0)
+        turn_half(yw[3][:, halves[0]], 3, 0, stop=True)
+        turn_half(ye[3][:, halves[1]], 3, 1)
+        gather(yw[3][:, halves[1]], 3, west_t, 1)
+        turn_half(yw[3][:, halves[1]], 3, 1)
         make_rest(0)
-        nc.vector.tensor_copy(yw[3][:, halves[1]], y[3][:].indirect(west_t[:, 16:32]))
-        turn_in(yw, 3, (2, 3), stop=True)
-        for b in range(1, NCH):
-            make_rest(b)
-        nc.vector.quantize_mx(out=w2_codes[:].bitcast(FP8X4), scales=w2_plane[:], in_=w2_grp[:].rearrange("p c t -> p (c t)"))
+        gather(ye[2][:, halves[0]], 1, east_t, 1)
+        turn_half(ye[2][:, halves[0]], 1, 1)
+        make_rest(1)
+        w2_grp.append(keep.tile([P, N // 2, PACK], BF16, name="w2_grp1", tag="part0", align_bytes=64))
+        for q in range(2):
+            cols = slice(q * P, (q + 1) * P)
+            nc.scalar.copy(w2_grp[1][:, cols].rearrange("p (c i) t -> p c t i", i=4), w2_raw[:, :, halves[1]][:, :, cols].rearrange("p t (c i) -> p c t i", i=4))
+        gather(ye[2][:, halves[1]], 1, west_t, 1)
+        turn_half(ye[2][:, halves[1]], 1, 1)
+        gather(ye[3][:, halves[1]], 2, west_t, 1)
+        turn_half(ye[3][:, halves[1]], 2, 1, stop=True)
+        make_rest(2)
+        make_rest(3)
         make_z(0)
         make_z(1)
+        w2_codes = keep.tile([P, N], U32, name="w2_codes", tag="part1", align_bytes=64)
+        for h in range(2):
+            nc.vector.quantize_mx(out=w2_codes[:, halves[h]].bitcast(FP8X4), scales=w2_plane[:, halves[h]], in_=w2_grp[h][:].rearrange("p c t -> p (c t)"))
         store(multiply(0, quantise_z(0), [(6, nc.scalar.copy, nc.sync), (7, nc.scalar.copy, nc.sync)]))
         make_z(2)
         store(multiply(1, quantise_z(1), [(0, nc.scalar.copy, nc.sync), (1, nc.scalar.copy, nc.sync)]))

@@ -115,10 +115,10 @@ def tile_picked_waveeq_none_p_kernel(tc, x_words, x_scales, w1, prev, c2, w2, of
         a_row = keep.tile([P, HALF], F32, name="a_row")
         nc.scalar.activation(a_row[:], c_ps[:].rearrange("p b j -> p (b j)"), COPY, scale=-2.0, bias=2.0)
 
-        w2_raw = keep.tile([P, PACK, N], F32, name="w2_raw", tag="words", align_bytes=64)
-        nc.sync.dma_start(w2_raw[:], w2.rearrange("(p j) c -> p j c", j=PACK))
-        prev_t = keep.tile([P, PACK, S], F32, name="prev_t", tag="raw0")
+        prev_t = keep.tile([P, PACK, S], F32, name="prev_t", tag="words", align_bytes=64)
         nc.sync.dma_start(prev_t[:], prev.rearrange("(p t) j -> p t j", t=PACK))
+        w2_raw = keep.tile([P, PACK, N], F32, name="w2_raw", tag="raw0")
+        nc.sync.dma_start(w2_raw[:], w2.rearrange("(p j) c -> p j c", j=PACK))
 
         def first_product(acc, t, cols):
             u, e = divmod(t, 2)
@@ -148,16 +148,15 @@ def tile_picked_waveeq_none_p_kernel(tc, x_words, x_scales, w1, prev, c2, w2, of
                 nc.tensor.matmul_mx(out=y_turned[:, 2 * u : 2 * u + 2].rearrange("j t p -> j (t p)"), lhsT=x_codes[:, cols].bitcast(FP8X4),
                                     lhsT_scale=x_plane[:, cols], rhs=w1_codes[u][:].bitcast(FP8X4), rhs_scale=w1_plane[u][:], start=True, stop=True)
             nc.scalar.activation(ay[b], y_turned[:], COPY, scale=a_col[:, b : b + 1])
-        for h in range(2):
-            nc.scalar.activation(ye[3][:, halves[h]], y[3][:].indirect(east_t[:, 16 * h : 16 * h + 16]), COPY)
+        nc.scalar.activation(ye[3][:], y[3][:].indirect(east_t[:]), COPY)
+        nc.scalar.activation(yw[3][:, halves[1]], y[3][:].indirect(west_t[:, 16:32]), COPY)
 
         w2_plane = keep.tile([P, N], U8, name="w2_plane", align_bytes=64)
-        w2_grp = [keep.tile([P, N // 2, PACK], BF16, name="w2_grp0", align_bytes=64)]
-        ay_right = keep.tile([P, PACK, HALF], F32, name="ay_right")
+        w2_codes = keep.tile([P, N], U32, name="w2_codes", align_bytes=64)
+        ay_right = keep.tile([P, PACK, HALF], F32, name="ay_right", tag="ay_right", align_bytes=64)
         own = [keep.tile([P, PACK, CH], F32, name=f"own{b}") for b in range(2)]
         for t in range(PACK):
             nc.gpsimd.tensor_tensor(ay_right[:, t, :], y[t][:, halves[1]], a_row[:], MULT)
-        nc.gpsimd.tensor_scalar(w2_grp[0][:], w2_raw[:, :, halves[0]].rearrange("p t c -> p c t"), 1.0, 0.0, MULT, ADD)
         for b in range(2, NCH):
             nc.gpsimd.tensor_tensor(own[b - 2][:], ay_right[:, :, (b - 2) * CH : (b - 1) * CH], prev_t[:, :, b * CH : (b + 1) * CH], SUB)
 
@@ -228,40 +227,30 @@ def tile_picked_waveeq_none_p_kernel(tc, x_words, x_scales, w1, prev, c2, w2, of
         turn_in(ye[0], 0, every, start=True)
         nc.vector.tensor_copy(yw[0][:], y[0][:].indirect(west_t[:]))
         turn_in(yw[0], 0, every)
-        gather(ye[1][:, halves[0]], 1, east_t, 0)
-        turn_half(ye[1][:, halves[0]], 1, 0)
         turn_in(ye[2], 2, every)
-        gather(yw[1][:, halves[0]], 1, west_t, 0)
-        turn_half(yw[1][:, halves[0]], 1, 0)
+        nc.vector.tensor_copy(ye[1][:], y[1][:].indirect(east_t[:]))
+        turn_in(ye[1], 1, every)
         open_rest(0)
+        open_rest(1)
+        nc.vector.tensor_copy(yw[1][:], y[1][:].indirect(west_t[:]))
+        turn_in(yw[1], 1, every)
         gather(yw[2][:, halves[0]], 2, west_t, 0)
         turn_half(yw[2][:, halves[0]], 2, 0)
-        open_rest(1)
-        turn_half(ye[3][:, halves[0]], 3, 0)
+        turn_in(ye[3], 3, every)
         gather(yw[3][:, halves[0]], 3, west_t, 0)
         turn_half(yw[3][:, halves[0]], 3, 0, stop=True)
-        turn_half(ye[3][:, halves[1]], 3, 1)
-        gather(yw[3][:, halves[1]], 3, west_t, 1)
         turn_half(yw[3][:, halves[1]], 3, 1)
-        make_rest(0)
-        gather(ye[2][:, halves[0]], 1, east_t, 1)
-        turn_half(ye[2][:, halves[0]], 1, 1)
-        make_rest(1)
-        w2_grp.append(keep.tile([P, N // 2, PACK], BF16, name="w2_grp1", tag="part0", align_bytes=64))
-        for q in range(2):
-            cols = slice(q * P, (q + 1) * P)
-            nc.scalar.copy(w2_grp[1][:, cols].rearrange("p (c i) t -> p c t i", i=4), w2_raw[:, :, halves[1]][:, :, cols].rearrange("p t (c i) -> p c t i", i=4))
-        gather(ye[2][:, halves[1]], 1, west_t, 1)
-        turn_half(ye[2][:, halves[1]], 1, 1)
-        gather(ye[3][:, halves[1]], 2, west_t, 1)
-        turn_half(ye[3][:, halves[1]], 2, 1, stop=True)
-        make_rest(2)
-        make_rest(3)
+        gather(ye[2][:, halves[1]], 2, west_t, 1)
+        turn_half(ye[2][:, halves[1]], 2, 1, stop=True)
+        for b in every:
+            make_rest(b)
+        w2_grp = keep.tile([P, N, PACK], BF16, name="w2_grp", tag="ay_right", align_bytes=64)
+        for half in halves:
+            nc.vector.tensor_copy(w2_grp[:, half].rearrange("p (c i) t -> p c t i", i=4), w2_raw[:, :, half].rearrange("p t (c i) -> p c t i", i=4))
+        for half in halves:
+            nc.vector.quantize_mx(out=w2_codes[:, half].bitcast(FP8X4), scales=w2_plane[:, half], in_=w2_grp[:, half].rearrange("p c t -> p (c t)"))
         make_z(0)
         make_z(1)
-        w2_codes = keep.tile([P, N], U32, name="w2_codes", tag="part1", align_bytes=64)
-        for h in range(2):
-            nc.vector.quantize_mx(out=w2_codes[:, halves[h]].bitcast(FP8X4), scales=w2_plane[:, halves[h]], in_=w2_grp[h][:].rearrange("p c t -> p (c t)"))
         store(multiply(0, quantise_z(0), [(6, nc.scalar.copy, nc.sync), (7, nc.scalar.copy, nc.sync)]))
         make_z(2)
         store(multiply(1, quantise_z(1), [(0, nc.scalar.copy, nc.sync), (1, nc.scalar.copy, nc.sync)]))

@@ -41,9 +41,8 @@ def tile_picked_waveeq_none_p_kernel(tc, x_words, x_scales, w1, prev, c2, w2, of
         nc.vector.memset(scale_win[:].bitcast(I32), 0)
         word_win = keep.tile([P, T], U32, name="word_win", tag="words", align_bytes=64)
         word_rows = x_words[0].rearrange("p c r -> p (c r)").bitcast(I32)
-        nc.sync.dma_start(word_win[:, 0 : XA // 2].bitcast(I32), word_rows[:, 0 : XA // 2])
+        nc.sync.dma_start(word_win[:, 0:XA].bitcast(I32), word_rows[:, 0:XA])
         nc.sync.dma_start(offs_t[:], offs)
-        nc.sync.dma_start(word_win[:, XA // 2 : XA].bitcast(I32), word_rows[:, XA // 2 : XA])
         for r in range(2):
             nc.sync.dma_start(scale_win[r:P:16, :].bitcast(I32), x_scales[0, r:16:2, :].bitcast(I32))
         c_sq = keep.tile([P, P], F32, name="c_sq")
@@ -88,10 +87,8 @@ def tile_picked_waveeq_none_p_kernel(tc, x_words, x_scales, w1, prev, c2, w2, of
 
         c_turned = bank(6, [P, P], "c_turned")
         turn(c_turned[:], c_sq[:])
-        a_col = keep.tile([P, 2], F32, name="a_col")
         c_col = keep.tile([P, NCH], F32, name="c_col")
-        nc.scalar.copy(c_col[:], c_turned[:, 0:NCH])
-        nc.scalar.activation(a_col[:], c_turned[:, 0:2], COPY, scale=-2.0, bias=2.0)
+        nc.scalar.activation(c_col[:], c_turned[:, 0:NCH], COPY, scale=-1.0)
 
         halves = [slice(0, S // 2), slice(S // 2, S)]
         x_codes = keep.tile([P, S], U32, name="x_codes", align_bytes=64)
@@ -109,14 +106,9 @@ def tile_picked_waveeq_none_p_kernel(tc, x_words, x_scales, w1, prev, c2, w2, of
             nc.vector.quantize_mx(out=w1_codes[u][:, lo:hi].bitcast(FP8X4), scales=w1_plane[u][:, lo:hi],
                                   in_=w1_grp[u][:].rearrange("p t m j -> p (t m j)")[:, PACK * lo : PACK * hi])
 
-        c_ps = bank(7, [P, 2, CH], "c_ps")
-        for b in range(2):
-            turn(c_ps[:, b, :], c_col[:, 2 + b : 3 + b].to_broadcast([P, P]))
-        a_row = keep.tile([P, HALF], F32, name="a_row")
-        nc.scalar.activation(a_row[:], c_ps[:].rearrange("p b j -> p (b j)"), COPY, scale=-2.0, bias=2.0)
-
         prev_t = keep.tile([P, PACK, S], F32, name="prev_t", tag="words", align_bytes=64)
-        nc.sync.dma_start(prev_t[:], prev.rearrange("(p t) j -> p t j", t=PACK))
+        for slabs in (slice(0, 1), slice(1, 2), slice(2, PACK)):
+            nc.sync.dma_start(prev_t[:, slabs], prev.rearrange("(p t) j -> p t j", t=PACK)[:, slabs])
         w2_raw = keep.tile([P, PACK, N], F32, name="w2_raw", tag="raw0")
         nc.sync.dma_start(w2_raw[:], w2.rearrange("(p j) c -> p j c", j=PACK))
 
@@ -125,40 +117,35 @@ def tile_picked_waveeq_none_p_kernel(tc, x_words, x_scales, w1, prev, c2, w2, of
             nc.tensor.matmul_mx(out=acc, lhsT=w1_codes[u][:, e * P : (e + 1) * P].bitcast(FP8X4), lhsT_scale=w1_plane[u][:, e * P : (e + 1) * P],
                                 rhs=x_codes[:, cols].bitcast(FP8X4), rhs_scale=x_plane[:, cols], start=True, stop=True)
 
-        pieces = [(0, slice(0, S // 2), nc.scalar.copy), (6, slice(S // 2, S - CH), nc.vector.tensor_copy), (7, slice(S - CH, S), nc.scalar.copy)]
-        for i, cols, copy in pieces:
+        def double_on_scalar(target, src):
+            nc.scalar.activation(target, src, COPY, scale=2.0)
+
+        def double_on_vector(target, src):
+            nc.vector.tensor_scalar(target, src, 2.0, None, MULT)
+
+        pieces = [(0, slice(0, S // 2), double_on_scalar), (6, slice(S // 2, S - CH), double_on_vector), (7, slice(S - CH, S), double_on_scalar)]
+        for i, cols, double in pieces:
             y_ps = bank(i, [P, cols.stop - cols.start], f"y_ps0_{i}")
             first_product(y_ps[:], 0, cols)
-            copy(y[0][:, cols], y_ps[:])
+            double(y[0][:, cols], y_ps[:])
         for t in range(1, PACK):
             y_ps = bank(t, [P, S], f"y_ps{t}")
             for cols in halves if t == 1 else [slice(0, S)]:
                 first_product(y_ps[:, cols], t, cols)
-            nc.scalar.copy(y[t][:, 0:S], y_ps[:])
+            double_on_scalar(y[t][:, 0:S], y_ps[:])
 
         ye = [keep.tile([P, S], F32, name=f"ye{t}") for t in range(PACK)]
         yw = [keep.tile([P, S], F32, name=f"yw{t}") for t in range(PACK)]
-        nc.scalar.activation(ye[2][:], y[2][:].indirect(east_t[:]), COPY)
+        for t in range(2, PACK):
+            nc.scalar.activation(ye[t][:], y[t][:].indirect(east_t[:]), COPY, scale=-0.5)
+        for h, half in enumerate(halves):
+            nc.scalar.activation(yw[3][:, half], y[3][:].indirect(west_t[:, 16 * h : 16 * h + 16]), COPY, scale=-0.5)
 
-        ay = [keep.tile([P, PACK, P], F32, name=f"ay{b}")[:] for b in range(2)]
-        for b in range(2):
-            cols = slice(b * CH, (b + 1) * CH)
-            y_turned = bank(4 + b, [P, PACK, P], f"y_turned{b}")
-            for u in range(2):
-                nc.tensor.matmul_mx(out=y_turned[:, 2 * u : 2 * u + 2].rearrange("j t p -> j (t p)"), lhsT=x_codes[:, cols].bitcast(FP8X4),
-                                    lhsT_scale=x_plane[:, cols], rhs=w1_codes[u][:].bitcast(FP8X4), rhs_scale=w1_plane[u][:], start=True, stop=True)
-            nc.scalar.activation(ay[b], y_turned[:], COPY, scale=a_col[:, b : b + 1])
-        nc.scalar.activation(ye[3][:], y[3][:].indirect(east_t[:]), COPY)
-        nc.scalar.activation(yw[3][:, halves[1]], y[3][:].indirect(west_t[:, 16:32]), COPY)
-
-        w2_plane = keep.tile([P, N], U8, name="w2_plane", align_bytes=64)
         w2_codes = keep.tile([P, N], U32, name="w2_codes", align_bytes=64)
-        ay_right = keep.tile([P, PACK, HALF], F32, name="ay_right", tag="ay_right", align_bytes=64)
-        own = [keep.tile([P, PACK, CH], F32, name=f"own{b}") for b in range(2)]
+        w2_plane = keep.tile([P, N], U8, name="w2_plane", align_bytes=64)
+        own = keep.tile([P, PACK, S], F32, name="own")
         for t in range(PACK):
-            nc.gpsimd.tensor_tensor(ay_right[:, t, :], y[t][:, halves[1]], a_row[:], MULT)
-        for b in range(2, NCH):
-            nc.gpsimd.tensor_tensor(own[b - 2][:], ay_right[:, :, (b - 2) * CH : (b - 1) * CH], prev_t[:, :, b * CH : (b + 1) * CH], SUB)
+            nc.gpsimd.tensor_tensor(own[:, t, :], y[t][:, 0:S], prev_t[:, t, :], SUB)
 
         out_rows = out.rearrange("(g p) j -> p g j", p=P)
 
@@ -166,7 +153,7 @@ def tile_picked_waveeq_none_p_kernel(tc, x_words, x_scales, w1, prev, c2, w2, of
             return [slice(0, CH // 2), slice(CH // 2, CH)] if b == NCH - 1 else [slice(0, CH)]
 
         def quantise_z(b):
-            z_codes = keep.tile([P, CH], U32, name=f"z_codes{b}", align_bytes=64)
+            z_codes = keep.tile([P, CH], U32, name=f"z_codes{b}", tag=f"part{(b + 1) % NCH}", align_bytes=64)
             z_plane = keep.tile([P, CH], U8, name=f"z_plane{b}", align_bytes=64)
             for cols in cuts(b):
                 nc.vector.quantize_mx(out=z_codes[:, cols].bitcast(FP8X4), scales=z_plane[:, cols], in_=z_grp[b][:, cols].rearrange("p j t -> p (j t)"))
@@ -189,10 +176,10 @@ def tile_picked_waveeq_none_p_kernel(tc, x_words, x_scales, w1, prev, c2, w2, of
                 copy(o_sb[:], o_ps[:])
                 queue.dma_start(out_rows[:, 2 * h : 2 * h + 2, b * CH : (b + 1) * CH], o_sb[:])
 
-        z_grp = {}
+        z_grp = [keep.tile([P, CH, PACK], BF16, name=f"z_grp{b}", align_bytes=64)[:] for b in range(NCH)]
         part = [keep.tile([P, PACK, P], F32, name=f"part{b}", tag=f"part{b}", align_bytes=64)[:] for b in range(NCH)]
-        turned = [bank(i, [P, PACK, P], f"turned{b}") for b, i in enumerate((6, 7, 0, 1))]
-        rest = [bank(i, [P, PACK, CH], f"rest{b}") for b, i in enumerate((4, 5, 2, 3))]
+        turned = [bank(i, [P, PACK, P], f"turned{b}") for b, i in enumerate((4, 5, 6, 7))]
+        rest = [bank(i, [P, PACK, CH], f"rest{b}") for b, i in enumerate((0, 1, 2, 3))]
 
         def turn_in(src, t, chunks, start=False, stop=False):
             for b in chunks:
@@ -201,59 +188,54 @@ def tile_picked_waveeq_none_p_kernel(tc, x_words, x_scales, w1, prev, c2, w2, of
         def make_rest(b):
             nc.scalar.activation(part[b], turned[b][:], COPY, scale=c_col[:, b : b + 1])
             for t in range(PACK):
-                turn(rest[b][:, t, :], part[b][:, t, :], b >= 2 and t == 0, t == PACK - 1)
+                turn(rest[b][:, t, :], part[b][:, t, :], t == 0, t == PACK - 1)
 
-        def make_z(b):
-            z_grp[b] = keep.tile([P, CH, PACK], BF16, name=f"z_grp{b}", align_bytes=64)[:]
-            other = prev_t[:, :, b * CH : (b + 1) * CH] if b < 2 else own[b - 2][:]
-            for cols in cuts(b):
+        def make_z(b, pieces=(slice(0, CH),)):
+            other = own[:, :, b * CH : (b + 1) * CH]
+            for cols in pieces:
                 nc.vector.tensor_tensor(z_grp[b][:, cols].rearrange("p (c i) t -> p c t i", i=2), rest[b][:, :, cols].rearrange("p t (c i) -> p c t i", i=2),
-                                        other[:, :, cols].rearrange("p t (c i) -> p c t i", i=2), SUB if b < 2 else ADD)
+                                        other[:, :, cols].rearrange("p t (c i) -> p c t i", i=2), ADD)
 
         every = range(NCH)
 
-        def gather(target, t, places, h):
-            nc.vector.tensor_copy(target, y[t][:].indirect(places[:, 16 * h : 16 * h + 16]))
+        def gather(target, t, places):
+            nc.vector.tensor_scalar(target, y[t][:].indirect(places), -0.5, 0.0, MULT, ADD)
 
         def turn_half(src, t, h, stop=False):
             for e in range(2):
                 turn(turned[2 * h + e][:, t, :], src[:, e * CH : (e + 1) * CH], False, stop)
 
-        def open_rest(b):
-            for t in range(PACK):
-                turn(rest[b][:, t, :], ay[b][:, t, :], t == 0, False)
-
-        nc.vector.tensor_copy(ye[0][:], y[0][:].indirect(east_t[:]))
-        turn_in(ye[0], 0, every, start=True)
-        nc.vector.tensor_copy(yw[0][:], y[0][:].indirect(west_t[:]))
+        turn_in(y[0], 0, every, start=True)
+        turn_in(y[1], 1, every)
+        gather(ye[0][:], 0, east_t[:])
+        turn_in(ye[0], 0, every)
+        turn_in(y[2], 2, every)
+        turn_in(y[3], 3, every)
+        gather(yw[0][:], 0, west_t[:])
         turn_in(yw[0], 0, every)
         turn_in(ye[2], 2, every)
-        nc.vector.tensor_copy(ye[1][:], y[1][:].indirect(east_t[:]))
+        gather(ye[1][:], 1, east_t[:])
         turn_in(ye[1], 1, every)
-        open_rest(0)
-        open_rest(1)
-        nc.vector.tensor_copy(yw[1][:], y[1][:].indirect(west_t[:]))
-        turn_in(yw[1], 1, every)
-        gather(yw[2][:, halves[0]], 2, west_t, 0)
-        turn_half(yw[2][:, halves[0]], 2, 0)
         turn_in(ye[3], 3, every)
-        gather(yw[3][:, halves[0]], 3, west_t, 0)
-        turn_half(yw[3][:, halves[0]], 3, 0, stop=True)
-        turn_half(yw[3][:, halves[1]], 3, 1)
-        gather(ye[2][:, halves[1]], 2, west_t, 1)
-        turn_half(ye[2][:, halves[1]], 2, 1, stop=True)
+        gather(yw[1][:], 1, west_t[:])
+        turn_in(yw[1], 1, every)
+        for h, half in enumerate(halves):
+            gather(yw[2][:, half], 2, west_t[:, 16 * h : 16 * h + 16])
+            turn_half(yw[2][:, half], 2, h)
+            turn_half(yw[3][:, half], 3, h, stop=True)
         for b in every:
             make_rest(b)
-        w2_grp = keep.tile([P, N, PACK], BF16, name="w2_grp", tag="ay_right", align_bytes=64)
+        w2_grp = keep.tile([P, N, PACK], BF16, name="w2_grp", tag="words", align_bytes=64)
         for half in halves:
             nc.vector.tensor_copy(w2_grp[:, half].rearrange("p (c i) t -> p c t i", i=4), w2_raw[:, :, half].rearrange("p t (c i) -> p c t i", i=4))
         for half in halves:
             nc.vector.quantize_mx(out=w2_codes[:, half].bitcast(FP8X4), scales=w2_plane[:, half], in_=w2_grp[:, half].rearrange("p c t -> p (c t)"))
         make_z(0)
         make_z(1)
-        store(multiply(0, quantise_z(0), [(6, nc.scalar.copy, nc.sync), (7, nc.scalar.copy, nc.sync)]))
+        store(multiply(0, quantise_z(0), [(7, nc.scalar.copy, nc.sync), (6, nc.scalar.copy, nc.sync)]))
         make_z(2)
-        store(multiply(1, quantise_z(1), [(0, nc.scalar.copy, nc.sync), (1, nc.scalar.copy, nc.sync)]))
-        ways = multiply(2, quantise_z(2), [(4, nc.scalar.copy, nc.sync), (5, nc.vector.tensor_copy, nc.sync)])
-        make_z(3)
-        store(ways + multiply(3, quantise_z(3), [(6, nc.scalar.copy, nc.scalar), (7, nc.vector.tensor_copy, nc.sync)]))
+        store(multiply(1, quantise_z(1), [(4, nc.scalar.copy, nc.sync), (5, nc.scalar.copy, nc.sync)]))
+        make_z(3, cuts(3)[:1])
+        ways = multiply(2, quantise_z(2), [(0, nc.scalar.copy, nc.sync), (1, nc.vector.tensor_copy, nc.sync)])
+        make_z(3, cuts(3)[1:])
+        store(ways + multiply(3, quantise_z(3), [(7, nc.scalar.copy, nc.scalar), (6, nc.vector.tensor_copy, nc.sync)]))

@@ -140,6 +140,7 @@ def tile_picked_waveeq_none_p_kernel(tc, x_words, x_scales, w1, prev, c2, w2, of
             nc.scalar.activation(ye[t][:], y[t][:].indirect(east_t[:]), COPY, scale=-0.5)
         for h, half in enumerate(halves):
             nc.scalar.activation(yw[3][:, half], y[3][:].indirect(west_t[:, 16 * h : 16 * h + 16]), COPY, scale=-0.5)
+        nc.scalar.activation(yw[2][:, halves[1]], y[2][:].indirect(west_t[:, 16:32]), COPY, scale=-0.5)
 
         w2_codes = keep.tile([P, N], U32, name="w2_codes", align_bytes=64)
         w2_plane = keep.tile([P, N], U8, name="w2_plane", align_bytes=64)
@@ -219,10 +220,11 @@ def tile_picked_waveeq_none_p_kernel(tc, x_words, x_scales, w1, prev, c2, w2, of
         turn_in(ye[3], 3, every)
         gather(yw[1][:], 1, west_t[:])
         turn_in(yw[1], 1, every)
-        for h, half in enumerate(halves):
-            gather(yw[2][:, half], 2, west_t[:, 16 * h : 16 * h + 16])
-            turn_half(yw[2][:, half], 2, h)
-            turn_half(yw[3][:, half], 3, h, stop=True)
+        gather(yw[2][:, halves[0]], 2, west_t[:, 0:16])
+        turn_half(yw[2][:, halves[0]], 2, 0)
+        turn_half(yw[3][:, halves[0]], 3, 0, stop=True)
+        turn_half(yw[3][:, halves[1]], 3, 1)
+        turn_half(yw[2][:, halves[1]], 2, 1, stop=True)
         for b in every:
             make_rest(b)
         w2_grp = keep.tile([P, N, PACK], BF16, name="w2_grp", tag="words", align_bytes=64)
@@ -238,4 +240,14 @@ def tile_picked_waveeq_none_p_kernel(tc, x_words, x_scales, w1, prev, c2, w2, of
         make_z(3, cuts(3)[:1])
         ways = multiply(2, quantise_z(2), [(0, nc.scalar.copy, nc.sync), (1, nc.vector.tensor_copy, nc.sync)])
         make_z(3, cuts(3)[1:])
-        store(ways + multiply(3, quantise_z(3), [(7, nc.scalar.copy, nc.scalar), (6, nc.vector.tensor_copy, nc.sync)]))
+        last = quantise_z(3)
+        store(ways)
+        for h, queue in enumerate((nc.scalar, nc.sync)):
+            o_sb = keep.tile([P, 2, CH], F32, name=f"o_sb3_{h}")
+            for e, copy in enumerate((nc.scalar.copy, nc.vector.tensor_copy)):
+                cols = slice((2 * h + e) * P, (2 * h + e + 1) * P)
+                o_ps = bank((7, 6, 4, 5)[2 * h + e], [P, CH], f"o_ps3_{h}_{e}")
+                nc.tensor.matmul_mx(out=o_ps[:], lhsT=w2_codes[:, cols].bitcast(FP8X4), lhsT_scale=w2_plane[:, cols],
+                                    rhs=last[0][:].bitcast(FP8X4), rhs_scale=last[1][:], start=True, stop=True)
+                copy(o_sb[:, e, :], o_ps[:])
+            queue.dma_start(out_rows[:, 2 * h : 2 * h + 2, 3 * CH : 4 * CH], o_sb[:])

@@ -187,9 +187,10 @@ def tile_picked_waveeq_none_p_kernel(tc, x_words, x_scales, w1, prev, c2, w2, of
                 turn(turned[b][:, t, :], src[:, b * CH : (b + 1) * CH], start, stop)
 
         def make_rest(b):
-            nc.scalar.activation(part[b], turned[b][:], COPY, scale=c_col[:, b : b + 1])
-            for t in range(PACK):
-                turn(rest[b][:, t, :], part[b][:, t, :], t == 0, t == PACK - 1)
+            for u in range(2):
+                nc.scalar.activation(part[b][:, 2 * u : 2 * u + 2], turned[b][:, 2 * u : 2 * u + 2], COPY, scale=c_col[:, b : b + 1])
+                for t in range(2 * u, 2 * u + 2):
+                    turn(rest[b][:, t, :], part[b][:, t, :], t == 0, t == PACK - 1)
 
         def make_z(b, pieces=(slice(0, CH),)):
             other = own[:, :, b * CH : (b + 1) * CH]

@@ -50,7 +50,7 @@ def tile_picked_waveeq_none_p_kernel(tc, x_words, x_scales, w1, prev, c2, w2, of
         nc.sync.dma_start(c_sq[0:NCH, :], c2[0].rearrange("(b j) -> b j", j=CH))
         nc.sync.dma_start(word_win[:, XA:].bitcast(I32), word_rows[:, XA:])
         w1_rows = w1.rearrange("(p j) c -> p j c", j=PACK)
-        w1_raw = [keep.tile([P, PACK, H // 2], F32, name=f"w1_raw{h}", tag=f"raw{h}") for h in range(2)]
+        w1_raw = [keep.tile([P, PACK, H // 2], F32, name=f"w1_raw{h}", tag=f"raw{h}", align_bytes=64) for h in range(2)]
         for h in range(2):
             nc.sync.dma_start(w1_raw[h][:], w1_rows[:, :, h * H // 2 : (h + 1) * H // 2])
         nc.sync.dma_start(east_t[:], east)
@@ -98,18 +98,29 @@ def tile_picked_waveeq_none_p_kernel(tc, x_words, x_scales, w1, prev, c2, w2, of
         w1_codes = [keep.tile([P, 2 * P], U32, name=f"w1_codes{u}", align_bytes=64) for u in range(2)]
         w1_plane = [keep.tile([P, 2 * P], U8, name=f"w1_plane{u}", align_bytes=64) for u in range(2)]
         w1_grp = [keep.tile([P, 2, P, PACK], BF16, name=f"w1_grp{u}", align_bytes=64) for u in range(2)]
-        for h, copy in enumerate((nc.scalar.copy, nc.vector.tensor_copy)):
+        def weave_w1(copy, h, u, lo, hi):
             dealt = w1_raw[h][:].rearrange("p j (m t) -> p m j t", t=PACK)
-            for u in range(2):
-                copy(w1_grp[u][:, :, h * P // 2 : (h + 1) * P // 2].rearrange("p t m j -> p m j t"), dealt[:, :, :, 2 * u : 2 * u + 2])
-        for u, lo, hi in [(0, 0, P), (0, P, 2 * P), (1, 0, 2 * P)]:
+            copy(w1_grp[u][:, :, h * P // 2 + lo : h * P // 2 + hi].rearrange("p t m j -> p m j t"), dealt[:, lo:hi, :, 2 * u : 2 * u + 2])
+
+        def quantise_w1(u, lo, hi):
             nc.vector.quantize_mx(out=w1_codes[u][:, lo:hi].bitcast(FP8X4), scales=w1_plane[u][:, lo:hi],
                                   in_=w1_grp[u][:].rearrange("p t m j -> p (t m j)")[:, PACK * lo : PACK * hi])
 
-        prev_t = keep.tile([P, PACK, S], F32, name="prev_t", tag="words", align_bytes=64)
-        for slabs in (slice(0, 1), slice(1, 2), slice(2, PACK)):
-            nc.sync.dma_start(prev_t[:, slabs], prev.rearrange("(p t) j -> p t j", t=PACK)[:, slabs])
-        w2_raw = keep.tile([P, PACK, N], F32, name="w2_raw", tag="raw0")
+        for u in range(2):
+            weave_w1(nc.scalar.copy, 0, u, 0, P // 2)
+        weave_w1(nc.vector.tensor_copy, 1, 0, 0, P // 2)
+        weave_w1(nc.vector.tensor_copy, 1, 1, 0, P // 4)
+        quantise_w1(0, 0, P)
+        weave_w1(nc.vector.tensor_copy, 1, 1, P // 4, P // 2)
+        quantise_w1(0, P, 2 * P)
+        quantise_w1(1, 0, 2 * P)
+
+        prev_rows = prev.rearrange("(p t) j -> p t j", t=PACK)
+        prev_t = [keep.tile([P, 2, S], F32, name=f"prev{u}", tag=tag, align_bytes=64) for u, tag in enumerate(("words", "raw0"))]
+        for t in range(2):
+            nc.sync.dma_start(prev_t[0][:, t, :], prev_rows[:, t, :])
+        nc.sync.dma_start(prev_t[1][:], prev_rows[:, 2:PACK])
+        w2_raw = keep.tile([P, PACK, N], F32, name="w2_raw", tag="raw1", align_bytes=64)
         nc.sync.dma_start(w2_raw[:], w2.rearrange("(p j) c -> p j c", j=PACK))
 
         def first_product(acc, t, cols):
@@ -146,7 +157,7 @@ def tile_picked_waveeq_none_p_kernel(tc, x_words, x_scales, w1, prev, c2, w2, of
         w2_plane = keep.tile([P, N], U8, name="w2_plane", align_bytes=64)
         own = keep.tile([P, PACK, S], F32, name="own")
         for t in range(PACK):
-            nc.gpsimd.tensor_tensor(own[:, t, :], y[t][:, 0:S], prev_t[:, t, :], SUB)
+            nc.gpsimd.tensor_tensor(own[:, t, :], y[t][:, 0:S], prev_t[t // 2][:, t % 2, :], SUB)
 
         out_rows = out.rearrange("(g p) j -> p g j", p=P)
 
@@ -219,16 +230,17 @@ def tile_picked_waveeq_none_p_kernel(tc, x_words, x_scales, w1, prev, c2, w2, of
         gather(ye[1][:], 1, east_t[:])
         turn_in(ye[1], 1, every)
         turn_in(ye[3], 3, every)
-        gather(yw[1][:], 1, west_t[:])
-        turn_in(yw[1], 1, every)
-        gather(yw[2][:, halves[0]], 2, west_t[:, 0:16])
-        turn_half(yw[2][:, halves[0]], 2, 0)
-        turn_half(yw[3][:, halves[0]], 3, 0, stop=True)
+        for t in (1, 3, 2):
+            if t != 3:
+                gather(yw[t][:, halves[0]], t, west_t[:, 0:16])
+            turn_half(yw[t][:, halves[0]], t, 0, stop=t == 2)
+        gather(prev_t[0][:, 0, halves[0]], 1, west_t[:, 16:32])
         turn_half(yw[3][:, halves[1]], 3, 1)
+        turn_half(prev_t[0][:, 0, halves[0]], 1, 1)
         turn_half(yw[2][:, halves[1]], 2, 1, stop=True)
         for b in every:
             make_rest(b)
-        w2_grp = keep.tile([P, N, PACK], BF16, name="w2_grp", tag="words", align_bytes=64)
+        w2_grp = keep.tile([P, N, PACK], BF16, name="w2_grp", tag="raw0", align_bytes=64)
         for half in halves:
             nc.vector.tensor_copy(w2_grp[:, half].rearrange("p (c i) t -> p c t i", i=4), w2_raw[:, :, half].rearrange("p t (c i) -> p c t i", i=4))
         for half in halves:

from contextlib import ExitStack

import concourse.mybir as mybir

K, T, S, N, H = 512, 2048, 512, 512, 512
FLOPS = 2 * K * H * S + 2 * H * N * S

F32 = mybir.dt.float32
BF16 = mybir.dt.bfloat16
I32 = mybir.dt.int32
U32 = mybir.dt.uint32
U16 = mybir.dt.uint16
U8 = mybir.dt.uint8
FP8X4 = mybir.dt.float8_e4m3fn_x4
ADD = mybir.AluOpType.add
MULT = mybir.AluOpType.mult
EQ = mybir.AluOpType.is_equal
SUB = mybir.AluOpType.subtract
COPY = mybir.ActivationFunctionType.Copy

P = 128
PACK = 4
CH = 128
NCH = S // CH
XA = 1024
HALF = S // 2


def tile_picked_waveeq_none_p_kernel(tc, x_words, x_scales, w1, prev, c2, w2, offs, east, west, out):
    nc = tc.nc
    with ExitStack() as ctx:
        lists = ctx.enter_context(tc.tile_pool(name="lists", bufs=1))
        keep = ctx.enter_context(tc.tile_pool(name="keep", bufs=1))
        psum = ctx.enter_context(tc.psum_pool(name="psum", bufs=1))

        offs_t = lists.tile([P, S // 16], U16, name="offs_t")
        east_t = lists.tile([P, S // 16], U16, name="east_t")
        west_t = lists.tile([P, S // 16], U16, name="west_t")

        scale_win = keep.tile([P, T], U8, name="scale_win")
        nc.vector.memset(scale_win[:].bitcast(I32), 0)
        word_win = keep.tile([P, T], U32, name="word_win", tag="words", align_bytes=64)
        word_rows = x_words[0].rearrange("p c r -> p (c r)").bitcast(I32)
        nc.sync.dma_start(word_win[:, 0:XA].bitcast(I32), word_rows[:, 0:XA])
        nc.sync.dma_start(offs_t[:], offs)
        for r in range(2):
            nc.sync.dma_start(scale_win[r:P:16, :].bitcast(I32), x_scales[0, r:16:2, :].bitcast(I32))
        c_sq = keep.tile([P, P], F32, name="c_sq")
        nc.vector.memset(c_sq[:], 0.0)
        nc.sync.dma_start(c_sq[0:NCH, :], c2[0].rearrange("(b j) -> b j", j=CH))
        nc.sync.dma_start(word_win[:, XA:].bitcast(I32), word_rows[:, XA:])
        w1_rows = w1.rearrange("(p j) c -> p j c", j=PACK)
        w1_raw = [keep.tile([P, PACK, H // 2], F32, name=f"w1_raw{h}", tag=f"raw{h}", align_bytes=64) for h in range(2)]
        for h in range(2):
            nc.sync.dma_start(w1_raw[h][:], w1_rows[:, :, h * H // 2 : (h + 1) * H // 2])
        nc.sync.dma_start(east_t[:], east)
        nc.sync.dma_start(west_t[:], west)

        x_plane = keep.tile([P, S], U8, name="x_plane", align_bytes=64)
        scale_got = keep.tile([P, S], U8, name="scale_got")
        nc.vector.tensor_copy(scale_got[:], scale_win[:].indirect(offs_t[:]))
        nc.vector.tensor_copy(x_plane[:].bitcast(I32), scale_got[:].bitcast(I32))
        for r in range(2):
            nc.sync.dma_start(x_plane[2 + r : P : 32, :].bitcast(I32), scale_got[16 + r : P : 32, :].bitcast(I32))

        y = [keep.tile([P, 2 * S], F32, name=f"y{t}") for t in range(PACK)]
        nc.vector.memset(y[0][:, S:], 0.0)
        for t in range(1, PACK):
            nc.scalar.activation(y[t][:, S:], y[0][:, S:], COPY)

        ident = keep.tile([P, P], F32, name="ident")
        ones = keep.tile([P, 32], F32, name="ones")
        count = keep.tile([P, 32], F32, name="count", align_bytes=64)
        count_t = keep.tile([P, 32], F32, name="count_t", align_bytes=64)
        nc.vector.memset(ones[:], 1.0)
        nc.vector.memset(ident[:], 0.0)
        nc.vector.tensor_tensor_scan(count[:], ones[:], ones[:], 0.0, MULT, ADD)
        nc.vector.transpose(count_t[:], count[:])
        for q in range(0, P, 32):
            nc.vector.tensor_tensor(ident[q : q + 32, q : q + 32], count[q : q + 32, :], count_t[q : q + 32, :], EQ)

        def bank(i, shape, name):
            return psum.tile(shape, F32, name=name, tag=f"bank{i}")

        def turn(target, src, start=True, stop=True):
            nc.tensor.matmul(target, lhsT=src, rhs=ident[:], start=start, stop=stop, is_transpose=True)

        c_turned = bank(6, [P, P], "c_turned")
        turn(c_turned[:], c_sq[:])
        c_col = keep.tile([P, NCH], F32, name="c_col")
        nc.scalar.activation(c_col[:], c_turned[:, 0:NCH], COPY, scale=-1.0)

        halves = [slice(0, S // 2), slice(S // 2, S)]
        x_codes = keep.tile([P, S], U32, name="x_codes", align_bytes=64)
        for h, half in enumerate(halves):
            nc.vector.tensor_copy(x_codes[:, half], word_win[:].indirect(offs_t[:, 16 * h : 16 * h + 16]))

        w1_codes = [keep.tile([P, 2 * P], U32, name=f"w1_codes{u}", align_bytes=64) for u in range(2)]
        w1_plane = [keep.tile([P, 2 * P], U8, name=f"w1_plane{u}", align_bytes=64) for u in range(2)]
        w1_grp = [keep.tile([P, 2, P, PACK], BF16, name=f"w1_grp{u}", align_bytes=64) for u in range(2)]
        def weave_w1(copy, h, u, lo, hi):
            dealt = w1_raw[h][:].rearrange("p j (m t) -> p m j t", t=PACK)
            copy(w1_grp[u][:, :, h * P // 2 + lo : h * P // 2 + hi].rearrange("p t m j -> p m j t"), dealt[:, lo:hi, :, 2 * u : 2 * u + 2])

        def quantise_w1(u, lo, hi):
            nc.vector.quantize_mx(out=w1_codes[u][:, lo:hi].bitcast(FP8X4), scales=w1_plane[u][:, lo:hi],
                                  in_=w1_grp[u][:].rearrange("p t m j -> p (t m j)")[:, PACK * lo : PACK * hi])

        for u in range(2):
            weave_w1(nc.scalar.copy, 0, u, 0, P // 2)
        weave_w1(nc.vector.tensor_copy, 1, 0, 0, P // 2)
        weave_w1(nc.vector.tensor_copy, 1, 1, 0, P // 4)
        quantise_w1(0, 0, P)
        weave_w1(nc.vector.tensor_copy, 1, 1, P // 4, P // 2)
        quantise_w1(0, P, 2 * P)
        quantise_w1(1, 0, 2 * P)

        prev_rows = prev.rearrange("(p t) j -> p t j", t=PACK)
        prev_t = [keep.tile([P, 2, S], F32, name=f"prev{u}", tag=tag, align_bytes=64) for u, tag in enumerate(("words", "raw0"))]
        for t in range(2):
            nc.sync.dma_start(prev_t[0][:, t, :], prev_rows[:, t, :])
        nc.sync.dma_start(prev_t[1][:], prev_rows[:, 2:PACK])
        w2_raw = keep.tile([P, PACK, N], F32, name="w2_raw", tag="raw1", align_bytes=64)
        nc.sync.dma_start(w2_raw[:], w2.rearrange("(p j) c -> p j c", j=PACK))

        def first_product(acc, t, cols):
            u, e = divmod(t, 2)
            nc.tensor.matmul_mx(out=acc, lhsT=w1_codes[u][:, e * P : (e + 1) * P].bitcast(FP8X4), lhsT_scale=w1_plane[u][:, e * P : (e + 1) * P],
                                rhs=x_codes[:, cols].bitcast(FP8X4), rhs_scale=x_plane[:, cols], start=True, stop=True)

        def double_on_scalar(target, src):
            nc.scalar.activation(target, src, COPY, scale=2.0)

        def double_on_vector(target, src):
            nc.vector.tensor_scalar(target, src, 2.0, None, MULT)

        pieces = [(0, slice(0, S // 2), double_on_scalar), (6, slice(S // 2, S - CH), double_on_vector), (7, slice(S - CH, S), double_on_scalar)]
        for i, cols, double in pieces:
            y_ps = bank(i, [P, cols.stop - cols.start], f"y_ps0_{i}")
            first_product(y_ps[:], 0, cols)
            double(y[0][:, cols], y_ps[:])
        for t in range(1, PACK):
            y_ps = bank(t, [P, S], f"y_ps{t}")
            for cols in halves if t == 1 else [slice(0, S)]:
                first_product(y_ps[:, cols], t, cols)
            double_on_scalar(y[t][:, 0:S], y_ps[:])

        ye = [keep.tile([P, S], F32, name=f"ye{t}") for t in range(PACK)]
        yw = [keep.tile([P, S], F32, name=f"yw{t}") for t in range(PACK)]
        for t in range(2, PACK):
            nc.scalar.activation(ye[t][:], y[t][:].indirect(east_t[:]), COPY, scale=-0.5)
        for h, half in enumerate(halves):
            nc.scalar.activation(yw[3][:, half], y[3][:].indirect(west_t[:, 16 * h : 16 * h + 16]), COPY, scale=-0.5)
        nc.scalar.activation(yw[2][:, halves[1]], y[2][:].indirect(west_t[:, 16:32]), COPY, scale=-0.5)

        w2_codes = keep.tile([P, N], U32, name="w2_codes", align_bytes=64)
        w2_plane = keep.tile([P, N], U8, name="w2_plane", align_bytes=64)
        own = keep.tile([P, PACK, S], F32, name="own")
        for t in range(PACK):
            nc.gpsimd.tensor_tensor(own[:, t, :], y[t][:, 0:S], prev_t[t // 2][:, t % 2, :], SUB)

        out_rows = out.rearrange("(g p) j -> p g j", p=P)

        def cuts(b):
            return [slice(0, CH // 2), slice(CH // 2, CH)] if b == NCH - 1 else [slice(0, CH)]

        def quantise_z(b):
            z_codes = keep.tile([P, CH], U32, name=f"z_codes{b}", tag=f"part{(b + 1) % NCH}", align_bytes=64)
            z_plane = keep.tile([P, CH], U8, name=f"z_plane{b}", align_bytes=64)
            for cols in cuts(b):
                nc.vector.quantize_mx(out=z_codes[:, cols].bitcast(FP8X4), scales=z_plane[:, cols], in_=z_grp[b][:, cols].rearrange("p j t -> p (j t)"))
            return z_codes, z_plane

        def multiply(b, z_mx, parts):
            ways = []
            for h, (i, copy, queue) in enumerate(parts):
                o_ps = bank(i, [P, 2, CH], f"o_ps{b}_{h}")
                for e in range(2):
                    cols = slice((2 * h + e) * P, (2 * h + e + 1) * P)
                    nc.tensor.matmul_mx(out=o_ps[:, e, :], lhsT=w2_codes[:, cols].bitcast(FP8X4), lhsT_scale=w2_plane[:, cols],
                                        rhs=z_mx[0][:].bitcast(FP8X4), rhs_scale=z_mx[1][:], start=True, stop=True)
                ways.append((b, h, o_ps, copy, queue))
            return ways

        def store(ways):
            for b, h, o_ps, copy, queue in ways:
                o_sb = keep.tile([P, 2, CH], F32, name=f"o_sb{b}_{h}")
                copy(o_sb[:], o_ps[:])
                queue.dma_start(out_rows[:, 2 * h : 2 * h + 2, b * CH : (b + 1) * CH], o_sb[:])

        z_grp = [keep.tile([P, CH, PACK], BF16, name=f"z_grp{b}", align_bytes=64)[:] for b in range(NCH)]
        part = [keep.tile([P, PACK, P], F32, name=f"part{b}", tag=f"part{b}", align_bytes=64)[:] for b in range(NCH)]
        turned = [bank(i, [P, PACK, P], f"turned{b}") for b, i in enumerate((4, 5, 6, 7))]
        rest = [bank(i, [P, PACK, CH], f"rest{b}") for b, i in enumerate((0, 1, 2, 3))]

        def turn_in(src, t, chunks, start=False, stop=False):
            for b in chunks:
                turn(turned[b][:, t, :], src[:, b * CH : (b + 1) * CH], start, stop)

        def make_rest(b):
            for u in range(2):
                nc.scalar.activation(part[b][:, 2 * u : 2 * u + 2], turned[b][:, 2 * u : 2 * u + 2], COPY, scale=c_col[:, b : b + 1])
                for t in range(2 * u, 2 * u + 2):
                    turn(rest[b][:, t, :], part[b][:, t, :], t == 0, t == PACK - 1)

        def make_z(b, pieces=(slice(0, CH),)):
            other = own[:, :, b * CH : (b + 1) * CH]
            for cols in pieces:
                nc.vector.tensor_tensor(z_grp[b][:, cols].rearrange("p (c i) t -> p c t i", i=2), rest[b][:, :, cols].rearrange("p t (c i) -> p c t i", i=2),
                                        other[:, :, cols].rearrange("p t (c i) -> p c t i", i=2), ADD)

        every = range(NCH)

        def gather(target, t, places):
            nc.vector.tensor_scalar(target, y[t][:].indirect(places), -0.5, 0.0, MULT, ADD)

        def turn_half(src, t, h, stop=False):
            for e in range(2):
                turn(turned[2 * h + e][:, t, :], src[:, e * CH : (e + 1) * CH], False, stop)

        turn_in(y[0], 0, every, start=True)
        turn_in(y[1], 1, every)
        gather(ye[0][:], 0, east_t[:])
        turn_in(ye[0], 0, every)
        turn_in(y[2], 2, every)
        turn_in(y[3], 3, every)
        gather(yw[0][:], 0, west_t[:])
        turn_in(yw[0], 0, every)
        turn_in(ye[2], 2, every)
        gather(ye[1][:], 1, east_t[:])
        turn_in(ye[1], 1, every)
        turn_in(ye[3], 3, every)
        for t in (1, 3, 2):
            if t != 3:
                gather(yw[t][:, halves[0]], t, west_t[:, 0:16])
            turn_half(yw[t][:, halves[0]], t, 0, stop=t == 2)
        gather(prev_t[0][:, 0, halves[0]], 1, west_t[:, 16:32])
        turn_half(yw[3][:, halves[1]], 3, 1)
        turn_half(prev_t[0][:, 0, halves[0]], 1, 1)
        turn_half(yw[2][:, halves[1]], 2, 1, stop=True)
        for b in every:
            make_rest(b)
        w2_grp = keep.tile([P, N, PACK], BF16, name="w2_grp", tag="raw0", align_bytes=64)
        for half in halves:
            nc.vector.tensor_copy(w2_grp[:, half].rearrange("p (c i) t -> p c t i", i=4), w2_raw[:, :, half].rearrange("p t (c i) -> p c t i", i=4))
        for half in halves:
            nc.vector.quantize_mx(out=w2_codes[:, half].bitcast(FP8X4), scales=w2_plane[:, half], in_=w2_grp[:, half].rearrange("p c t -> p (c t)"))
        make_z(0)
        make_z(1)
        store(multiply(0, quantise_z(0), [(7, nc.scalar.copy, nc.sync), (6, nc.scalar.copy, nc.sync)]))
        make_z(2)
        store(multiply(1, quantise_z(1), [(4, nc.scalar.copy, nc.sync), (5, nc.scalar.copy, nc.sync)]))
        make_z(3, cuts(3)[:1])
        ways = multiply(2, quantise_z(2), [(0, nc.scalar.copy, nc.sync), (1, nc.vector.tensor_copy, nc.sync)])
        make_z(3, cuts(3)[1:])
        last = quantise_z(3)
        store(ways)
        for h, queue in enumerate((nc.scalar, nc.sync)):
            o_sb = keep.tile([P, 2, CH], F32, name=f"o_sb3_{h}")
            for e, copy in enumerate((nc.scalar.copy, nc.vector.tensor_copy)):
                cols = slice((2 * h + e) * P, (2 * h + e + 1) * P)
                o_ps = bank((7, 6, 4, 5)[2 * h + e], [P, CH], f"o_ps3_{h}_{e}")
                nc.tensor.matmul_mx(out=o_ps[:], lhsT=w2_codes[:, cols].bitcast(FP8X4), lhsT_scale=w2_plane[:, cols],
                                    rhs=last[0][:].bitcast(FP8X4), rhs_scale=last[1][:], start=True, stop=True)
                copy(o_sb[:, e, :], o_ps[:])
            queue.dma_start(out_rows[:, 2 * h : 2 * h + 2, 3 * CH : 4 * CH], o_sb[:])
